import numpy as np
import ml_dtypes


def mxq(x, axis, fmt="e4m3"):
    dtype, down = {"e4m3": (ml_dtypes.float8_e4m3fn, 7), "e5m2": (ml_dtypes.float8_e5m2, 14)}[fmt]
    v = np.moveaxis(np.asarray(x, np.float32).astype(ml_dtypes.bfloat16).astype(np.float64), axis, -1)
    blocks = v.reshape(v.shape[:-1] + (-1, 32))
    amax = np.abs(blocks).max(-1, keepdims=True)
    byte = np.maximum(np.where(amax > 0, np.frexp(amax)[1] - 1 + 127, 0) - down, 1)
    scale = np.exp2(byte - 127.0)
    codes = (blocks / scale).astype(np.float32).astype(dtype).astype(np.float64)
    return np.moveaxis((codes * scale).reshape(v.shape), -1, axis)


WIDE = False


def mx_kscale(k):
    if not WIDE:
        return np.ones(k)
    levels = np.array([10, -10, 5, -5, 0])
    if k % 512:
        return np.exp2(np.random.permutation(np.resize(levels, k // 32))).repeat(32)
    a = np.empty((k // 512, 16))
    for p in range(k // 512):
        a[p, :8] = np.random.permutation(np.resize(levels, 8))
        for g in range(8):
            far = levels[np.abs(levels - a[p, g]) >= 10]
            a[p, g + 8] = far[np.random.randint(len(far))]
    return np.exp2(a.ravel()).repeat(32)


def f64(x):
    return np.asarray(x).astype(np.float64)


def striped(idx):
    return np.tile(idx.reshape(-1, 16).T, (8, 1)).astype(np.uint16)


def unstriped(offs):
    return offs[:16].T.reshape(-1).astype(np.int64)


K, T, E, C, N = 2048, 512, 8, 256, 256
TOP = 4


def by_expert(wq, xq):
    return np.concatenate([wq[e].T @ xq[:, e * C:(e + 1) * C] for e in range(E)], axis=1)


def setup_inputs():
    n = np.random.standard_normal
    s = mx_kscale(K)[:, None]
    deal = np.repeat(np.arange(E), C).reshape(TOP, T)[:, np.random.permutation(T)]
    deal = np.take_along_axis(deal, np.argsort(np.random.rand(TOP, T), axis=0), axis=0)
    for _ in range(8):
        s_, t_ = np.random.permutation(T).reshape(2, -1); r = np.random.randint(TOP, size=T // 2); x, y = deal[r, s_].copy(), deal[r, t_].copy()
        ok = ~((deal[:, s_] == y).any(0) | (deal[:, t_] == x).any(0)); deal[r[ok], s_[ok]] = y[ok]; deal[r[ok], t_[ok]] = x[ok]
    order = np.lexsort((np.random.rand(TOP * T), deal.reshape(-1)))
    slot_token = order % T; pos = np.empty(TOP * T, np.int64); pos[order] = np.arange(TOP * T); pos = pos.reshape(TOP, T)
    g = np.random.uniform(0.5, 1.5, (TOP, T)); g = g / g.sum(0)
    w_slot = np.empty(E * C)
    for r in range(TOP): w_slot[pos[r]] = g[r]
    return {
        "xT": (n((K, T)) * s).astype(np.float32),
        "w": (n((E, K, N)) / np.sqrt(K) / s[None]).astype(np.float32),
        "b": (0.3 * n((N, E))).astype(np.float32),
        "gate": np.tile(w_slot, (K, 1)).astype(np.float32),
        "offs": striped(slot_token),
        "pos1": striped(pos[0]),
        "pos2": striped(pos[1]),
        "pos3": striped(pos[2]),
        "pos4": striped(pos[3]),
    }


def reference(xT, w, b, gate, offs, pos1, pos2, pos3, pos4):
    idx = unstriped(offs)
    xq = mxq(f64(gate) * f64(xT)[:, idx], 0, "e4m3")
    y = by_expert(mxq(f64(w), 1, "e4m3"), xq)
    y = y + np.repeat(f64(b), C, axis=1)
    return y[:, unstriped(pos1)] + y[:, unstriped(pos2)] + y[:, unstriped(pos3)] + y[:, unstriped(pos4)]

@@ -1,0 +1,224 @@
+from contextlib import ExitStack
+
+import concourse.mybir as mybir
+
+K, T, E, C, N = 2048, 512, 8, 256, 256
+TOP = 4
+S = E * C
+
+FLOPS = 2 * K * N * S
+BYTES = 4 * (K * T + E * K * N + N * E + S + N * T) + 2 * 128 * (S + TOP * T) // 16
+
+F32 = mybir.dt.float32
+BF16 = mybir.dt.bfloat16
+U32 = mybir.dt.uint32
+U16 = mybir.dt.uint16
+U8 = mybir.dt.uint8
+FP8X4 = mybir.dt.float8_e4m3fn_x4
+MULT = mybir.AluOpType.mult
+ADD = mybir.AluOpType.add
+IDENT = mybir.ActivationFunctionType.Identity
+
+P = 128
+PACK = 4
+PASSES = K // (P * PACK)
+HALVES = 2
+EH = E // HALVES
+SH = S // HALVES
+STEPS = HALVES * PASSES
+NT = N // P
+WINDOW = SH + 16
+LIST = 16
+
+
+def tile_moe_pre_lin_bias_kernel(tc, xT, w, b, gate, offs, pos1, pos2, pos3, pos4, out):
+    nc = tc.nc
+    x_rows = xT.rearrange("(g p j) t -> g j p t", p=P, j=PACK)
+    w_rows = w.rearrange("e (g p j) n -> g p e (j n)", p=P, j=PACK)
+
+    with ExitStack() as ctx:
+        keep = ctx.enter_context(tc.tile_pool(name="keep", bufs=1))
+        two = ctx.enter_context(tc.tile_pool(name="two", bufs=2))
+        three = ctx.enter_context(tc.tile_pool(name="three", bufs=3))
+        four = ctx.enter_context(tc.tile_pool(name="four", bufs=4))
+        psum = ctx.enter_context(tc.psum_pool(name="psum", bufs=1))
+
+        slot_tokens = keep.tile([P, S // LIST], U16, name="slot_tokens")
+        token_slots = [keep.tile([P, T // LIST], U16, name="token_slots%d" % r) for r in range(TOP)]
+        gates = keep.tile([P, S], F32, name="gates")
+        bias = keep.tile([P, NT, E], F32, name="bias")
+        windows = {(g, j): keep.tile([P, WINDOW], F32, name="window%d_%d" % (g, j)) for g in range(PASSES) for j in range(PACK)}
+        y = [keep.tile([P, S], F32, name="y%d" % t) for t in range(NT)]
+
+        w_raw, w_bf, w_codes, w_scales = {}, {}, {}, {}
+        x_f32, x_bf, x_codes, x_scales = {}, {}, {}, {}
+        banks = {}
+
+        def load_x(g, j):
+            nc.sync.dma_start(out=windows[g, j][:, 0:T], in_=x_rows[g, j])
+
+        def load_gate(lo, hi):
+            nc.sync.dma_start(out=gates[:, lo:hi], in_=gate[0:P, lo:hi])
+
+        def load_w(s, pair):
+            h, g = divmod(s, PASSES)
+            e0 = h * EH + 2 * pair
+            w_raw[s, pair] = four.tile([P, 2, PACK * N], F32, name="w_raw")
+            nc.sync.dma_start(out=w_raw[s, pair][:], in_=w_rows[g, :, e0 : e0 + 2, :])
+
+        def interleave(dst, src):
+            nc.scalar.copy(
+                out=dst.rearrange("p (c i t) -> p c t i", i=4, t=PACK),
+                in_=src.rearrange("p t (c i) -> p c t i", i=4),
+            )
+
+        def round_w(s, pair):
+            if pair == 0:
+                w_bf[s] = three.tile([P, EH * N * PACK], BF16, name="w_bf", align_bytes=64)
+            for q in range(2):
+                col = (2 * pair + q) * N * PACK
+                interleave(w_bf[s][:, col : col + N * PACK], w_raw[s, pair][:, q, :].rearrange("p (t n) -> p t n", t=PACK))
+
+        def quantise_w(s, lo, hi):
+            if lo == 0:
+                w_codes[s] = two.tile([P, EH * N], U32, name="w_codes", align_bytes=64)
+                w_scales[s] = two.tile([P, EH * N], U8, name="w_scales", align_bytes=64)
+            nc.vector.quantize_mx(out=w_codes[s][:, lo:hi].bitcast(FP8X4), scales=w_scales[s][:, lo:hi], in_=w_bf[s][:, PACK * lo : PACK * hi])
+
+        def gather_x(s, j, lo, hi):
+            h, g = divmod(s, PASSES)
+            if j == 0 and lo == 0:
+                x_f32[s] = two.tile([P, PACK, SH], F32, name="x_f32")
+            a, z = h * SH + lo, h * SH + hi
+            nc.vector.tensor_tensor(
+                x_f32[s][:, j, lo:hi],
+                windows[g, j][:].indirect(slot_tokens[:, a // LIST : z // LIST]),
+                gates[:, a:z],
+                MULT,
+            )
+
+        def round_x(s, lo, hi):
+            if lo == 0:
+                x_bf[s] = two.tile([P, SH * PACK], BF16, name="x_bf", align_bytes=64)
+            interleave(x_bf[s][:, PACK * lo : PACK * hi], x_f32[s][:, :, lo:hi])
+
+        def quantise_x(s, lo, hi):
+            if lo == 0:
+                x_codes[s] = two.tile([P, SH], U32, name="x_codes", align_bytes=64)
+                x_scales[s] = two.tile([P, SH], U8, name="x_scales", align_bytes=64)
+            nc.vector.quantize_mx(out=x_codes[s][:, lo:hi].bitcast(FP8X4), scales=x_scales[s][:, lo:hi], in_=x_bf[s][:, PACK * lo : PACK * hi])
+
+        def multiply(s, q):
+            h, g = divmod(s, PASSES)
+            slots = slice(q * C, (q + 1) * C)
+            for t in range(NT):
+                if g == 0:
+                    banks[q, t] = psum.tile([P, C], F32, name="bank%d_%d" % (q, t))
+                cols = slice(q * N + t * P, q * N + (t + 1) * P)
+                nc.tensor.matmul_mx(
+                    out=banks[q, t][:],
+                    lhsT=w_codes[s][:, cols].bitcast(FP8X4),
+                    lhsT_scale=w_scales[s][:, cols],
+                    rhs=x_codes[s][:, slots].bitcast(FP8X4),
+                    rhs_scale=x_scales[s][:, slots],
+                    start=(g == 0),
+                    stop=(g == PASSES - 1),
+                )
+
+        def add_bias(h, q, t):
+            e = h * EH + q
+            nc.scalar.activation(out=y[t][:, e * C : (e + 1) * C], in_=banks[q, t][:], func=IDENT, bias=bias[:, t, e : e + 1])
+
+        def finish(s):
+            quantise_w(s, 0, EH * N)
+            quantise_x(s, 0, SH)
+            for q in range(EH):
+                multiply(s, q)
+            if s % PASSES == PASSES - 1:
+                for q in range(EH):
+                    for t in range(NT):
+                        add_bias(s // PASSES, q, t)
+
+        nc.sync.dma_start(slot_tokens[:], offs)
+        load_x(0, 0)
+        load_gate(0, C)
+        load_gate(C, SH)
+        load_x(0, 1)
+        load_w(0, 0)
+        load_x(0, 2)
+        load_x(0, 3)
+        load_w(0, 1)
+
+        last = STEPS - 1
+        for s in range(last):
+            if s + 1 < PASSES:
+                for j in range(PACK):
+                    load_x(s + 1, j)
+            load_w(s + 1, 0)
+            load_w(s + 1, 1)
+            if s == 1:
+                load_gate(SH, S)
+                nc.sync.dma_start(out=bias[:], in_=b.rearrange("(t p) e -> p t e", p=P))
+                for r, pos in enumerate((pos1, pos2, pos3, pos4)):
+                    nc.sync.dma_start(token_slots[r][:], pos)
+            if s == 0:
+                round_w(0, 0)
+                round_w(0, 1)
+                gather_x(0, 0, 0, C)
+                gather_x(0, 0, C, SH)
+            else:
+                gather_x(s, 0, 0, SH)
+            for j in range(1, PACK):
+                gather_x(s, j, 0, SH)
+            round_x(s, 0, SH)
+            round_w(s + 1, 0)
+            round_w(s + 1, 1)
+            if s > 0:
+                finish(s - 1)
+
+        h = HALVES - 1
+        for j in range(PACK):
+            gather_x(last, j, 0, 2 * C)
+        round_x(last, 0, 2 * C)
+        finish(last - 1)
+        for j in range(PACK):
+            gather_x(last, j, 2 * C, 3 * C)
+        round_x(last, 2 * C, 3 * C)
+        quantise_w(last, 0, 2 * N)
+        quantise_x(last, 0, 2 * C)
+        multiply(last, 0)
+        multiply(last, 1)
+        for j in range(PACK):
+            gather_x(last, j, 3 * C, 4 * C)
+        round_x(last, 3 * C, 4 * C)
+        quantise_w(last, 2 * N, 4 * N)
+        quantise_x(last, 2 * C, 3 * C)
+        multiply(last, 2)
+        quantise_x(last, 3 * C, 4 * C)
+        multiply(last, 3)
+        for t in range(NT):
+            for q in range(EH):
+                add_bias(h, q, t)
+
+        picked = [two.tile([P, TOP, T], F32, name="x_f32") for t in range(NT)]
+        total = [keep.tile([P, 2, T], F32, name="total%d" % t) for t in range(NT)]
+
+        def fetch(t, r):
+            nc.vector.tensor_copy(picked[t][:, r, :], y[t][:].indirect(token_slots[r][:]))
+
+        def add(t, r):
+            left = picked[t][:, 0, :] if r == 1 else total[t][:, r % 2, :]
+            nc.vector.tensor_tensor(total[t][:, (r + 1) % 2, :], left, picked[t][:, r, :], ADD)
+
+        for t in range(NT):
+            fetch(t, 0)
+            if t > 0:
+                add(t - 1, 3)
+                nc.sync.dma_start(out=out[(t - 1) * P : t * P, :], in_=total[t - 1][:, 0, :])
+            fetch(t, 1)
+            fetch(t, 2)
+            add(t, 1)
+            fetch(t, 3)
+            add(t, 2)
+        add(NT - 1, 3)
+        nc.sync.dma_start(out=out[(NT - 1) * P : NT * P, :], in_=total[NT - 1][:, 0, :])

@@ -29,6 +29,7 @@ STEPS = HALVES * PASSES
 NT = N // P
 WINDOW = SH + 16
 LIST = 16
+HELD = 3
 
 
 def tile_moe_pre_lin_bias_kernel(tc, xT, w, b, gate, offs, pos1, pos2, pos3, pos4, out):
@@ -76,13 +77,15 @@ def tile_moe_pre_lin_bias_kernel(tc, xT, w, b, gate, offs, pos1, pos2, pos3, pos
             if pair == 0:
                 w_bf[s] = three.tile([P, EH * N * PACK], BF16, name="w_bf", align_bytes=64)
             for q in range(2):
-                col = (2 * pair + q) * N * PACK
-                interleave(w_bf[s][:, col : col + N * PACK], w_raw[s, pair][:, q, :].rearrange("p (t n) -> p t n", t=PACK))
+                rows = w_raw[s, pair][:, q, :].rearrange("p (j n) -> p j n", j=PACK)
+                for t in range(NT):
+                    col = (t * EH + 2 * pair + q) * P * PACK
+                    interleave(w_bf[s][:, col : col + P * PACK], rows[:, :, t * P : (t + 1) * P])
 
         def quantise_w(s, lo, hi):
             if lo == 0:
-                w_codes[s] = two.tile([P, EH * N], U32, name="w_codes", align_bytes=64)
-                w_scales[s] = two.tile([P, EH * N], U8, name="w_scales", align_bytes=64)
+                w_codes[s] = three.tile([P, EH * N], U32, name="w_codes", align_bytes=64)
+                w_scales[s] = three.tile([P, EH * N], U8, name="w_scales", align_bytes=64)
             nc.vector.quantize_mx(out=w_codes[s][:, lo:hi].bitcast(FP8X4), scales=w_scales[s][:, lo:hi], in_=w_bf[s][:, PACK * lo : PACK * hi])
 
         def gather_x(s, j, lo, hi):
@@ -104,43 +107,49 @@ def tile_moe_pre_lin_bias_kernel(tc, xT, w, b, gate, offs, pos1, pos2, pos3, pos
 
         def quantise_x(s, lo, hi):
             if lo == 0:
-                x_codes[s] = two.tile([P, SH], U32, name="x_codes", align_bytes=64)
-                x_scales[s] = two.tile([P, SH], U8, name="x_scales", align_bytes=64)
+                x_codes[s] = three.tile([P, SH], U32, name="x_codes", align_bytes=64)
+                x_scales[s] = three.tile([P, SH], U8, name="x_scales", align_bytes=64)
             nc.vector.quantize_mx(out=x_codes[s][:, lo:hi].bitcast(FP8X4), scales=x_scales[s][:, lo:hi], in_=x_bf[s][:, PACK * lo : PACK * hi])
 
-        def multiply(s, q):
-            h, g = divmod(s, PASSES)
+        def multiply(s, q, t):
+            g = s % PASSES
             slots = slice(q * C, (q + 1) * C)
-            for t in range(NT):
-                if g == 0:
-                    banks[q, t] = psum.tile([P, C], F32, name="bank%d_%d" % (q, t))
-                cols = slice(q * N + t * P, q * N + (t + 1) * P)
-                nc.tensor.matmul_mx(
-                    out=banks[q, t][:],
-                    lhsT=w_codes[s][:, cols].bitcast(FP8X4),
-                    lhsT_scale=w_scales[s][:, cols],
-                    rhs=x_codes[s][:, slots].bitcast(FP8X4),
-                    rhs_scale=x_scales[s][:, slots],
-                    start=(g == 0),
-                    stop=(g == PASSES - 1),
-                )
+            cols = slice((t * EH + q) * P, (t * EH + q + 1) * P)
+            if g == 0:
+                banks[q, t] = psum.tile([P, C], F32, name="bank%d_%d" % (q, t))
+            nc.tensor.matmul_mx(
+                out=banks[q, t][:],
+                lhsT=w_codes[s][:, cols].bitcast(FP8X4),
+                lhsT_scale=w_scales[s][:, cols],
+                rhs=x_codes[s][:, slots].bitcast(FP8X4),
+                rhs_scale=x_scales[s][:, slots],
+                start=(g == 0),
+                stop=(g == PASSES - 1),
+            )
 
         def add_bias(h, q, t):
             e = h * EH + q
             nc.scalar.activation(out=y[t][:, e * C : (e + 1) * C], in_=banks[q, t][:], func=IDENT, bias=bias[:, t, e : e + 1])
 
         def finish(s):
-            quantise_w(s, 0, EH * N)
+            tiles = NT if s < STEPS - HELD else 1
+            quantise_w(s, 0, tiles * EH * P)
             quantise_x(s, 0, SH)
-            for q in range(EH):
-                multiply(s, q)
-            if s % PASSES == PASSES - 1:
+            for t in range(tiles):
                 for q in range(EH):
-                    for t in range(NT):
+                    multiply(s, q, t)
+            if s % PASSES == PASSES - 1:
+                for t in range(NT):
+                    for q in range(EH):
                         add_bias(s // PASSES, q, t)
 
+        def finish_held(s):
+            quantise_w(s, EH * P, NT * EH * P)
+            for q in range(EH):
+                multiply(s, q, 1)
+
         nc.sync.dma_start(slot_tokens[:], offs)
-        load_x(0, 0)
+        nc.scalar.dma_start(out=windows[0, 0][:, 0:T], in_=x_rows[0, 0])
         load_gate(0, C)
         load_gate(C, SH)
         load_x(0, 1)
@@ -184,41 +193,31 @@ def tile_moe_pre_lin_bias_kernel(tc, xT, w, b, gate, offs, pos1, pos2, pos3, pos
         for j in range(PACK):
             gather_x(last, j, 2 * C, 3 * C)
         round_x(last, 2 * C, 3 * C)
-        quantise_w(last, 0, 2 * N)
+        quantise_w(last, 0, EH * P)
         quantise_x(last, 0, 2 * C)
-        multiply(last, 0)
-        multiply(last, 1)
+        multiply(last, 0, 0)
+        multiply(last, 1, 0)
         for j in range(PACK):
             gather_x(last, j, 3 * C, 4 * C)
         round_x(last, 3 * C, 4 * C)
-        quantise_w(last, 2 * N, 4 * N)
-        quantise_x(last, 2 * C, 3 * C)
-        multiply(last, 2)
-        quantise_x(last, 3 * C, 4 * C)
-        multiply(last, 3)
-        for t in range(NT):
-            for q in range(EH):
-                add_bias(h, q, t)
+        for q in range(2, EH):
+            quantise_x(last, q * C, (q + 1) * C)
+            multiply(last, q, 0)
+        for q in range(EH):
+            add_bias(h, q, 0)
+        for s in range(STEPS - HELD, STEPS):
+            finish_held(s)
+        for q in range(EH):
+            add_bias(h, q, 1)
 
         picked = [two.tile([P, TOP, T], F32, name="x_f32") for t in range(NT)]
-        total = [keep.tile([P, 2, T], F32, name="total%d" % t) for t in range(NT)]
-
-        def fetch(t, r):
-            nc.vector.tensor_copy(picked[t][:, r, :], y[t][:].indirect(token_slots[r][:]))
-
-        def add(t, r):
-            left = picked[t][:, 0, :] if r == 1 else total[t][:, r % 2, :]
-            nc.vector.tensor_tensor(total[t][:, (r + 1) % 2, :], left, picked[t][:, r, :], ADD)
+        total = [two.tile([P, 2, T], F32, name="x_bf", align_bytes=64) for t in range(NT)]
 
         for t in range(NT):
-            fetch(t, 0)
-            if t > 0:
-                add(t - 1, 3)
-                nc.sync.dma_start(out=out[(t - 1) * P : t * P, :], in_=total[t - 1][:, 0, :])
-            fetch(t, 1)
-            fetch(t, 2)
-            add(t, 1)
-            fetch(t, 3)
-            add(t, 2)
-        add(NT - 1, 3)
-        nc.sync.dma_start(out=out[(NT - 1) * P : NT * P, :], in_=total[NT - 1][:, 0, :])
+            for r in range(TOP):
+                nc.vector.tensor_copy(picked[t][:, r, :], y[t][:].indirect(token_slots[r][:]))
+            for r in range(1, TOP):
+                engine = nc.vector if t == NT - 1 and r > 1 else nc.gpsimd
+                left = picked[t][:, 0, :] if r == 1 else total[t][:, r % 2, :]
+                engine.tensor_tensor(total[t][:, (r + 1) % 2, :], left, picked[t][:, r, :], ADD)
+            nc.sync.dma_start(out=out[t * P : (t + 1) * P, :], in_=total[t][:, 0, :])

@@ -54,6 +54,7 @@ def tile_moe_pre_lin_bias_kernel(tc, xT, w, b, gate, offs, pos1, pos2, pos3, pos
         w_raw, w_bf, w_codes, w_scales = {}, {}, {}, {}
         x_f32, x_bf, x_codes, x_scales = {}, {}, {}, {}
         banks = {}
+        late_codes = {}
 
         def load_x(g, j):
             nc.sync.dma_start(out=windows[g, j][:, 0:T], in_=x_rows[g, j])
@@ -88,13 +89,13 @@ def tile_moe_pre_lin_bias_kernel(tc, xT, w, b, gate, offs, pos1, pos2, pos3, pos
                 w_scales[s] = three.tile([P, EH * N], U8, name="w_scales", align_bytes=64)
             nc.vector.quantize_mx(out=w_codes[s][:, lo:hi].bitcast(FP8X4), scales=w_scales[s][:, lo:hi], in_=w_bf[s][:, PACK * lo : PACK * hi])
 
-        def gather_x(s, j, lo, hi):
+        def gather_x(s, j, lo, hi, into=None):
             h, g = divmod(s, PASSES)
             if j == 0 and lo == 0:
                 x_f32[s] = two.tile([P, PACK, SH], F32, name="x_f32")
             a, z = h * SH + lo, h * SH + hi
             nc.vector.tensor_tensor(
-                x_f32[s][:, j, lo:hi],
+                x_f32[s][:, j, lo:hi] if into is None else into[:, j, :],
                 windows[g, j][:].indirect(slot_tokens[:, a // LIST : z // LIST]),
                 gates[:, a:z],
                 MULT,
@@ -115,16 +116,17 @@ def tile_moe_pre_lin_bias_kernel(tc, xT, w, b, gate, offs, pos1, pos2, pos3, pos
             g = s % PASSES
             slots = slice(q * C, (q + 1) * C)
             cols = slice((t * EH + q) * P, (t * EH + q + 1) * P)
+            closing = STEPS - 2 if (s >= STEPS - HELD and t == 1) else s - g + PASSES - 1
             if g == 0:
                 banks[q, t] = psum.tile([P, C], F32, name="bank%d_%d" % (q, t))
             nc.tensor.matmul_mx(
                 out=banks[q, t][:],
-                lhsT=w_codes[s][:, cols].bitcast(FP8X4),
+                lhsT=(late_codes[s][:, q * P : (q + 1) * P] if t == 1 and s in late_codes else w_codes[s][:, cols]).bitcast(FP8X4),
                 lhsT_scale=w_scales[s][:, cols],
                 rhs=x_codes[s][:, slots].bitcast(FP8X4),
                 rhs_scale=x_scales[s][:, slots],
                 start=(g == 0),
-                stop=(g == PASSES - 1),
+                stop=(s == closing),
             )
 
         def add_bias(h, q, t):
@@ -142,11 +144,6 @@ def tile_moe_pre_lin_bias_kernel(tc, xT, w, b, gate, offs, pos1, pos2, pos3, pos
                 for t in range(NT):
                     for q in range(EH):
                         add_bias(s // PASSES, q, t)
-
-        def finish_held(s):
-            quantise_w(s, EH * P, NT * EH * P)
-            for q in range(EH):
-                multiply(s, q, 1)
 
         nc.sync.dma_start(slot_tokens[:], offs)
         nc.scalar.dma_start(out=windows[0, 0][:, 0:T], in_=x_rows[0, 0])
@@ -193,31 +190,39 @@ def tile_moe_pre_lin_bias_kernel(tc, xT, w, b, gate, offs, pos1, pos2, pos3, pos
         for j in range(PACK):
             gather_x(last, j, 2 * C, 3 * C)
         round_x(last, 2 * C, 3 * C)
-        quantise_w(last, 0, EH * P)
+        quantise_w(last, 0, 2 * P)
         quantise_x(last, 0, 2 * C)
         multiply(last, 0, 0)
         multiply(last, 1, 0)
+        x_end = keep.tile([P, PACK, C], F32, name="end", align_bytes=64)
         for j in range(PACK):
-            gather_x(last, j, 3 * C, 4 * C)
-        round_x(last, 3 * C, 4 * C)
+            gather_x(last, j, 3 * C, 4 * C, x_end)
+        interleave(x_bf[last][:, PACK * 3 * C : PACK * 4 * C], x_end[:])
+        quantise_w(last, 2 * P, EH * P)
         for q in range(2, EH):
             quantise_x(last, q * C, (q + 1) * C)
             multiply(last, q, 0)
         for q in range(EH):
             add_bias(h, q, 0)
-        for s in range(STEPS - HELD, STEPS):
-            finish_held(s)
+        quantise_w(STEPS - HELD, EH * P, NT * EH * P)
+        codes_end = keep.tile([P, HELD - 1, EH * P], U32, name="end", align_bytes=64)
+        for i, s in enumerate(range(last, STEPS - HELD, -1)):
+            late_codes[s] = codes_end[:, i, :]
+            nc.vector.quantize_mx(out=late_codes[s].bitcast(FP8X4), scales=w_scales[s][:, EH * P :], in_=w_bf[s][:, PACK * EH * P :])
         for q in range(EH):
+            for s in [last] + list(range(STEPS - HELD, last)):
+                multiply(s, q, 1)
             add_bias(h, q, 1)
 
         picked = [two.tile([P, TOP, T], F32, name="x_f32") for t in range(NT)]
         total = [two.tile([P, 2, T], F32, name="x_bf", align_bytes=64) for t in range(NT)]
 
-        for t in range(NT):
+        pieces = [(0, 0, T), (1, 0, T // 2), (1, T // 2, T)]
+        for i, (t, lo, hi) in enumerate(pieces):
             for r in range(TOP):
-                nc.vector.tensor_copy(picked[t][:, r, :], y[t][:].indirect(token_slots[r][:]))
+                nc.vector.tensor_copy(picked[t][:, r, lo:hi], y[t][:].indirect(token_slots[r][:, lo // LIST : hi // LIST]))
             for r in range(1, TOP):
-                engine = nc.vector if t == NT - 1 and r > 1 else nc.gpsimd
-                left = picked[t][:, 0, :] if r == 1 else total[t][:, r % 2, :]
-                engine.tensor_tensor(total[t][:, (r + 1) % 2, :], left, picked[t][:, r, :], ADD)
-            nc.sync.dma_start(out=out[t * P : (t + 1) * P, :], in_=total[t][:, 0, :])
+                engine = nc.vector if i == len(pieces) - 1 and r > 1 else nc.gpsimd
+                left = picked[t][:, 0, lo:hi] if r == 1 else total[t][:, r % 2, lo:hi]
+                engine.tensor_tensor(total[t][:, (r + 1) % 2, lo:hi], left, picked[t][:, r, lo:hi], ADD)
+            nc.sync.dma_start(out=out[t * P : (t + 1) * P, lo:hi], in_=total[t][:, 0, lo:hi])

@@ -30,6 +30,7 @@ NT = N // P
 WINDOW = SH + 16
 LIST = 16
 HELD = 3
+STAGE = 4 * PACK * SH
 
 
 def tile_moe_pre_lin_bias_kernel(tc, xT, w, b, gate, offs, pos1, pos2, pos3, pos4, out):
@@ -42,6 +43,7 @@ def tile_moe_pre_lin_bias_kernel(tc, xT, w, b, gate, offs, pos1, pos2, pos3, pos
         two = ctx.enter_context(tc.tile_pool(name="two", bufs=2))
         three = ctx.enter_context(tc.tile_pool(name="three", bufs=3))
         four = ctx.enter_context(tc.tile_pool(name="four", bufs=4))
+        stage = ctx.enter_context(tc.tile_pool(name="stage", bufs=1))
         psum = ctx.enter_context(tc.psum_pool(name="psum", bufs=1))
 
         slot_tokens = keep.tile([P, S // LIST], U16, name="slot_tokens")
@@ -92,7 +94,7 @@ def tile_moe_pre_lin_bias_kernel(tc, xT, w, b, gate, offs, pos1, pos2, pos3, pos
         def gather_x(s, j, lo, hi, into=None):
             h, g = divmod(s, PASSES)
             if j == 0 and lo == 0:
-                x_f32[s] = two.tile([P, PACK, SH], F32, name="x_f32")
+                x_f32[s] = stage.tile([P, PACK, SH], F32, name="x_f32_%d" % (s % 2), offset=(s % 2) * STAGE, align_bytes=64)
             a, z = h * SH + lo, h * SH + hi
             nc.vector.tensor_tensor(
                 x_f32[s][:, j, lo:hi] if into is None else into[:, j, :],
@@ -116,7 +118,7 @@ def tile_moe_pre_lin_bias_kernel(tc, xT, w, b, gate, offs, pos1, pos2, pos3, pos
             g = s % PASSES
             slots = slice(q * C, (q + 1) * C)
             cols = slice((t * EH + q) * P, (t * EH + q + 1) * P)
-            closing = STEPS - 2 if (s >= STEPS - HELD and t == 1) else s - g + PASSES - 1
+            closing = s - g + PASSES - 1
             if g == 0:
                 banks[q, t] = psum.tile([P, C], F32, name="bank%d_%d" % (q, t))
             nc.tensor.matmul_mx(
@@ -183,46 +185,41 @@ def tile_moe_pre_lin_bias_kernel(tc, xT, w, b, gate, offs, pos1, pos2, pos3, pos
                 finish(s - 1)
 
         h = HALVES - 1
+        cut = (EH - 1) * C
         for j in range(PACK):
-            gather_x(last, j, 0, 2 * C)
+            gather_x(last, j, 0, cut)
         round_x(last, 0, 2 * C)
+        round_x(last, 2 * C, cut)
+        x_end = stage.tile([P, PACK, C], F32, name="x_end", offset=0, align_bytes=64)
+        for j in range(PACK):
+            gather_x(last, j, cut, SH, x_end)
+        interleave(x_bf[last][:, PACK * cut :], x_end[:])
         finish(last - 1)
-        for j in range(PACK):
-            gather_x(last, j, 2 * C, 3 * C)
-        round_x(last, 2 * C, 3 * C)
-        quantise_w(last, 0, 2 * P)
-        quantise_x(last, 0, 2 * C)
-        multiply(last, 0, 0)
-        multiply(last, 1, 0)
-        x_end = keep.tile([P, PACK, C], F32, name="end", align_bytes=64)
-        for j in range(PACK):
-            gather_x(last, j, 3 * C, 4 * C, x_end)
-        interleave(x_bf[last][:, PACK * 3 * C : PACK * 4 * C], x_end[:])
-        quantise_w(last, 2 * P, EH * P)
-        for q in range(2, EH):
-            quantise_x(last, q * C, (q + 1) * C)
-            multiply(last, q, 0)
-        for q in range(EH):
-            add_bias(h, q, 0)
-        quantise_w(STEPS - HELD, EH * P, NT * EH * P)
-        codes_end = keep.tile([P, HELD - 1, EH * P], U32, name="end", align_bytes=64)
-        for i, s in enumerate(range(last, STEPS - HELD, -1)):
+        quantise_w(last, 0, EH * P)
+        for lo, hi in ((0, 2), (2, 3), (3, 4)):
+            quantise_x(last, lo * C, hi * C)
+            for q in range(lo, hi):
+                multiply(last, q, 0)
+                add_bias(h, q, 0)
+        codes_end = stage.tile([P, HELD, EH * P], U32, name="codes_end", offset=0, align_bytes=64)
+        for i, s in enumerate(range(STEPS - HELD, STEPS)):
             late_codes[s] = codes_end[:, i, :]
             nc.vector.quantize_mx(out=late_codes[s].bitcast(FP8X4), scales=w_scales[s][:, EH * P :], in_=w_bf[s][:, PACK * EH * P :])
-        for q in range(EH):
-            for s in [last] + list(range(STEPS - HELD, last)):
+            for q in range(EH):
                 multiply(s, q, 1)
-            add_bias(h, q, 1)
+                if s == last:
+                    add_bias(h, q, 1)
 
-        picked = [two.tile([P, TOP, T], F32, name="x_f32") for t in range(NT)]
-        total = [two.tile([P, 2, T], F32, name="x_bf", align_bytes=64) for t in range(NT)]
-
-        pieces = [(0, 0, T), (1, 0, T // 2), (1, T // 2, T)]
-        for i, (t, lo, hi) in enumerate(pieces):
+        running = [stage.tile([P, TOP, T], F32, name="running%d" % t, offset=STAGE + t * 4 * TOP * T, align_bytes=64) for t in range(NT)]
+        token_halves = [slice(0, T // 2), slice(T // 2, T)]
+        for t in range(NT):
             for r in range(TOP):
-                nc.vector.tensor_copy(picked[t][:, r, lo:hi], y[t][:].indirect(token_slots[r][:, lo // LIST : hi // LIST]))
-            for r in range(1, TOP):
-                engine = nc.vector if i == len(pieces) - 1 and r > 1 else nc.gpsimd
-                left = picked[t][:, 0, lo:hi] if r == 1 else total[t][:, r % 2, lo:hi]
-                engine.tensor_tensor(total[t][:, (r + 1) % 2, lo:hi], left, picked[t][:, r, lo:hi], ADD)
-            nc.sync.dma_start(out=out[t * P : (t + 1) * P, lo:hi], in_=total[t][:, 0, lo:hi])
+                for i, tokens in enumerate(token_halves):
+                    picked = y[t][:].indirect(token_slots[r][:, tokens.start // LIST : tokens.stop // LIST])
+                    if r == 0:
+                        nc.vector.tensor_copy(running[t][:, 0, tokens], picked)
+                    else:
+                        nc.vector.tensor_tensor(running[t][:, r, tokens], picked, running[t][:, r - 1, tokens], ADD)
+                    if r == TOP - 1:
+                        queue = nc.sync if i == 0 else nc.scalar
+                        queue.dma_start(out=out[t * P : (t + 1) * P, tokens], in_=running[t][:, r, tokens])

@@ -29,8 +29,9 @@ STEPS = HALVES * PASSES
 NT = N // P
 WINDOW = SH + 16
 LIST = 16
-HELD = 3
+HELD = 4
 STAGE = 4 * PACK * SH
+CUT = 5 * C // 2
 
 
 def tile_moe_pre_lin_bias_kernel(tc, xT, w, b, gate, offs, pos1, pos2, pos3, pos4, out):
@@ -41,7 +42,6 @@ def tile_moe_pre_lin_bias_kernel(tc, xT, w, b, gate, offs, pos1, pos2, pos3, pos
     with ExitStack() as ctx:
         keep = ctx.enter_context(tc.tile_pool(name="keep", bufs=1))
         two = ctx.enter_context(tc.tile_pool(name="two", bufs=2))
-        three = ctx.enter_context(tc.tile_pool(name="three", bufs=3))
         four = ctx.enter_context(tc.tile_pool(name="four", bufs=4))
         stage = ctx.enter_context(tc.tile_pool(name="stage", bufs=1))
         psum = ctx.enter_context(tc.psum_pool(name="psum", bufs=1))
@@ -78,23 +78,25 @@ def tile_moe_pre_lin_bias_kernel(tc, xT, w, b, gate, offs, pos1, pos2, pos3, pos
 
         def round_w(s, pair):
             if pair == 0:
-                w_bf[s] = three.tile([P, EH * N * PACK], BF16, name="w_bf", align_bytes=64)
-            for q in range(2):
-                rows = w_raw[s, pair][:, q, :].rearrange("p (j n) -> p j n", j=PACK)
-                for t in range(NT):
-                    col = (t * EH + 2 * pair + q) * P * PACK
-                    interleave(w_bf[s][:, col : col + P * PACK], rows[:, :, t * P : (t + 1) * P])
+                w_bf[s] = four.tile([P, EH * N * PACK], BF16, name="w_bf", align_bytes=64)
+            rows = w_raw[s, pair][:].rearrange("p q (j t c i) -> p t q c j i", j=PACK, t=NT, i=4)
+            for t in range(NT):
+                col = (t * EH + 2 * pair) * P * PACK
+                nc.scalar.copy(
+                    out=w_bf[s][:, col : col + 2 * P * PACK].rearrange("p (q c i j) -> p q c j i", q=2, i=4, j=PACK),
+                    in_=rows[:, t],
+                )
 
         def quantise_w(s, lo, hi):
             if lo == 0:
-                w_codes[s] = three.tile([P, EH * N], U32, name="w_codes", align_bytes=64)
-                w_scales[s] = three.tile([P, EH * N], U8, name="w_scales", align_bytes=64)
+                w_codes[s] = two.tile([P, EH * N], U32, name="w_codes", align_bytes=64)
+                w_scales[s] = four.tile([P, EH * N], U8, name="w_scales", align_bytes=64)
             nc.vector.quantize_mx(out=w_codes[s][:, lo:hi].bitcast(FP8X4), scales=w_scales[s][:, lo:hi], in_=w_bf[s][:, PACK * lo : PACK * hi])
 
         def gather_x(s, j, lo, hi, into=None):
             h, g = divmod(s, PASSES)
             if j == 0 and lo == 0:
-                x_f32[s] = stage.tile([P, PACK, SH], F32, name="x_f32_%d" % (s % 2), offset=(s % 2) * STAGE, align_bytes=64)
+                x_f32[s] = stage.tile([P, PACK, CUT if s == STEPS - 1 else SH], F32, name="x_f32_%d" % (s % 2), offset=(s % 2) * STAGE, align_bytes=64)
             a, z = h * SH + lo, h * SH + hi
             nc.vector.tensor_tensor(
                 x_f32[s][:, j, lo:hi] if into is None else into[:, j, :],
@@ -109,14 +111,16 @@ def tile_moe_pre_lin_bias_kernel(tc, xT, w, b, gate, offs, pos1, pos2, pos3, pos
             interleave(x_bf[s][:, PACK * lo : PACK * hi], x_f32[s][:, :, lo:hi])
 
         def quantise_x(s, lo, hi):
-            if lo == 0:
-                x_codes[s] = three.tile([P, SH], U32, name="x_codes", align_bytes=64)
-                x_scales[s] = three.tile([P, SH], U8, name="x_scales", align_bytes=64)
-            nc.vector.quantize_mx(out=x_codes[s][:, lo:hi].bitcast(FP8X4), scales=x_scales[s][:, lo:hi], in_=x_bf[s][:, PACK * lo : PACK * hi])
+            pool, tag = (four, "") if lo == 0 else (keep, "_%d" % lo)
+            codes = pool.tile([P, hi - lo], U32, name="x_codes" + tag, align_bytes=64)
+            scales = pool.tile([P, hi - lo], U8, name="x_scales" + tag, align_bytes=64)
+            nc.vector.quantize_mx(out=codes[:].bitcast(FP8X4), scales=scales[:], in_=x_bf[s][:, PACK * lo : PACK * hi])
+            for q in range(lo // C, hi // C):
+                x_codes[s, q] = codes[:, q * C - lo : (q + 1) * C - lo]
+                x_scales[s, q] = scales[:, q * C - lo : (q + 1) * C - lo]
 
         def multiply(s, q, t):
             g = s % PASSES
-            slots = slice(q * C, (q + 1) * C)
             cols = slice((t * EH + q) * P, (t * EH + q + 1) * P)
             closing = s - g + PASSES - 1
             if g == 0:
@@ -125,8 +129,8 @@ def tile_moe_pre_lin_bias_kernel(tc, xT, w, b, gate, offs, pos1, pos2, pos3, pos
                 out=banks[q, t][:],
                 lhsT=(late_codes[s][:, q * P : (q + 1) * P] if t == 1 and s in late_codes else w_codes[s][:, cols]).bitcast(FP8X4),
                 lhsT_scale=w_scales[s][:, cols],
-                rhs=x_codes[s][:, slots].bitcast(FP8X4),
-                rhs_scale=x_scales[s][:, slots],
+                rhs=x_codes[s, q].bitcast(FP8X4),
+                rhs_scale=x_scales[s, q],
                 start=(g == 0),
                 stop=(s == closing),
             )
@@ -178,19 +182,18 @@ def tile_moe_pre_lin_bias_kernel(tc, xT, w, b, gate, offs, pos1, pos2, pos3, pos
                 gather_x(s, 0, 0, SH)
             for j in range(1, PACK):
                 gather_x(s, j, 0, SH)
-            round_x(s, 0, SH)
             round_w(s + 1, 0)
             round_w(s + 1, 1)
+            round_x(s, 0, SH)
             if s > 0:
                 finish(s - 1)
 
         h = HALVES - 1
-        cut = (EH - 1) * C
+        cut = CUT
         for j in range(PACK):
             gather_x(last, j, 0, cut)
-        round_x(last, 0, 2 * C)
-        round_x(last, 2 * C, cut)
-        x_end = stage.tile([P, PACK, C], F32, name="x_end", offset=0, align_bytes=64)
+        round_x(last, 0, cut)
+        x_end = stage.tile([P, PACK, SH - cut], F32, name="x_end", offset=STAGE + 4 * PACK * cut, align_bytes=64)
         for j in range(PACK):
             gather_x(last, j, cut, SH, x_end)
         interleave(x_bf[last][:, PACK * cut :], x_end[:])
@@ -201,7 +204,7 @@ def tile_moe_pre_lin_bias_kernel(tc, xT, w, b, gate, offs, pos1, pos2, pos3, pos
             for q in range(lo, hi):
                 multiply(last, q, 0)
                 add_bias(h, q, 0)
-        codes_end = stage.tile([P, HELD, EH * P], U32, name="codes_end", offset=0, align_bytes=64)
+        codes_end = stage.tile([P, HELD, EH * P], U32, name="codes_end", offset=2 * STAGE - 4 * HELD * EH * P, align_bytes=64)
         for i, s in enumerate(range(STEPS - HELD, STEPS)):
             late_codes[s] = codes_end[:, i, :]
             nc.vector.quantize_mx(out=late_codes[s].bitcast(FP8X4), scales=w_scales[s][:, EH * P :], in_=w_bf[s][:, PACK * EH * P :])
@@ -210,7 +213,7 @@ def tile_moe_pre_lin_bias_kernel(tc, xT, w, b, gate, offs, pos1, pos2, pos3, pos
                 if s == last:
                     add_bias(h, q, 1)
 
-        running = [stage.tile([P, TOP, T], F32, name="running%d" % t, offset=STAGE + t * 4 * TOP * T, align_bytes=64) for t in range(NT)]
+        running = [stage.tile([P, TOP, T], F32, name="running%d" % t, offset=t * 4 * TOP * T, align_bytes=64) for t in range(NT)]
         token_halves = [slice(0, T // 2), slice(T // 2, T)]
         for t in range(NT):
             for r in range(TOP):

@@ -28,6 +28,15 @@ SH = S // HALVES
 STEPS = HALVES * PASSES
 NT = N // P
 WINDOW = SH + 16
+STAGE_BYTES = 4 * PACK * SH
+WIDE_PASSES = 2
+WIDE_WINDOW = 2 * WINDOW
+RING = 3
+SWAP = 2 * PACK * SH
+X_PLACE = {0: 5, 4: 4, 1: 1, 5: 0, 2: 4, 3: 5, 6: 0, 7: 1}
+W_PLACE = (0, 2, 4, 0, 2, 0, 2, 2)
+BIG = 4 * WIDE_WINDOW
+ODD = STAGE_BYTES + PACK * 4 * WINDOW
 LIST = 16
 HELD = 4
 STAGE = 4 * PACK * SH
@@ -41,25 +50,33 @@ def tile_moe_pre_lin_bias_kernel(tc, xT, w, b, gate, offs, pos1, pos2, pos3, pos
 
     with ExitStack() as ctx:
         keep = ctx.enter_context(tc.tile_pool(name="keep", bufs=1))
-        two = ctx.enter_context(tc.tile_pool(name="two", bufs=2))
-        four = ctx.enter_context(tc.tile_pool(name="four", bufs=4))
         stage = ctx.enter_context(tc.tile_pool(name="stage", bufs=1))
+        tokens_pool = ctx.enter_context(tc.tile_pool(name="tokens", bufs=1))
+        swap = ctx.enter_context(tc.tile_pool(name="swap", bufs=1))
+        codes_pool = ctx.enter_context(tc.tile_pool(name="codes", bufs=1))
         psum = ctx.enter_context(tc.psum_pool(name="psum", bufs=1))
 
         slot_tokens = keep.tile([P, S // LIST], U16, name="slot_tokens")
         token_slots = [keep.tile([P, T // LIST], U16, name="token_slots%d" % r) for r in range(TOP)]
         gates = keep.tile([P, S], F32, name="gates")
         bias = keep.tile([P, NT, E], F32, name="bias")
-        windows = {(g, j): keep.tile([P, WINDOW], F32, name="window%d_%d" % (g, j)) for g in range(PASSES) for j in range(PACK)}
-        y = [keep.tile([P, S], F32, name="y%d" % t) for t in range(NT)]
+        windows = {}
+        y = [tokens_pool.tile([P, S], F32, name="y%d" % t, offset=(4 + t) * BIG, align_bytes=64) for t in range(NT)]
 
         w_raw, w_bf, w_codes, w_scales = {}, {}, {}, {}
         x_f32, x_bf, x_codes, x_scales = {}, {}, {}, {}
         banks = {}
         late_codes = {}
+        x_wide = {}
 
-        def load_x(g, j):
-            nc.sync.dma_start(out=windows[g, j][:, 0:T], in_=x_rows[g, j])
+        def load_x(g, j, queue=nc.sync):
+            if g < WIDE_PASSES:
+                windows[g, j] = tokens_pool.tile([P, WIDE_WINDOW], F32, name="wide%d_%d" % (g, j), offset=(g * PACK + j) * BIG, align_bytes=64)
+            elif g == WIDE_PASSES:
+                windows[g, j] = stage.tile([P, WINDOW], F32, name="window2_%d" % j, offset=STAGE + j * 4 * WINDOW, align_bytes=64)
+            else:
+                windows[g, j] = tokens_pool.tile([P, WINDOW], F32, name="window3_%d" % j, offset=j * 4 * WINDOW, align_bytes=64)
+            queue.dma_start(out=windows[g, j][:, 0:T], in_=x_rows[g, j])
 
         def load_gate(lo, hi):
             nc.sync.dma_start(out=gates[:, lo:hi], in_=gate[0:P, lo:hi])
@@ -67,7 +84,8 @@ def tile_moe_pre_lin_bias_kernel(tc, xT, w, b, gate, offs, pos1, pos2, pos3, pos
         def load_w(s, pair):
             h, g = divmod(s, PASSES)
             e0 = h * EH + 2 * pair
-            w_raw[s, pair] = four.tile([P, 2, PACK * N], F32, name="w_raw")
+            place = W_PLACE[s] + pair
+            w_raw[s, pair] = swap.tile([P, 2, PACK * N], F32, name="w_raw%d" % place, offset=place * SWAP, align_bytes=64)
             nc.sync.dma_start(out=w_raw[s, pair][:], in_=w_rows[g, :, e0 : e0 + 2, :])
 
         def interleave(dst, src):
@@ -78,7 +96,10 @@ def tile_moe_pre_lin_bias_kernel(tc, xT, w, b, gate, offs, pos1, pos2, pos3, pos
 
         def round_w(s, pair):
             if pair == 0:
-                w_bf[s] = four.tile([P, EH * N * PACK], BF16, name="w_bf", align_bytes=64)
+                if s % 4 < 2:
+                    w_bf[s] = keep.tile([P, EH * N * PACK], BF16, name="w_bf%d" % (s % 4), align_bytes=64)
+                else:
+                    w_bf[s] = tokens_pool.tile([P, EH * N * PACK], BF16, name="w_bf%d" % (s % 4), offset=(s % 4) * BIG, align_bytes=64)
             rows = w_raw[s, pair][:].rearrange("p q (j t c i) -> p t q c j i", j=PACK, t=NT, i=4)
             for t in range(NT):
                 col = (t * EH + 2 * pair) * P * PACK
@@ -89,14 +110,16 @@ def tile_moe_pre_lin_bias_kernel(tc, xT, w, b, gate, offs, pos1, pos2, pos3, pos
 
         def quantise_w(s, lo, hi):
             if lo == 0:
-                w_codes[s] = two.tile([P, EH * N], U32, name="w_codes", align_bytes=64)
-                w_scales[s] = four.tile([P, EH * N], U8, name="w_scales", align_bytes=64)
+                width = EH * N if s < PASSES else EH * P
+                place = s * EH * N if s < PASSES else (s - PASSES) * EH * P
+                w_codes[s] = codes_pool.tile([P, width], U32, name="w_codes%d" % s, offset=4 * place, align_bytes=64)
+                w_scales[s] = keep.tile([P, EH * N], U8, name="w_scales%d" % (0, 1, 2, 3, 0, 4, 1, 2)[s], align_bytes=64)
             nc.vector.quantize_mx(out=w_codes[s][:, lo:hi].bitcast(FP8X4), scales=w_scales[s][:, lo:hi], in_=w_bf[s][:, PACK * lo : PACK * hi])
 
         def gather_x(s, j, lo, hi, into=None):
             h, g = divmod(s, PASSES)
             if j == 0 and lo == 0:
-                x_f32[s] = stage.tile([P, PACK, CUT if s == STEPS - 1 else SH], F32, name="x_f32_%d" % (s % 2), offset=(s % 2) * STAGE, align_bytes=64)
+                x_f32[s] = stage.tile([P, PACK, CUT if s == STEPS - 1 else SH], F32, name="x_f32_%d" % (s % 2), offset=(s % 2) * ODD, align_bytes=64)
             a, z = h * SH + lo, h * SH + hi
             nc.vector.tensor_tensor(
                 x_f32[s][:, j, lo:hi] if into is None else into[:, j, :],
@@ -105,15 +128,29 @@ def tile_moe_pre_lin_bias_kernel(tc, xT, w, b, gate, offs, pos1, pos2, pos3, pos
                 MULT,
             )
 
+        def gather_wide(g, j, a, z):
+            if j == 0 and a == 0:
+                wide = stage.tile([P, PACK, S], F32, name="x_wide%d" % g, offset=g * ODD, align_bytes=64)
+                x_wide[g] = wide
+                for half in range(HALVES):
+                    x_f32[half * PASSES + g] = wide[:, :, half * SH : (half + 1) * SH]
+            nc.vector.tensor_tensor(x_wide[g][:, j, a:z], windows[g, j][:].indirect(slot_tokens[:, a // LIST : z // LIST]), gates[:, a:z], MULT)
+
         def round_x(s, lo, hi):
             if lo == 0:
-                x_bf[s] = two.tile([P, SH * PACK], BF16, name="x_bf", align_bytes=64)
+                place = X_PLACE[s]
+                x_bf[s] = swap.tile([P, SH * PACK], BF16, name="x_bf%d" % place, offset=place * SWAP, align_bytes=64)
             interleave(x_bf[s][:, PACK * lo : PACK * hi], x_f32[s][:, :, lo:hi])
 
         def quantise_x(s, lo, hi):
-            pool, tag = (four, "") if lo == 0 else (keep, "_%d" % lo)
-            codes = pool.tile([P, hi - lo], U32, name="x_codes" + tag, align_bytes=64)
-            scales = pool.tile([P, hi - lo], U8, name="x_scales" + tag, align_bytes=64)
+            if s == PASSES + 1 or s == STEPS - 1:
+                at = 6 * BIG if s == PASSES + 1 else (7 * BIG + 5 * lo)
+                codes = tokens_pool.tile([P, hi - lo], U32, name="x_codes%d_%d" % (s, lo), offset=at, align_bytes=64)
+                scales = tokens_pool.tile([P, hi - lo], U8, name="x_scales%d_%d" % (s, lo), offset=at + 4 * (hi - lo), align_bytes=64)
+            else:
+                tag = "kept" if s == PASSES else "ring"
+                codes = keep.tile([P, hi - lo], U32, name="x_codes_" + tag, align_bytes=64)
+                scales = keep.tile([P, hi - lo], U8, name="x_scales_" + tag, align_bytes=64)
             nc.vector.quantize_mx(out=codes[:].bitcast(FP8X4), scales=scales[:], in_=x_bf[s][:, PACK * lo : PACK * hi])
             for q in range(lo // C, hi // C):
                 x_codes[s, q] = codes[:, q * C - lo : (q + 1) * C - lo]
@@ -141,8 +178,10 @@ def tile_moe_pre_lin_bias_kernel(tc, xT, w, b, gate, offs, pos1, pos2, pos3, pos
 
         def finish(s):
             tiles = NT if s < STEPS - HELD else 1
-            quantise_w(s, 0, tiles * EH * P)
-            quantise_x(s, 0, SH)
+            if s not in w_codes:
+                quantise_w(s, 0, tiles * EH * P)
+            if (s, 0) not in x_codes:
+                quantise_x(s, 0, SH)
             for t in range(tiles):
                 for q in range(EH):
                     multiply(s, q, t)
@@ -152,48 +191,89 @@ def tile_moe_pre_lin_bias_kernel(tc, xT, w, b, gate, offs, pos1, pos2, pos3, pos
                         add_bias(s // PASSES, q, t)
 
         nc.sync.dma_start(slot_tokens[:], offs)
-        nc.scalar.dma_start(out=windows[0, 0][:, 0:T], in_=x_rows[0, 0])
-        load_gate(0, C)
-        load_gate(C, SH)
+        def fetch_w(s):
+            load_w(s, 0)
+            load_w(s, 1)
+
+        def round_both(s):
+            round_w(s, 0)
+            round_w(s, 1)
+
+        gate_cuts = (0, C, SH, S)
+        load_x(0, 0, nc.scalar)
+        for lo, hi in zip(gate_cuts, gate_cuts[1:]):
+            load_gate(lo, hi)
         load_x(0, 1)
         load_w(0, 0)
         load_x(0, 2)
-        load_x(0, 3)
         load_w(0, 1)
+        load_x(0, 3)
+        fetch_w(1)
+        load_w(2, 0)
+        load_x(1, 0)
+        load_w(2, 1)
+        load_x(1, 1)
+        round_both(0)
+        round_both(1)
+        for lo, hi in zip(gate_cuts, gate_cuts[1:]):
+            gather_wide(0, 0, lo, hi)
+        for j in range(1, PACK):
+            gather_wide(0, j, 0, S)
+        round_both(2)
+        load_x(1, 2)
+        load_x(1, 3)
+        fetch_w(3)
+        fetch_w(4)
+        round_x(0, 0, SH)
+        round_x(PASSES, 0, SH)
+        round_both(3)
+        fetch_w(5)
+        for g in range(WIDE_PASSES, PASSES):
+            for j in range(PACK):
+                load_x(g, j)
+        nc.sync.dma_start(out=bias[:], in_=b.rearrange("(t p) e -> p t e", p=P))
+        for r, pos in enumerate((pos1, pos2, pos3, pos4)):
+            nc.sync.dma_start(token_slots[r][:], pos)
+        quantise_w(0, 0, NT * EH * P)
+        quantise_w(1, 0, NT * EH * P)
+        gather_wide(1, 0, 0, S)
+        gather_wide(1, 1, 0, S)
+        finish(0)
+        gather_wide(1, 2, 0, S)
+        quantise_x(PASSES, 0, SH)
+        round_both(4)
+        fetch_w(6)
+        round_both(5)
+        gather_wide(1, 3, 0, S)
+        round_x(1, 0, SH)
+        round_x(PASSES + 1, 0, SH)
 
         last = STEPS - 1
-        for s in range(last):
-            if s + 1 < PASSES:
-                for j in range(PACK):
-                    load_x(s + 1, j)
-            load_w(s + 1, 0)
-            load_w(s + 1, 1)
-            if s == 1:
-                load_gate(SH, S)
-                nc.sync.dma_start(out=bias[:], in_=b.rearrange("(t p) e -> p t e", p=P))
-                for r, pos in enumerate((pos1, pos2, pos3, pos4)):
-                    nc.sync.dma_start(token_slots[r][:], pos)
-            if s == 0:
-                round_w(0, 0)
-                round_w(0, 1)
-                gather_x(0, 0, 0, C)
-                gather_x(0, 0, C, SH)
-            else:
-                gather_x(s, 0, 0, SH)
-            for j in range(1, PACK):
-                gather_x(s, j, 0, SH)
-            round_w(s + 1, 0)
-            round_w(s + 1, 1)
-            round_x(s, 0, SH)
-            if s > 0:
-                finish(s - 1)
+        for j in range(PACK):
+            gather_x(2, j, 0, SH)
+        finish(1)
+        quantise_x(PASSES + 1, 0, SH)
+        round_x(2, 0, SH)
+        round_both(6)
+        fetch_w(7)
+        for j in range(PACK):
+            gather_x(3, j, 0, SH)
+        round_x(3, 0, SH)
+        finish(2)
+        round_both(7)
+        for j in range(PACK):
+            gather_x(6, j, 0, SH)
+        round_x(6, 0, SH)
+        finish(3)
+        finish(4)
+        finish(5)
 
         h = HALVES - 1
         cut = CUT
         for j in range(PACK):
             gather_x(last, j, 0, cut)
         round_x(last, 0, cut)
-        x_end = stage.tile([P, PACK, SH - cut], F32, name="x_end", offset=STAGE + 4 * PACK * cut, align_bytes=64)
+        x_end = stage.tile([P, PACK, SH - cut], F32, name="x_end", offset=ODD + 4 * PACK * cut, align_bytes=64)
         for j in range(PACK):
             gather_x(last, j, cut, SH, x_end)
         interleave(x_bf[last][:, PACK * cut :], x_end[:])
@@ -204,7 +284,7 @@ def tile_moe_pre_lin_bias_kernel(tc, xT, w, b, gate, offs, pos1, pos2, pos3, pos
             for q in range(lo, hi):
                 multiply(last, q, 0)
                 add_bias(h, q, 0)
-        codes_end = stage.tile([P, HELD, EH * P], U32, name="codes_end", offset=2 * STAGE - 4 * HELD * EH * P, align_bytes=64)
+        codes_end = stage.tile([P, HELD, EH * P], U32, name="codes_end", offset=ODD + STAGE - 4 * HELD * EH * P, align_bytes=64)
         for i, s in enumerate(range(STEPS - HELD, STEPS)):
             late_codes[s] = codes_end[:, i, :]
             nc.vector.quantize_mx(out=late_codes[s].bitcast(FP8X4), scales=w_scales[s][:, EH * P :], in_=w_bf[s][:, PACK * EH * P :])
@@ -213,7 +293,7 @@ def tile_moe_pre_lin_bias_kernel(tc, xT, w, b, gate, offs, pos1, pos2, pos3, pos
                 if s == last:
                     add_bias(h, q, 1)
 
-        running = [stage.tile([P, TOP, T], F32, name="running%d" % t, offset=t * 4 * TOP * T, align_bytes=64) for t in range(NT)]
+        running = [stage.tile([P, TOP, T], F32, name="running%d" % t, offset=ODD + STAGE + t * 4 * TOP * T, align_bytes=64) for t in range(NT)]
         token_halves = [slice(0, T // 2), slice(T // 2, T)]
         for t in range(NT):
             for r in range(TOP):

@@ -54,32 +54,33 @@ def tile_moe_pre_lin_bias_kernel(tc, xT, w, b, gate, offs, pos1, pos2, pos3, pos
         tokens_pool = ctx.enter_context(tc.tile_pool(name="tokens", bufs=1))
         swap = ctx.enter_context(tc.tile_pool(name="swap", bufs=1))
         codes_pool = ctx.enter_context(tc.tile_pool(name="codes", bufs=1))
+        sums = ctx.enter_context(tc.tile_pool(name="sums", bufs=1))
         psum = ctx.enter_context(tc.psum_pool(name="psum", bufs=1))
 
         slot_tokens = keep.tile([P, S // LIST], U16, name="slot_tokens")
         token_slots = [keep.tile([P, T // LIST], U16, name="token_slots%d" % r) for r in range(TOP)]
         gates = keep.tile([P, S], F32, name="gates")
-        bias = keep.tile([P, NT, E], F32, name="bias")
+        bias = sums.tile([P, NT, E], F32, name="bias", offset=0)
         windows = {}
         y = [tokens_pool.tile([P, S], F32, name="y%d" % t, offset=(4 + t) * BIG, align_bytes=64) for t in range(NT)]
 
         w_raw, w_bf, w_codes, w_scales = {}, {}, {}, {}
         x_f32, x_bf, x_codes, x_scales = {}, {}, {}, {}
         banks = {}
-        late_codes = {}
+        w_now, w_held = {}, {}
         x_wide = {}
 
-        def load_x(g, j, queue=nc.sync):
+        def load_x(g, j):
             if g < WIDE_PASSES:
                 windows[g, j] = tokens_pool.tile([P, WIDE_WINDOW], F32, name="wide%d_%d" % (g, j), offset=(g * PACK + j) * BIG, align_bytes=64)
             elif g == WIDE_PASSES:
                 windows[g, j] = stage.tile([P, WINDOW], F32, name="window2_%d" % j, offset=STAGE + j * 4 * WINDOW, align_bytes=64)
             else:
                 windows[g, j] = tokens_pool.tile([P, WINDOW], F32, name="window3_%d" % j, offset=j * 4 * WINDOW, align_bytes=64)
-            queue.dma_start(out=windows[g, j][:, 0:T], in_=x_rows[g, j])
+            nc.sync.dma_start(out=windows[g, j][:, 0:T], in_=x_rows[g, j])
 
-        def load_gate(lo, hi):
-            nc.sync.dma_start(out=gates[:, lo:hi], in_=gate[0:P, lo:hi])
+        def load_gate(lo, hi, queue):
+            queue.dma_start(out=gates[:, lo:hi], in_=gate[0:P, lo:hi])
 
         def load_w(s, pair):
             h, g = divmod(s, PASSES)
@@ -94,27 +95,42 @@ def tile_moe_pre_lin_bias_kernel(tc, xT, w, b, gate, offs, pos1, pos2, pos3, pos
                 in_=src.rearrange("p t (c i) -> p c t i", i=4),
             )
 
+        def rounded_tile(slot):
+            if slot < 2:
+                return keep.tile([P, EH * N * PACK], BF16, name="w_bf%d" % slot, align_bytes=64)
+            return tokens_pool.tile([P, EH * N * PACK], BF16, name="w_bf%d" % slot, offset=slot * BIG, align_bytes=64)
+
         def round_w(s, pair):
-            if pair == 0:
-                if s % 4 < 2:
-                    w_bf[s] = keep.tile([P, EH * N * PACK], BF16, name="w_bf%d" % (s % 4), align_bytes=64)
-                else:
-                    w_bf[s] = tokens_pool.tile([P, EH * N * PACK], BF16, name="w_bf%d" % (s % 4), offset=(s % 4) * BIG, align_bytes=64)
+            if pair == 0 and s < PASSES:
+                both = rounded_tile(s)
+                w_now[s] = both[:]
+                for t in range(NT):
+                    w_bf[s, t] = both[:].rearrange("p (t e x) -> p t e x", t=NT, e=EH)[:, t]
+            elif pair == 0 and s % 2 == 0:
+                now = rounded_tile(0 if s == PASSES else 3)
+                w_held[s] = rounded_tile(1 if s == PASSES else 2)
+                for u in range(2):
+                    w_now[s + u] = now[:, u * EH * P * PACK : (u + 1) * EH * P * PACK]
+                    w_bf[s + u, 0] = now[:].rearrange("p (u e x) -> p u e x", u=2, e=EH)[:, u]
+                    w_bf[s + u, 1] = w_held[s][:].rearrange("p (e u x) -> p u e x", u=2, e=EH)[:, u]
             rows = w_raw[s, pair][:].rearrange("p q (j t c i) -> p t q c j i", j=PACK, t=NT, i=4)
             for t in range(NT):
-                col = (t * EH + 2 * pair) * P * PACK
                 nc.scalar.copy(
-                    out=w_bf[s][:, col : col + 2 * P * PACK].rearrange("p (q c i j) -> p q c j i", q=2, i=4, j=PACK),
+                    out=w_bf[s, t][:, 2 * pair : 2 * pair + 2, :].rearrange("p q (c i j) -> p q c j i", i=4, j=PACK),
                     in_=rows[:, t],
                 )
 
-        def quantise_w(s, lo, hi):
-            if lo == 0:
-                width = EH * N if s < PASSES else EH * P
-                place = s * EH * N if s < PASSES else (s - PASSES) * EH * P
-                w_codes[s] = codes_pool.tile([P, width], U32, name="w_codes%d" % s, offset=4 * place, align_bytes=64)
-                w_scales[s] = keep.tile([P, EH * N], U8, name="w_scales%d" % (0, 1, 2, 3, 0, 4, 1, 2)[s], align_bytes=64)
-            nc.vector.quantize_mx(out=w_codes[s][:, lo:hi].bitcast(FP8X4), scales=w_scales[s][:, lo:hi], in_=w_bf[s][:, PACK * lo : PACK * hi])
+        def quantise_w(s):
+            tiles = NT if s < PASSES else 1
+            place = s * EH * N if s < PASSES else (s - PASSES) * EH * P
+            codes = codes_pool.tile([P, tiles * EH * P], U32, name="w_codes%d" % s, offset=4 * place, align_bytes=64)
+            scales = keep.tile([P, tiles * EH * P], U8, name="w_scales%d" % (0, 1, 2, 3, 0, 4, 1, 2)[s], align_bytes=64)
+            nc.vector.quantize_mx(out=codes[:].bitcast(FP8X4), scales=scales[:], in_=w_now[s])
+            for t in range(tiles):
+                for q in range(EH):
+                    cols = slice((t * EH + q) * P, (t * EH + q + 1) * P)
+                    w_codes[s, q, t] = codes[:, cols]
+                    w_scales[s, q, t] = scales[:, cols]
 
         def gather_x(s, j, lo, hi, into=None):
             h, g = divmod(s, PASSES)
@@ -158,14 +174,13 @@ def tile_moe_pre_lin_bias_kernel(tc, xT, w, b, gate, offs, pos1, pos2, pos3, pos
 
         def multiply(s, q, t):
             g = s % PASSES
-            cols = slice((t * EH + q) * P, (t * EH + q + 1) * P)
             closing = s - g + PASSES - 1
             if g == 0:
                 banks[q, t] = psum.tile([P, C], F32, name="bank%d_%d" % (q, t))
             nc.tensor.matmul_mx(
                 out=banks[q, t][:],
-                lhsT=(late_codes[s][:, q * P : (q + 1) * P] if t == 1 and s in late_codes else w_codes[s][:, cols]).bitcast(FP8X4),
-                lhsT_scale=w_scales[s][:, cols],
+                lhsT=w_codes[s, q, t].bitcast(FP8X4),
+                lhsT_scale=w_scales[s, q, t],
                 rhs=x_codes[s, q].bitcast(FP8X4),
                 rhs_scale=x_scales[s, q],
                 start=(g == 0),
@@ -178,8 +193,8 @@ def tile_moe_pre_lin_bias_kernel(tc, xT, w, b, gate, offs, pos1, pos2, pos3, pos
 
         def finish(s):
             tiles = NT if s < STEPS - HELD else 1
-            if s not in w_codes:
-                quantise_w(s, 0, tiles * EH * P)
+            if (s, 0, 0) not in w_codes:
+                quantise_w(s)
             if (s, 0) not in x_codes:
                 quantise_x(s, 0, SH)
             for t in range(tiles):
@@ -200,9 +215,9 @@ def tile_moe_pre_lin_bias_kernel(tc, xT, w, b, gate, offs, pos1, pos2, pos3, pos
             round_w(s, 1)
 
         gate_cuts = (0, C, SH, S)
-        load_x(0, 0, nc.scalar)
+        load_x(0, 0)
         for lo, hi in zip(gate_cuts, gate_cuts[1:]):
-            load_gate(lo, hi)
+            load_gate(lo, hi, nc.scalar if lo == 0 else nc.sync)
         load_x(0, 1)
         load_w(0, 0)
         load_x(0, 2)
@@ -234,8 +249,8 @@ def tile_moe_pre_lin_bias_kernel(tc, xT, w, b, gate, offs, pos1, pos2, pos3, pos
         nc.sync.dma_start(out=bias[:], in_=b.rearrange("(t p) e -> p t e", p=P))
         for r, pos in enumerate((pos1, pos2, pos3, pos4)):
             nc.sync.dma_start(token_slots[r][:], pos)
-        quantise_w(0, 0, NT * EH * P)
-        quantise_w(1, 0, NT * EH * P)
+        quantise_w(0)
+        quantise_w(1)
         gather_wide(1, 0, 0, S)
         gather_wide(1, 1, 0, S)
         finish(0)
@@ -278,31 +293,49 @@ def tile_moe_pre_lin_bias_kernel(tc, xT, w, b, gate, offs, pos1, pos2, pos3, pos
             gather_x(last, j, cut, SH, x_end)
         interleave(x_bf[last][:, PACK * cut :], x_end[:])
         finish(last - 1)
-        quantise_w(last, 0, EH * P)
+        quantise_w(last)
         for lo, hi in ((0, 2), (2, 3), (3, 4)):
             quantise_x(last, lo * C, hi * C)
             for q in range(lo, hi):
                 multiply(last, q, 0)
                 add_bias(h, q, 0)
-        codes_end = stage.tile([P, HELD, EH * P], U32, name="codes_end", offset=ODD + STAGE - 4 * HELD * EH * P, align_bytes=64)
-        for i, s in enumerate(range(STEPS - HELD, STEPS)):
-            late_codes[s] = codes_end[:, i, :]
-            nc.vector.quantize_mx(out=late_codes[s].bitcast(FP8X4), scales=w_scales[s][:, EH * P :], in_=w_bf[s][:, PACK * EH * P :])
-            for q in range(EH):
-                multiply(s, q, 1)
-                if s == last:
-                    add_bias(h, q, 1)
+        codes_end = stage.tile([P, EH, PASSES * P], U32, name="codes_end", offset=ODD + STAGE - 4 * HELD * EH * P, align_bytes=64)
+        scales_end = keep.tile([P, EH, PASSES * P], U8, name="scales_end", align_bytes=64)
+        for q in range(EH):
+            for s in range(PASSES, STEPS, 2):
+                cols = slice((s - PASSES) * P, (s - PASSES + 2) * P)
+                nc.vector.quantize_mx(
+                    out=codes_end[:, q, cols].bitcast(FP8X4),
+                    scales=scales_end[:, q, cols],
+                    in_=w_held[s][:, q * 2 * P * PACK : (q + 1) * 2 * P * PACK],
+                )
+                for u in (s, s + 1):
+                    w_codes[u, q, 1] = codes_end[:, q, (u - PASSES) * P : (u - PASSES + 1) * P]
+                    w_scales[u, q, 1] = scales_end[:, q, (u - PASSES) * P : (u - PASSES + 1) * P]
+                    multiply(u, q, 1)
+            add_bias(h, q, 1)
 
         running = [stage.tile([P, TOP, T], F32, name="running%d" % t, offset=ODD + STAGE + t * 4 * TOP * T, align_bytes=64) for t in range(NT)]
-        token_halves = [slice(0, T // 2), slice(T // 2, T)]
-        for t in range(NT):
-            for r in range(TOP):
-                for i, tokens in enumerate(token_halves):
-                    picked = y[t][:].indirect(token_slots[r][:, tokens.start // LIST : tokens.stop // LIST])
-                    if r == 0:
-                        nc.vector.tensor_copy(running[t][:, 0, tokens], picked)
-                    else:
-                        nc.vector.tensor_tensor(running[t][:, r, tokens], picked, running[t][:, r - 1, tokens], ADD)
-                    if r == TOP - 1:
-                        queue = nc.sync if i == 0 else nc.scalar
-                        queue.dma_start(out=out[t * P : (t + 1) * P, tokens], in_=running[t][:, r, tokens])
+        first, second, whole = slice(0, T // 2), slice(T // 2, T), slice(0, T)
+        partial = {(t, r): running[t][:, r, :] for t in range(NT) for r in range(TOP)}
+        third = sums.tile([P, T], F32, name="third", offset=0)
+        partial[0, 2] = third[:]
+
+        def combine(t, r, tokens, queue=nc.sync):
+            picked = y[t][:].indirect(token_slots[r][:, tokens.start // LIST : tokens.stop // LIST])
+            if r == 0:
+                nc.vector.tensor_copy(partial[t, 0][:, tokens], picked)
+            else:
+                nc.vector.tensor_tensor(partial[t, r][:, tokens], picked, partial[t, r - 1][:, tokens], ADD)
+            if r == TOP - 1:
+                queue.dma_start(out=out[t * P : (t + 1) * P, tokens], in_=partial[t, r][:, tokens])
+
+        for r in range(2):
+            combine(0, r, first)
+            combine(0, r, second)
+        for r in range(2):
+            combine(1, r, whole)
+            combine(0, r + 2, whole)
+        for r in range(2, TOP):
+            combine(1, r, first)
+            combine(1, r, second, nc.scalar)

@@ -40,7 +40,7 @@ ODD = STAGE_BYTES + PACK * 4 * WINDOW
 LIST = 16
 HELD = 4
 STAGE = 4 * PACK * SH
-CUT = 5 * C // 2
+CUT = 2 * C
 
 
 def tile_moe_pre_lin_bias_kernel(tc, xT, w, b, gate, offs, pos1, pos2, pos3, pos4, out):
@@ -70,17 +70,17 @@ def tile_moe_pre_lin_bias_kernel(tc, xT, w, b, gate, offs, pos1, pos2, pos3, pos
         w_now, w_held = {}, {}
         x_wide = {}
 
-        def load_x(g, j):
+        def load_x(g, j, queue=nc.sync):
             if g < WIDE_PASSES:
                 windows[g, j] = tokens_pool.tile([P, WIDE_WINDOW], F32, name="wide%d_%d" % (g, j), offset=(g * PACK + j) * BIG, align_bytes=64)
             elif g == WIDE_PASSES:
                 windows[g, j] = stage.tile([P, WINDOW], F32, name="window2_%d" % j, offset=STAGE + j * 4 * WINDOW, align_bytes=64)
             else:
                 windows[g, j] = tokens_pool.tile([P, WINDOW], F32, name="window3_%d" % j, offset=j * 4 * WINDOW, align_bytes=64)
-            nc.sync.dma_start(out=windows[g, j][:, 0:T], in_=x_rows[g, j])
+            queue.dma_start(out=windows[g, j][:, 0:T], in_=x_rows[g, j])
 
-        def load_gate(lo, hi, queue):
-            queue.dma_start(out=gates[:, lo:hi], in_=gate[0:P, lo:hi])
+        def load_gate(lo, hi):
+            nc.sync.dma_start(out=gates[:, lo:hi], in_=gate[0:P, lo:hi])
 
         def load_w(s, pair):
             h, g = divmod(s, PASSES)
@@ -134,11 +134,11 @@ def tile_moe_pre_lin_bias_kernel(tc, xT, w, b, gate, offs, pos1, pos2, pos3, pos
 
         def gather_x(s, j, lo, hi, into=None):
             h, g = divmod(s, PASSES)
-            if j == 0 and lo == 0:
-                x_f32[s] = stage.tile([P, PACK, CUT if s == STEPS - 1 else SH], F32, name="x_f32_%d" % (s % 2), offset=(s % 2) * ODD, align_bytes=64)
+            if s not in x_f32:
+                x_f32[s] = stage.tile([P, PACK, SH], F32, name="x_f32_%d" % (s % 2), offset=(s % 2) * ODD, align_bytes=64)
             a, z = h * SH + lo, h * SH + hi
             nc.vector.tensor_tensor(
-                x_f32[s][:, j, lo:hi] if into is None else into[:, j, :],
+                x_f32[s][:, j, lo:hi] if into is None else into,
                 windows[g, j][:].indirect(slot_tokens[:, a // LIST : z // LIST]),
                 gates[:, a:z],
                 MULT,
@@ -214,10 +214,10 @@ def tile_moe_pre_lin_bias_kernel(tc, xT, w, b, gate, offs, pos1, pos2, pos3, pos
             round_w(s, 0)
             round_w(s, 1)
 
-        gate_cuts = (0, C, SH, S)
-        load_x(0, 0)
+        gate_cuts = (0, 256, 832, S)
+        load_x(0, 0, nc.scalar)
         for lo, hi in zip(gate_cuts, gate_cuts[1:]):
-            load_gate(lo, hi, nc.scalar if lo == 0 else nc.sync)
+            load_gate(lo, hi)
         load_x(0, 1)
         load_w(0, 0)
         load_x(0, 2)
@@ -284,14 +284,19 @@ def tile_moe_pre_lin_bias_kernel(tc, xT, w, b, gate, offs, pos1, pos2, pos3, pos
         finish(5)
 
         h = HALVES - 1
-        cut = CUT
+        flat = stage.tile([P, CUT + 6 * SH], F32, name="x_last", offset=ODD, align_bytes=64)
+        x_f32[last] = flat[:, 0 : PACK * SH].rearrange("p (j c) -> p j c", j=PACK)
+        rest = flat[:, CUT:].rearrange("p (a b c) -> p a b c", a=2, b=3)
         for j in range(PACK):
-            gather_x(last, j, 0, cut)
-        round_x(last, 0, cut)
-        x_end = stage.tile([P, PACK, SH - cut], F32, name="x_end", offset=ODD + 4 * PACK * cut, align_bytes=64)
-        for j in range(PACK):
-            gather_x(last, j, cut, SH, x_end)
-        interleave(x_bf[last][:, PACK * cut :], x_end[:])
+            gather_x(last, j, 0, SH if j < 2 else CUT)
+        round_x(last, 0, CUT)
+        for b2 in range(2):
+            gather_x(last, 2 + b2, CUT, SH, rest[:, 1, b2, 0 : SH - CUT])
+        for lo in range(CUT, SH, C):
+            nc.scalar.copy(
+                out=x_bf[last][:, PACK * lo : PACK * (lo + C)].rearrange("p (c i a b) -> p c a b i", i=4, a=2, b=2),
+                in_=rest[:, :, 0:2, lo - CUT : lo - CUT + C].rearrange("p a b (c i) -> p c a b i", i=4),
+            )
         finish(last - 1)
         quantise_w(last)
         for lo, hi in ((0, 2), (2, 3), (3, 4)):
@@ -302,15 +307,16 @@ def tile_moe_pre_lin_bias_kernel(tc, xT, w, b, gate, offs, pos1, pos2, pos3, pos
         codes_end = stage.tile([P, EH, PASSES * P], U32, name="codes_end", offset=ODD + STAGE - 4 * HELD * EH * P, align_bytes=64)
         scales_end = keep.tile([P, EH, PASSES * P], U8, name="scales_end", align_bytes=64)
         for q in range(EH):
+            codes = codes_end[:, q, :]
             for s in range(PASSES, STEPS, 2):
                 cols = slice((s - PASSES) * P, (s - PASSES + 2) * P)
                 nc.vector.quantize_mx(
-                    out=codes_end[:, q, cols].bitcast(FP8X4),
+                    out=codes[:, cols].bitcast(FP8X4),
                     scales=scales_end[:, q, cols],
                     in_=w_held[s][:, q * 2 * P * PACK : (q + 1) * 2 * P * PACK],
                 )
                 for u in (s, s + 1):
-                    w_codes[u, q, 1] = codes_end[:, q, (u - PASSES) * P : (u - PASSES + 1) * P]
+                    w_codes[u, q, 1] = codes[:, (u - PASSES) * P : (u - PASSES + 1) * P]
                     w_scales[u, q, 1] = scales_end[:, q, (u - PASSES) * P : (u - PASSES + 1) * P]
                     multiply(u, q, 1)
             add_bias(h, q, 1)
@@ -336,6 +342,8 @@ def tile_moe_pre_lin_bias_kernel(tc, xT, w, b, gate, offs, pos1, pos2, pos3, pos
         for r in range(2):
             combine(1, r, whole)
             combine(0, r + 2, whole)
-        for r in range(2, TOP):
-            combine(1, r, first)
-            combine(1, r, second, nc.scalar)
+        combine(1, 2, first)
+        combine(1, 2, second)
+        combine(1, 3, first)
+        combine(1, 3, slice(T // 2, 3 * T // 4), nc.scalar)
+        combine(1, 3, slice(3 * T // 4, T))

@@ -22,25 +22,25 @@ IDENT = mybir.ActivationFunctionType.Identity
 P = 128
 PACK = 4
 PASSES = K // (P * PACK)
-HALVES = 2
-EH = E // HALVES
-SH = S // HALVES
-STEPS = HALVES * PASSES
+LAST = PASSES - 1
 NT = N // P
-WINDOW = SH + 16
-STAGE_BYTES = 4 * PACK * SH
-WIDE_PASSES = 2
-WIDE_WINDOW = 2 * WINDOW
-RING = 3
-SWAP = 2 * PACK * SH
-X_PLACE = {0: 5, 4: 4, 1: 1, 5: 0, 2: 4, 3: 5, 6: 0, 7: 1}
-W_PLACE = (0, 2, 4, 0, 2, 0, 2, 2)
-BIG = 4 * WIDE_WINDOW
-ODD = STAGE_BYTES + PACK * 4 * WINDOW
+PAIRS = E // 2
+SH = S // 2
 LIST = 16
-HELD = 4
-STAGE = 4 * PACK * SH
-CUT = 2 * C
+WINDOW = S + LIST
+SLOTS = 7
+UNITS = 6
+KB = 1024
+
+SLOT = 4 * WINDOW
+AT_WINDOWS = 0
+AT_STAGE = SLOTS * SLOT
+AT_UNITS = AT_STAGE + 64 * KB
+AT_W = AT_UNITS + UNITS * 8 * KB
+AT_HELD = AT_W + 16 * KB
+AT_WCODES = AT_HELD + 16 * KB
+AT_XCODES = AT_WCODES + 20 * KB
+AT_BIAS = AT_XCODES + 10 * KB
 
 
 def tile_moe_pre_lin_bias_kernel(tc, xT, w, b, gate, offs, pos1, pos2, pos3, pos4, out):
@@ -50,281 +50,224 @@ def tile_moe_pre_lin_bias_kernel(tc, xT, w, b, gate, offs, pos1, pos2, pos3, pos
 
     with ExitStack() as ctx:
         keep = ctx.enter_context(tc.tile_pool(name="keep", bufs=1))
-        stage = ctx.enter_context(tc.tile_pool(name="stage", bufs=1))
-        tokens_pool = ctx.enter_context(tc.tile_pool(name="tokens", bufs=1))
-        swap = ctx.enter_context(tc.tile_pool(name="swap", bufs=1))
-        codes_pool = ctx.enter_context(tc.tile_pool(name="codes", bufs=1))
-        sums = ctx.enter_context(tc.tile_pool(name="sums", bufs=1))
+        arena = ctx.enter_context(tc.tile_pool(name="arena", bufs=1))
         psum = ctx.enter_context(tc.psum_pool(name="psum", bufs=1))
+
+        def placed(name, shape, dtype, at):
+            return arena.tile([P] + shape, dtype, name=name, offset=at, align_bytes=64)
 
         slot_tokens = keep.tile([P, S // LIST], U16, name="slot_tokens")
         token_slots = [keep.tile([P, T // LIST], U16, name="token_slots%d" % r) for r in range(TOP)]
         gates = keep.tile([P, S], F32, name="gates")
-        bias = sums.tile([P, NT, E], F32, name="bias", offset=0)
-        windows = {}
-        y = [tokens_pool.tile([P, S], F32, name="y%d" % t, offset=(4 + t) * BIG, align_bytes=64) for t in range(NT)]
+        bias = placed("bias", [NT, E], F32, AT_BIAS)
+        banks = {(t, i): psum.tile([P, 2 * C], F32, name="bank%d_%d" % (t, i)) for t in range(NT) for i in range(PAIRS)}
+        added = {key: 0 for key in banks}
 
-        w_raw, w_bf, w_codes, w_scales = {}, {}, {}, {}
-        x_f32, x_bf, x_codes, x_scales = {}, {}, {}, {}
-        banks = {}
-        w_now, w_held = {}, {}
-        x_wide = {}
+        windows, w_raw, w_bf, w_mx, x_mx = {}, {}, {}, {}, {}
+
+        def window_at(g, j):
+            return AT_WINDOWS + (g * PACK + j) % SLOTS * SLOT
+
+        def unit_at(g, i):
+            return AT_UNITS + (g * PAIRS + i) % UNITS * 8 * KB
 
         def load_x(g, j, queue=nc.sync):
-            if g < WIDE_PASSES:
-                windows[g, j] = tokens_pool.tile([P, WIDE_WINDOW], F32, name="wide%d_%d" % (g, j), offset=(g * PACK + j) * BIG, align_bytes=64)
-            elif g == WIDE_PASSES:
-                windows[g, j] = stage.tile([P, WINDOW], F32, name="window2_%d" % j, offset=STAGE + j * 4 * WINDOW, align_bytes=64)
-            else:
-                windows[g, j] = tokens_pool.tile([P, WINDOW], F32, name="window3_%d" % j, offset=j * 4 * WINDOW, align_bytes=64)
+            windows[g, j] = placed("window%d_%d" % (g, j), [WINDOW], F32, window_at(g, j))
             queue.dma_start(out=windows[g, j][:, 0:T], in_=x_rows[g, j])
 
-        def load_gate(lo, hi):
-            nc.sync.dma_start(out=gates[:, lo:hi], in_=gate[0:P, lo:hi])
+        def load_w(g, i):
+            w_raw[g, i] = placed("w_raw%d_%d" % (g, i), [2, PACK * N], F32, unit_at(g, i))
+            nc.sync.dma_start(out=w_raw[g, i][:], in_=w_rows[g, :, 2 * i : 2 * i + 2, :])
 
-        def load_w(s, pair):
-            h, g = divmod(s, PASSES)
-            e0 = h * EH + 2 * pair
-            place = W_PLACE[s] + pair
-            w_raw[s, pair] = swap.tile([P, 2, PACK * N], F32, name="w_raw%d" % place, offset=place * SWAP, align_bytes=64)
-            nc.sync.dma_start(out=w_raw[s, pair][:], in_=w_rows[g, :, e0 : e0 + 2, :])
+        def rounded_w(g, i, t):
+            if g < 2:
+                key, at, width, first = (g, t), AT_W + (g * NT + t) * 8 * KB, 8, 2 * i
+            elif t == 0:
+                key, at, width, first = ("late", i // 2), AT_W + (i // 2) * 8 * KB, 8, 4 * (i % 2) + 2 * (g - 2)
+            else:
+                key, at, width, first = ("held", i), AT_HELD + i * 4 * KB, 4, 2 * (g - 2)
+            if key not in w_bf:
+                w_bf[key] = placed("w_bf_%s_%d" % key, [width * P * PACK], BF16, at)
+            return w_bf[key][:, first * P * PACK : (first + 2) * P * PACK]
 
-        def interleave(dst, src):
+        def round_w(g, i):
+            rows = w_raw[g, i][:].rearrange("p q (j t c i) -> p t q c j i", j=PACK, t=NT, i=4)
+            for t in range(NT):
+                nc.scalar.copy(out=rounded_w(g, i, t).rearrange("p (q c i j) -> p q c j i", q=2, i=4, j=PACK), in_=rows[:, t])
+
+        def quantise(name, values, words, at):
+            codes = placed("codes_" + name, [words], U32, at)
+            scales = placed("scales_" + name, [words], U8, at + 4 * words)
+            nc.vector.quantize_mx(out=codes[:].bitcast(FP8X4), scales=scales[:], in_=values)
+            return codes, scales
+
+        def quantise_w(key, members, at):
+            codes, scales = quantise("w_%s_%d" % key, w_bf[key][:], len(members) * P, at)
+            for n, member in enumerate(members):
+                w_mx[member] = (codes[:, n * P : (n + 1) * P], scales[:, n * P : (n + 1) * P])
+
+        def quantise_x(g, lo, hi, values, at):
+            codes, scales = quantise("x%d_%d" % (g, lo), values, hi - lo, at)
+            for e in range(lo // C, hi // C):
+                cols = slice(e * C - lo, (e + 1) * C - lo)
+                x_mx[g, e] = (codes[:, cols], scales[:, cols])
+
+        def gather(g, j, lo, hi, into):
+            nc.vector.tensor_tensor(into, windows[g, j][:].indirect(slot_tokens[:, lo // LIST : hi // LIST]), gates[:, lo:hi], MULT)
+
+        def round_x(dst, src):
             nc.scalar.copy(
                 out=dst.rearrange("p (c i t) -> p c t i", i=4, t=PACK),
                 in_=src.rearrange("p t (c i) -> p c t i", i=4),
             )
 
-        def rounded_tile(slot):
-            if slot < 2:
-                return keep.tile([P, EH * N * PACK], BF16, name="w_bf%d" % slot, align_bytes=64)
-            return tokens_pool.tile([P, EH * N * PACK], BF16, name="w_bf%d" % slot, offset=slot * BIG, align_bytes=64)
+        def multiply(g, e, t):
+            key = (t, e // 2)
+            nc.tensor.matmul_mx(
+                out=banks[key][:, (e % 2) * C : (e % 2 + 1) * C],
+                lhsT=w_mx[g, e, t][0].bitcast(FP8X4),
+                lhsT_scale=w_mx[g, e, t][1],
+                rhs=x_mx[g, e][0].bitcast(FP8X4),
+                rhs_scale=x_mx[g, e][1],
+                start=(added[key] == 0),
+                stop=(added[key] == 2 * PASSES - 1),
+            )
+            added[key] = added[key] + 1
 
-        def round_w(s, pair):
-            if pair == 0 and s < PASSES:
-                both = rounded_tile(s)
-                w_now[s] = both[:]
-                for t in range(NT):
-                    w_bf[s, t] = both[:].rearrange("p (t e x) -> p t e x", t=NT, e=EH)[:, t]
-            elif pair == 0 and s % 2 == 0:
-                now = rounded_tile(0 if s == PASSES else 3)
-                w_held[s] = rounded_tile(1 if s == PASSES else 2)
-                for u in range(2):
-                    w_now[s + u] = now[:, u * EH * P * PACK : (u + 1) * EH * P * PACK]
-                    w_bf[s + u, 0] = now[:].rearrange("p (u e x) -> p u e x", u=2, e=EH)[:, u]
-                    w_bf[s + u, 1] = w_held[s][:].rearrange("p (e u x) -> p u e x", u=2, e=EH)[:, u]
-            rows = w_raw[s, pair][:].rearrange("p q (j t c i) -> p t q c j i", j=PACK, t=NT, i=4)
-            for t in range(NT):
-                nc.scalar.copy(
-                    out=w_bf[s, t][:, 2 * pair : 2 * pair + 2, :].rearrange("p q (c i j) -> p q c j i", i=4, j=PACK),
-                    in_=rows[:, t],
+        def add_bias(t, i):
+            for e in (2 * i, 2 * i + 1):
+                nc.scalar.activation(
+                    out=y[t][:, e * C : (e + 1) * C],
+                    in_=banks[t, i][:, (e % 2) * C : (e % 2 + 1) * C],
+                    func=IDENT,
+                    bias=bias[:, t, e : e + 1],
                 )
 
-        def quantise_w(s):
-            tiles = NT if s < PASSES else 1
-            place = s * EH * N if s < PASSES else (s - PASSES) * EH * P
-            codes = codes_pool.tile([P, tiles * EH * P], U32, name="w_codes%d" % s, offset=4 * place, align_bytes=64)
-            scales = keep.tile([P, tiles * EH * P], U8, name="w_scales%d" % (0, 1, 2, 3, 0, 4, 1, 2)[s], align_bytes=64)
-            nc.vector.quantize_mx(out=codes[:].bitcast(FP8X4), scales=scales[:], in_=w_now[s])
-            for t in range(tiles):
-                for q in range(EH):
-                    cols = slice((t * EH + q) * P, (t * EH + q + 1) * P)
-                    w_codes[s, q, t] = codes[:, cols]
-                    w_scales[s, q, t] = scales[:, cols]
+        stage = [placed("stage%d" % g, [PACK, S], F32, AT_STAGE + (g % 2) * 32 * KB) for g in range(LAST)]
+        x_bf = {}
 
-        def gather_x(s, j, lo, hi, into=None):
-            h, g = divmod(s, PASSES)
-            if s not in x_f32:
-                x_f32[s] = stage.tile([P, PACK, SH], F32, name="x_f32_%d" % (s % 2), offset=(s % 2) * ODD, align_bytes=64)
-            a, z = h * SH + lo, h * SH + hi
-            nc.vector.tensor_tensor(
-                x_f32[s][:, j, lo:hi] if into is None else into,
-                windows[g, j][:].indirect(slot_tokens[:, a // LIST : z // LIST]),
-                gates[:, a:z],
-                MULT,
-            )
+        def round_half(g, h):
+            x_bf[g, h] = placed("x_bf%d_%d" % (g, h), [SH * PACK], BF16, unit_at(g + 1, PAIRS - 1 - h))
+            round_x(x_bf[g, h][:], stage[g][:, :, h * SH : (h + 1) * SH])
 
-        def gather_wide(g, j, a, z):
-            if j == 0 and a == 0:
-                wide = stage.tile([P, PACK, S], F32, name="x_wide%d" % g, offset=g * ODD, align_bytes=64)
-                x_wide[g] = wide
-                for half in range(HALVES):
-                    x_f32[half * PASSES + g] = wide[:, :, half * SH : (half + 1) * SH]
-            nc.vector.tensor_tensor(x_wide[g][:, j, a:z], windows[g, j][:].indirect(slot_tokens[:, a // LIST : z // LIST]), gates[:, a:z], MULT)
-
-        def round_x(s, lo, hi):
-            if lo == 0:
-                place = X_PLACE[s]
-                x_bf[s] = swap.tile([P, SH * PACK], BF16, name="x_bf%d" % place, offset=place * SWAP, align_bytes=64)
-            interleave(x_bf[s][:, PACK * lo : PACK * hi], x_f32[s][:, :, lo:hi])
-
-        def quantise_x(s, lo, hi):
-            if s == PASSES + 1 or s == STEPS - 1:
-                at = 6 * BIG if s == PASSES + 1 else (7 * BIG + 5 * lo)
-                codes = tokens_pool.tile([P, hi - lo], U32, name="x_codes%d_%d" % (s, lo), offset=at, align_bytes=64)
-                scales = tokens_pool.tile([P, hi - lo], U8, name="x_scales%d_%d" % (s, lo), offset=at + 4 * (hi - lo), align_bytes=64)
-            else:
-                tag = "kept" if s == PASSES else "ring"
-                codes = keep.tile([P, hi - lo], U32, name="x_codes_" + tag, align_bytes=64)
-                scales = keep.tile([P, hi - lo], U8, name="x_scales_" + tag, align_bytes=64)
-            nc.vector.quantize_mx(out=codes[:].bitcast(FP8X4), scales=scales[:], in_=x_bf[s][:, PACK * lo : PACK * hi])
-            for q in range(lo // C, hi // C):
-                x_codes[s, q] = codes[:, q * C - lo : (q + 1) * C - lo]
-                x_scales[s, q] = scales[:, q * C - lo : (q + 1) * C - lo]
-
-        def multiply(s, q, t):
-            g = s % PASSES
-            closing = s - g + PASSES - 1
-            if g == 0:
-                banks[q, t] = psum.tile([P, C], F32, name="bank%d_%d" % (q, t))
-            nc.tensor.matmul_mx(
-                out=banks[q, t][:],
-                lhsT=w_codes[s, q, t].bitcast(FP8X4),
-                lhsT_scale=w_scales[s, q, t],
-                rhs=x_codes[s, q].bitcast(FP8X4),
-                rhs_scale=x_scales[s, q],
-                start=(g == 0),
-                stop=(s == closing),
-            )
-
-        def add_bias(h, q, t):
-            e = h * EH + q
-            nc.scalar.activation(out=y[t][:, e * C : (e + 1) * C], in_=banks[q, t][:], func=IDENT, bias=bias[:, t, e : e + 1])
-
-        def finish(s):
-            tiles = NT if s < STEPS - HELD else 1
-            if (s, 0, 0) not in w_codes:
-                quantise_w(s)
-            if (s, 0) not in x_codes:
-                quantise_x(s, 0, SH)
-            for t in range(tiles):
-                for q in range(EH):
-                    multiply(s, q, t)
-            if s % PASSES == PASSES - 1:
-                for t in range(NT):
-                    for q in range(EH):
-                        add_bias(s // PASSES, q, t)
-
-        nc.sync.dma_start(slot_tokens[:], offs)
-        def fetch_w(s):
-            load_w(s, 0)
-            load_w(s, 1)
-
-        def round_both(s):
-            round_w(s, 0)
-            round_w(s, 1)
+        def finish_early(g):
+            for h in range(2):
+                quantise_x(g, h * SH, (h + 1) * SH, x_bf[g, h][:], AT_XCODES + h * 5 * KB)
+                for e in range(h * PAIRS, (h + 1) * PAIRS):
+                    for t in range(NT):
+                        multiply(g, e, t)
 
         gate_cuts = (0, 256, 832, S)
+        nc.sync.dma_start(slot_tokens[:], offs)
         load_x(0, 0, nc.scalar)
         for lo, hi in zip(gate_cuts, gate_cuts[1:]):
-            load_gate(lo, hi)
-        load_x(0, 1)
-        load_w(0, 0)
-        load_x(0, 2)
-        load_w(0, 1)
-        load_x(0, 3)
-        fetch_w(1)
-        load_w(2, 0)
-        load_x(1, 0)
-        load_w(2, 1)
-        load_x(1, 1)
-        round_both(0)
-        round_both(1)
-        for lo, hi in zip(gate_cuts, gate_cuts[1:]):
-            gather_wide(0, 0, lo, hi)
+            nc.sync.dma_start(out=gates[:, lo:hi], in_=gate[0:P, lo:hi])
         for j in range(1, PACK):
-            gather_wide(0, j, 0, S)
-        round_both(2)
-        load_x(1, 2)
-        load_x(1, 3)
-        fetch_w(3)
-        fetch_w(4)
-        round_x(0, 0, SH)
-        round_x(PASSES, 0, SH)
-        round_both(3)
-        fetch_w(5)
-        for g in range(WIDE_PASSES, PASSES):
-            for j in range(PACK):
-                load_x(g, j)
+            load_x(0, j)
+            load_w(0, j - 1)
+        load_w(0, PAIRS - 1)
+        for i in range(PAIRS):
+            round_w(0, i)
+            load_x(1, i)
+            load_w(1, i)
         nc.sync.dma_start(out=bias[:], in_=b.rearrange("(t p) e -> p t e", p=P))
         for r, pos in enumerate((pos1, pos2, pos3, pos4)):
             nc.sync.dma_start(token_slots[r][:], pos)
-        quantise_w(0)
-        quantise_w(1)
-        gather_wide(1, 0, 0, S)
-        gather_wide(1, 1, 0, S)
-        finish(0)
-        gather_wide(1, 2, 0, S)
-        quantise_x(PASSES, 0, SH)
-        round_both(4)
-        fetch_w(6)
-        round_both(5)
-        gather_wide(1, 3, 0, S)
-        round_x(1, 0, SH)
-        round_x(PASSES + 1, 0, SH)
 
-        last = STEPS - 1
+        for lo, hi in zip(gate_cuts, gate_cuts[1:]):
+            gather(0, 0, lo, hi, stage[0][:, 0, lo:hi])
+        for j in range(1, PACK):
+            gather(0, j, 0, S, stage[0][:, j, :])
+            if j == 2:
+                for t in range(NT):
+                    quantise_w((0, t), [(0, e, t) for e in range(E)], AT_WCODES + t * 5 * KB)
+        for i in range(PAIRS):
+            round_w(1, i)
+            load_w(2, i)
         for j in range(PACK):
-            gather_x(2, j, 0, SH)
-        finish(1)
-        quantise_x(PASSES + 1, 0, SH)
-        round_x(2, 0, SH)
-        round_both(6)
-        fetch_w(7)
-        for j in range(PACK):
-            gather_x(3, j, 0, SH)
-        round_x(3, 0, SH)
-        finish(2)
-        round_both(7)
-        for j in range(PACK):
-            gather_x(6, j, 0, SH)
-        round_x(6, 0, SH)
-        finish(3)
-        finish(4)
-        finish(5)
+            load_x(2, j)
+        for h in range(2):
+            round_half(0, h)
 
-        h = HALVES - 1
-        flat = stage.tile([P, CUT + 6 * SH], F32, name="x_last", offset=ODD, align_bytes=64)
-        x_f32[last] = flat[:, 0 : PACK * SH].rearrange("p (j c) -> p j c", j=PACK)
-        rest = flat[:, CUT:].rearrange("p (a b c) -> p a b c", a=2, b=3)
+        for j in range(2):
+            gather(1, j, 0, S, stage[1][:, j, :])
+        for t in range(NT):
+            quantise_w((1, t), [(1, e, t) for e in range(E)], AT_WCODES + (NT + t) * 5 * KB)
+        finish_early(0)
+        for j in range(2, PACK):
+            gather(1, j, 0, S, stage[1][:, j, :])
+        for i in range(PAIRS):
+            round_w(2, i)
+            load_w(LAST, i)
         for j in range(PACK):
-            gather_x(last, j, 0, SH if j < 2 else CUT)
-        round_x(last, 0, CUT)
-        for b2 in range(2):
-            gather_x(last, 2 + b2, CUT, SH, rest[:, 1, b2, 0 : SH - CUT])
-        for lo in range(CUT, SH, C):
-            nc.scalar.copy(
-                out=x_bf[last][:, PACK * lo : PACK * (lo + C)].rearrange("p (c i a b) -> p c a b i", i=4, a=2, b=2),
-                in_=rest[:, :, 0:2, lo - CUT : lo - CUT + C].rearrange("p a b (c i) -> p c a b i", i=4),
-            )
-        finish(last - 1)
-        quantise_w(last)
-        for lo, hi in ((0, 2), (2, 3), (3, 4)):
-            quantise_x(last, lo * C, hi * C)
-            for q in range(lo, hi):
-                multiply(last, q, 0)
-                add_bias(h, q, 0)
-        codes_end = stage.tile([P, EH, PASSES * P], U32, name="codes_end", offset=ODD + STAGE - 4 * HELD * EH * P, align_bytes=64)
-        scales_end = keep.tile([P, EH, PASSES * P], U8, name="scales_end", align_bytes=64)
-        for q in range(EH):
-            codes = codes_end[:, q, :]
-            for s in range(PASSES, STEPS, 2):
-                cols = slice((s - PASSES) * P, (s - PASSES + 2) * P)
-                nc.vector.quantize_mx(
-                    out=codes[:, cols].bitcast(FP8X4),
-                    scales=scales_end[:, q, cols],
-                    in_=w_held[s][:, q * 2 * P * PACK : (q + 1) * 2 * P * PACK],
-                )
-                for u in (s, s + 1):
-                    w_codes[u, q, 1] = codes[:, (u - PASSES) * P : (u - PASSES + 1) * P]
-                    w_scales[u, q, 1] = scales_end[:, q, (u - PASSES) * P : (u - PASSES + 1) * P]
-                    multiply(u, q, 1)
-            add_bias(h, q, 1)
+            load_x(LAST, j)
+        for h in range(2):
+            round_half(1, h)
 
-        running = [stage.tile([P, TOP, T], F32, name="running%d" % t, offset=ODD + STAGE + t * 4 * TOP * T, align_bytes=64) for t in range(NT)]
+        for j in range(2):
+            gather(2, j, 0, S, stage[2][:, j, :])
+        finish_early(1)
+        for j in range(2, PACK):
+            gather(2, j, 0, S, stage[2][:, j, :])
+        for i in range(PAIRS):
+            round_w(LAST, i)
+        for h in range(2):
+            round_half(2, h)
+
+        y = [placed("y%d" % t, [S], F32, window_at(2, t + 1)) for t in range(NT)]
+        flat = placed("last_stage", [8 * SH], F32, AT_STAGE + 32 * KB)
+        for j in range(2):
+            gather(LAST, j, 0, S, flat[:, j * S : (j + 1) * S])
+        for h in range(2):
+            for j in range(2, PACK):
+                gather(LAST, j, h * SH, (h + 1) * SH, flat[:, (2 * j + h) * SH : (2 * j + h + 1) * SH])
+        planes = flat[:].rearrange("p (j s) -> p j s", j=PACK)
+        last_bf = [placed("last_bf%d" % h, [SH * PACK], BF16, unit_at(LAST, h)) for h in range(2)]
+        round_x(last_bf[0][:], planes[:, :, 0:SH])
+        for n in range(2):
+            round_x(last_bf[1][:, n * 2 * PACK * C : (n + 1) * 2 * PACK * C], planes[:, :, SH + n * 2 * C : SH + (n + 1) * 2 * C])
+
+        def quantise_late(h, at):
+            quantise_w(("late", h), [(g, 4 * h + 2 * i + q, 0) for i in range(2) for g in (2, LAST) for q in range(2)], at)
+
+        def quantise_held(i, at):
+            quantise_w(("held", i), [(g, 2 * i + q, 1) for g in (2, LAST) for q in range(2)], at)
+
+        def multiply_held(i):
+            for g in (2, LAST):
+                for e in (2 * i, 2 * i + 1):
+                    multiply(g, e, 1)
+            add_bias(1, i)
+
+        quantise_late(0, window_at(LAST, 1))
+        quantise_x(2, 0, SH, x_bf[2, 0][:], AT_XCODES)
+        for e in range(PAIRS):
+            multiply(2, e, 0)
+        quantise_x(2, SH, S, x_bf[2, 1][:], AT_XCODES + 5 * KB)
+        quantise_x(LAST, 0, SH, last_bf[0][:], AT_WCODES)
+        for e in range(PAIRS):
+            multiply(LAST, e, 0)
+        for i in range(2):
+            add_bias(0, i)
+        quantise_late(1, unit_at(LAST, 0))
+        for e in range(PAIRS, E):
+            multiply(2, e, 0)
+        quantise_held(0, unit_at(LAST, 0) + 5 * KB)
+        for n in range(2):
+            lo = SH + n * 2 * C
+            quantise_x(LAST, lo, lo + 2 * C, last_bf[1][:, n * 2 * PACK * C : (n + 1) * 2 * PACK * C], AT_WCODES + 5 * KB + n * 5 * KB // 2)
+            for e in range(lo // C, lo // C + 2):
+                multiply(LAST, e, 0)
+            add_bias(0, 2 + n)
+        multiply_held(0)
+        for i in range(1, PAIRS):
+            quantise_held(i, AT_STAGE + 32 * KB + i * 3 * KB)
+            multiply_held(i)
+
+        running = [placed("running%d" % t, [TOP, T], F32, AT_STAGE + t * 4 * TOP * T) for t in range(NT)]
         first, second, whole = slice(0, T // 2), slice(T // 2, T), slice(0, T)
         partial = {(t, r): running[t][:, r, :] for t in range(NT) for r in range(TOP)}
-        third = sums.tile([P, T], F32, name="third", offset=0)
+        third = placed("third", [T], F32, AT_BIAS + 64 - 4 * T)
         partial[0, 2] = third[:]
 
         def combine(t, r, tokens, queue=nc.sync):

@@ -222,7 +222,7 @@ def tile_moe_pre_lin_bias_kernel(tc, xT, w, b, gate, offs, pos1, pos2, pos3, pos
             for j in range(2, PACK):
                 gather(LAST, j, h * SH, (h + 1) * SH, flat[:, (2 * j + h) * SH : (2 * j + h + 1) * SH])
         planes = flat[:].rearrange("p (j s) -> p j s", j=PACK)
-        last_bf = [placed("last_bf%d" % h, [SH * PACK], BF16, unit_at(LAST, h)) for h in range(2)]
+        last_bf = [placed("last_bf%d" % h, [SH * PACK], BF16, unit_at(2, PAIRS - 1 - h)) for h in range(2)]
         round_x(last_bf[0][:], planes[:, :, 0:SH])
         for n in range(2):
             round_x(last_bf[1][:, n * 2 * PACK * C : (n + 1) * 2 * PACK * C], planes[:, :, SH + n * 2 * C : SH + (n + 1) * 2 * C])
@@ -243,24 +243,23 @@ def tile_moe_pre_lin_bias_kernel(tc, xT, w, b, gate, offs, pos1, pos2, pos3, pos
         quantise_x(2, 0, SH, x_bf[2, 0][:], AT_XCODES)
         for e in range(PAIRS):
             multiply(2, e, 0)
-        quantise_x(2, SH, S, x_bf[2, 1][:], AT_XCODES + 5 * KB)
         quantise_x(LAST, 0, SH, last_bf[0][:], AT_WCODES)
         for e in range(PAIRS):
             multiply(LAST, e, 0)
         for i in range(2):
             add_bias(0, i)
-        quantise_late(1, unit_at(LAST, 0))
-        for e in range(PAIRS, E):
-            multiply(2, e, 0)
-        quantise_held(0, unit_at(LAST, 0) + 5 * KB)
+        behind = unit_at(2, PAIRS - 1)
+        quantise_late(1, behind)
         for n in range(2):
             lo = SH + n * 2 * C
-            quantise_x(LAST, lo, lo + 2 * C, last_bf[1][:, n * 2 * PACK * C : (n + 1) * 2 * PACK * C], AT_WCODES + 5 * KB + n * 5 * KB // 2)
-            for e in range(lo // C, lo // C + 2):
-                multiply(LAST, e, 0)
+            cols = slice(n * 2 * PACK * C, (n + 1) * 2 * PACK * C)
+            quantise_x(2, lo, lo + 2 * C, x_bf[2, 1][:, cols], behind + 5 * KB + n * 5 * KB // 2)
+            quantise_x(LAST, lo, lo + 2 * C, last_bf[1][:, cols], AT_WCODES + 5 * KB + n * 5 * KB // 2)
+            for g in (2, LAST):
+                for e in range(lo // C, lo // C + 2):
+                    multiply(g, e, 0)
             add_bias(0, 2 + n)
-        multiply_held(0)
-        for i in range(1, PAIRS):
+        for i in range(PAIRS):
             quantise_held(i, AT_STAGE + 32 * KB + i * 3 * KB)
             multiply_held(i)
 

@@ -150,12 +150,11 @@ def tile_moe_pre_lin_bias_kernel(tc, xT, w, b, gate, offs, pos1, pos2, pos3, pos
             x_bf[g, h] = placed("x_bf%d_%d" % (g, h), [SH * PACK], BF16, unit_at(g + 1, PAIRS - 1 - h))
             round_x(x_bf[g, h][:], stage[g][:, :, h * SH : (h + 1) * SH])
 
-        def finish_early(g):
-            for h in range(2):
-                quantise_x(g, h * SH, (h + 1) * SH, x_bf[g, h][:], AT_XCODES + h * 5 * KB)
-                for e in range(h * PAIRS, (h + 1) * PAIRS):
-                    for t in range(NT):
-                        multiply(g, e, t)
+        def finish_half(g, h, at):
+            quantise_x(g, h * SH, (h + 1) * SH, x_bf[g, h][:], at)
+            for e in range(h * PAIRS, (h + 1) * PAIRS):
+                for t in range(NT):
+                    multiply(g, e, t)
 
         gate_cuts = (0, 256, 832, S)
         nc.sync.dma_start(slot_tokens[:], offs)
@@ -193,7 +192,8 @@ def tile_moe_pre_lin_bias_kernel(tc, xT, w, b, gate, offs, pos1, pos2, pos3, pos
             gather(1, j, 0, S, stage[1][:, j, :])
         for t in range(NT):
             quantise_w((1, t), [(1, e, t) for e in range(E)], AT_WCODES + (NT + t) * 5 * KB)
-        finish_early(0)
+        for h in range(2):
+            finish_half(0, h, AT_XCODES + h * 5 * KB)
         for j in range(2, PACK):
             gather(1, j, 0, S, stage[1][:, j, :])
         for i in range(PAIRS):
@@ -206,7 +206,7 @@ def tile_moe_pre_lin_bias_kernel(tc, xT, w, b, gate, offs, pos1, pos2, pos3, pos
 
         for j in range(2):
             gather(2, j, 0, S, stage[2][:, j, :])
-        finish_early(1)
+        finish_half(1, 0, AT_XCODES)
         for j in range(2, PACK):
             gather(2, j, 0, S, stage[2][:, j, :])
         for i in range(PAIRS):
@@ -222,7 +222,7 @@ def tile_moe_pre_lin_bias_kernel(tc, xT, w, b, gate, offs, pos1, pos2, pos3, pos
             for j in range(2, PACK):
                 gather(LAST, j, h * SH, (h + 1) * SH, flat[:, (2 * j + h) * SH : (2 * j + h + 1) * SH])
         planes = flat[:].rearrange("p (j s) -> p j s", j=PACK)
-        last_bf = [placed("last_bf%d" % h, [SH * PACK], BF16, unit_at(2, PAIRS - 1 - h)) for h in range(2)]
+        last_bf = [placed("last_bf%d" % h, [SH * PACK], BF16, (unit_at(2, PAIRS - 1), unit_at(LAST, 0))[h]) for h in range(2)]
         round_x(last_bf[0][:], planes[:, :, 0:SH])
         for n in range(2):
             round_x(last_bf[1][:, n * 2 * PACK * C : (n + 1) * 2 * PACK * C], planes[:, :, SH + n * 2 * C : SH + (n + 1) * 2 * C])
@@ -239,6 +239,7 @@ def tile_moe_pre_lin_bias_kernel(tc, xT, w, b, gate, offs, pos1, pos2, pos3, pos
                     multiply(g, e, 1)
             add_bias(1, i)
 
+        finish_half(1, 1, window_at(LAST, 0))
         quantise_late(0, window_at(LAST, 1))
         quantise_x(2, 0, SH, x_bf[2, 0][:], AT_XCODES)
         for e in range(PAIRS):

@@ -68,16 +68,29 @@ def tile_moe_pre_lin_bias_kernel(tc, xT, w, b, gate, offs, pos1, pos2, pos3, pos
         def window_at(g, j):
             return AT_WINDOWS + (g * PACK + j) % SLOTS * SLOT
 
-        def unit_at(g, i):
-            return AT_UNITS + (g * PAIRS + i) % UNITS * 8 * KB
+        def unit(n):
+            return AT_UNITS + n * 8 * KB
 
         def load_x(g, j, queue=nc.sync):
             windows[g, j] = placed("window%d_%d" % (g, j), [WINDOW], F32, window_at(g, j))
             queue.dma_start(out=windows[g, j][:, 0:T], in_=x_rows[g, j])
 
+        raw_at = {
+            0: (unit(0), unit(1), unit(2), unit(3)),
+            1: (AT_XCODES, AT_WCODES + 10 * KB, window_at(1, 2), unit(4)),
+            2: (unit(0), unit(1), unit(2), unit(2)),
+            3: (unit(4), unit(5), unit(0), unit(0)),
+        }
+        double = {}
+
         def load_w(g, i):
-            w_raw[g, i] = placed("w_raw%d_%d" % (g, i), [2, PACK * N], F32, unit_at(g, i))
-            nc.sync.dma_start(out=w_raw[g, i][:], in_=w_rows[g, :, 2 * i : 2 * i + 2, :])
+            if g > 0 and raw_at[g][i] == raw_at[g][PAIRS - 1]:
+                if g not in double:
+                    double[g] = placed("w_raw%d_end" % g, [2, 2, PACK * N], F32, raw_at[g][i])
+                w_raw[g, i] = double[g][:, i % 2]
+            else:
+                w_raw[g, i] = placed("w_raw%d_%d" % (g, i), [2, PACK * N], F32, raw_at[g][i])[:]
+            nc.sync.dma_start(out=w_raw[g, i], in_=w_rows[g, :, 2 * i : 2 * i + 2, :])
 
         def rounded_w(g, i, t):
             if g < 2:
@@ -91,7 +104,7 @@ def tile_moe_pre_lin_bias_kernel(tc, xT, w, b, gate, offs, pos1, pos2, pos3, pos
             return w_bf[key][:, first * P * PACK : (first + 2) * P * PACK]
 
         def round_w(g, i):
-            rows = w_raw[g, i][:].rearrange("p q (j t c i) -> p t q c j i", j=PACK, t=NT, i=4)
+            rows = w_raw[g, i].rearrange("p q (j t c i) -> p t q c j i", j=PACK, t=NT, i=4)
             for t in range(NT):
                 nc.scalar.copy(out=rounded_w(g, i, t).rearrange("p (q c i j) -> p q c j i", q=2, i=4, j=PACK), in_=rows[:, t])
 
@@ -147,7 +160,7 @@ def tile_moe_pre_lin_bias_kernel(tc, xT, w, b, gate, offs, pos1, pos2, pos3, pos
         x_bf = {}
 
         def round_half(g, h):
-            x_bf[g, h] = placed("x_bf%d_%d" % (g, h), [SH * PACK], BF16, unit_at(g + 1, PAIRS - 1 - h))
+            x_bf[g, h] = placed("x_bf%d_%d" % (g, h), [SH * PACK], BF16, raw_at[g + 1][PAIRS - 1] + h * 8 * KB)
             round_x(x_bf[g, h][:], stage[g][:, :, h * SH : (h + 1) * SH])
 
         def finish_half(g, h, at):
@@ -167,7 +180,8 @@ def tile_moe_pre_lin_bias_kernel(tc, xT, w, b, gate, offs, pos1, pos2, pos3, pos
         load_w(0, PAIRS - 1)
         for i in range(PAIRS):
             round_w(0, i)
-            load_x(1, i)
+            if i < 2:
+                load_x(1, i)
             load_w(1, i)
         nc.sync.dma_start(out=bias[:], in_=b.rearrange("(t p) e -> p t e", p=P))
         for r, pos in enumerate((pos1, pos2, pos3, pos4)):
@@ -182,7 +196,10 @@ def tile_moe_pre_lin_bias_kernel(tc, xT, w, b, gate, offs, pos1, pos2, pos3, pos
                     quantise_w((0, t), [(0, e, t) for e in range(E)], AT_WCODES + t * 5 * KB)
         for i in range(PAIRS):
             round_w(1, i)
+            if i == 2:
+                load_x(1, 2, nc.scalar)
             load_w(2, i)
+        load_x(1, 3)
         for j in range(PACK):
             load_x(2, j)
         for h in range(2):
@@ -222,7 +239,7 @@ def tile_moe_pre_lin_bias_kernel(tc, xT, w, b, gate, offs, pos1, pos2, pos3, pos
             for j in range(2, PACK):
                 gather(LAST, j, h * SH, (h + 1) * SH, flat[:, (2 * j + h) * SH : (2 * j + h + 1) * SH])
         planes = flat[:].rearrange("p (j s) -> p j s", j=PACK)
-        last_bf = [placed("last_bf%d" % h, [SH * PACK], BF16, (unit_at(2, PAIRS - 1), unit_at(LAST, 0))[h]) for h in range(2)]
+        last_bf = [placed("last_bf%d" % h, [SH * PACK], BF16, unit(UNITS - 1 - h)) for h in range(2)]
         round_x(last_bf[0][:], planes[:, :, 0:SH])
         for n in range(2):
             round_x(last_bf[1][:, n * 2 * PACK * C : (n + 1) * 2 * PACK * C], planes[:, :, SH + n * 2 * C : SH + (n + 1) * 2 * C])
@@ -249,7 +266,7 @@ def tile_moe_pre_lin_bias_kernel(tc, xT, w, b, gate, offs, pos1, pos2, pos3, pos
             multiply(LAST, e, 0)
         for i in range(2):
             add_bias(0, i)
-        behind = unit_at(2, PAIRS - 1)
+        behind = unit(UNITS - 1)
         quantise_late(1, behind)
         for n in range(2):
             lo = SH + n * 2 * C

@@ -34,7 +34,7 @@ KB = 1024
 
 SLOT = 4 * WINDOW
 AT_WINDOWS = 0
-AT_STAGE = SLOTS * SLOT
+AT_STAGE = -(-SLOTS * SLOT // 256) * 256
 AT_UNITS = AT_STAGE + 64 * KB
 AT_W = AT_UNITS + UNITS * 8 * KB
 AT_HELD = AT_W + 16 * KB
@@ -72,19 +72,22 @@ def tile_moe_pre_lin_bias_kernel(tc, xT, w, b, gate, offs, pos1, pos2, pos3, pos
             return AT_UNITS + n * 8 * KB
 
         def load_x(g, j, queue=nc.sync):
-            windows[g, j] = placed("window%d_%d" % (g, j), [WINDOW], F32, window_at(g, j))
+            if (g, j) == (LAST, PACK - 1):
+                windows[g, j] = placed("window_end", [SH + LIST], F32, raw_at[LAST][0])
+            else:
+                windows[g, j] = placed("window%d_%d" % (g, j), [WINDOW], F32, window_at(g, j))
             queue.dma_start(out=windows[g, j][:, 0:T], in_=x_rows[g, j])
 
         raw_at = {
             0: (unit(0), unit(1), unit(2), unit(3)),
-            1: (AT_XCODES, AT_WCODES + 10 * KB, window_at(1, 2), unit(4)),
+            1: (AT_XCODES, AT_WCODES + 10 * KB, unit(4), window_at(1, 2)),
             2: (unit(0), unit(1), unit(2), unit(2)),
             3: (unit(4), unit(5), unit(0), unit(0)),
         }
         double = {}
 
         def load_w(g, i):
-            if g > 0 and raw_at[g][i] == raw_at[g][PAIRS - 1]:
+            if g > 0 and raw_at[g][i] == raw_at[g][2]:
                 if g not in double:
                     double[g] = placed("w_raw%d_end" % g, [2, 2, PACK * N], F32, raw_at[g][i])
                 w_raw[g, i] = double[g][:, i % 2]
@@ -103,14 +106,14 @@ def tile_moe_pre_lin_bias_kernel(tc, xT, w, b, gate, offs, pos1, pos2, pos3, pos
                 w_bf[key] = placed("w_bf_%s_%d" % key, [width * P * PACK], BF16, at)
             return w_bf[key][:, first * P * PACK : (first + 2) * P * PACK]
 
-        def round_w(g, i):
+        def round_w(g, i, tiles=range(NT)):
             rows = w_raw[g, i].rearrange("p q (j t c i) -> p t q c j i", j=PACK, t=NT, i=4)
-            for t in range(NT):
+            for t in tiles:
                 nc.scalar.copy(out=rounded_w(g, i, t).rearrange("p (q c i j) -> p q c j i", q=2, i=4, j=PACK), in_=rows[:, t])
 
         def quantise(name, values, words, at):
-            codes = placed("codes_" + name, [words], U32, at)
-            scales = placed("scales_" + name, [words], U8, at + 4 * words)
+            scales = placed("scales_" + name, [words], U8, at)
+            codes = placed("codes_" + name, [words], U32, at + words)
             nc.vector.quantize_mx(out=codes[:].bitcast(FP8X4), scales=scales[:], in_=values)
             return codes, scales
 
@@ -160,7 +163,7 @@ def tile_moe_pre_lin_bias_kernel(tc, xT, w, b, gate, offs, pos1, pos2, pos3, pos
         x_bf = {}
 
         def round_half(g, h):
-            x_bf[g, h] = placed("x_bf%d_%d" % (g, h), [SH * PACK], BF16, raw_at[g + 1][PAIRS - 1] + h * 8 * KB)
+            x_bf[g, h] = placed("x_bf%d_%d" % (g, h), [SH * PACK], BF16, raw_at[g + 1][2] + h * 8 * KB)
             round_x(x_bf[g, h][:], stage[g][:, :, h * SH : (h + 1) * SH])
 
         def finish_half(g, h, at):
@@ -178,10 +181,10 @@ def tile_moe_pre_lin_bias_kernel(tc, xT, w, b, gate, offs, pos1, pos2, pos3, pos
             load_x(0, j)
             load_w(0, j - 1)
         load_w(0, PAIRS - 1)
+        for j in (0, 1, 3):
+            load_x(1, j)
         for i in range(PAIRS):
             round_w(0, i)
-            if i < 2:
-                load_x(1, i)
             load_w(1, i)
         nc.sync.dma_start(out=bias[:], in_=b.rearrange("(t p) e -> p t e", p=P))
         for r, pos in enumerate((pos1, pos2, pos3, pos4)):
@@ -196,38 +199,36 @@ def tile_moe_pre_lin_bias_kernel(tc, xT, w, b, gate, offs, pos1, pos2, pos3, pos
                     quantise_w((0, t), [(0, e, t) for e in range(E)], AT_WCODES + t * 5 * KB)
         for i in range(PAIRS):
             round_w(1, i)
-            if i == 2:
-                load_x(1, 2, nc.scalar)
             load_w(2, i)
-        load_x(1, 3)
+        load_x(1, 2, nc.scalar)
         for j in range(PACK):
             load_x(2, j)
         for h in range(2):
             round_half(0, h)
 
-        for j in range(2):
+        for j in (0, 1, 3):
             gather(1, j, 0, S, stage[1][:, j, :])
         for t in range(NT):
             quantise_w((1, t), [(1, e, t) for e in range(E)], AT_WCODES + (NT + t) * 5 * KB)
+        gather(1, 2, 0, S, stage[1][:, 2, :])
         for h in range(2):
             finish_half(0, h, AT_XCODES + h * 5 * KB)
-        for j in range(2, PACK):
-            gather(1, j, 0, S, stage[1][:, j, :])
         for i in range(PAIRS):
-            round_w(2, i)
+            round_w(2, i, (0,))
+        for i in range(PAIRS):
+            round_w(2, i, (1,))
             load_w(LAST, i)
-        for j in range(PACK):
+        for j in range(PACK - 1):
             load_x(LAST, j)
         for h in range(2):
             round_half(1, h)
 
-        for j in range(2):
+        for j in range(PACK):
             gather(2, j, 0, S, stage[2][:, j, :])
         finish_half(1, 0, AT_XCODES)
-        for j in range(2, PACK):
-            gather(2, j, 0, S, stage[2][:, j, :])
         for i in range(PAIRS):
             round_w(LAST, i)
+        load_x(LAST, PACK - 1)
         for h in range(2):
             round_half(2, h)
 
@@ -267,17 +268,19 @@ def tile_moe_pre_lin_bias_kernel(tc, xT, w, b, gate, offs, pos1, pos2, pos3, pos
         for i in range(2):
             add_bias(0, i)
         behind = unit(UNITS - 1)
-        quantise_late(1, behind)
+        quantise_held(0, behind)
+        multiply_held(0)
+        quantise_late(1, behind + 5 * KB // 2)
         for n in range(2):
             lo = SH + n * 2 * C
             cols = slice(n * 2 * PACK * C, (n + 1) * 2 * PACK * C)
-            quantise_x(2, lo, lo + 2 * C, x_bf[2, 1][:, cols], behind + 5 * KB + n * 5 * KB // 2)
+            quantise_x(2, lo, lo + 2 * C, x_bf[2, 1][:, cols], behind + 15 * KB // 2 + n * 5 * KB // 2)
             quantise_x(LAST, lo, lo + 2 * C, last_bf[1][:, cols], AT_WCODES + 5 * KB + n * 5 * KB // 2)
             for g in (2, LAST):
                 for e in range(lo // C, lo // C + 2):
                     multiply(g, e, 0)
             add_bias(0, 2 + n)
-        for i in range(PAIRS):
+        for i in range(1, PAIRS):
             quantise_held(i, AT_STAGE + 32 * KB + i * 3 * KB)
             multiply_held(i)
 

@@ -242,8 +242,12 @@ def tile_moe_pre_lin_bias_kernel(tc, xT, w, b, gate, offs, pos1, pos2, pos3, pos
         planes = flat[:].rearrange("p (j s) -> p j s", j=PACK)
         last_bf = [placed("last_bf%d" % h, [SH * PACK], BF16, unit(UNITS - 1 - h)) for h in range(2)]
         round_x(last_bf[0][:], planes[:, :, 0:SH])
-        for n in range(2):
-            round_x(last_bf[1][:, n * 2 * PACK * C : (n + 1) * 2 * PACK * C], planes[:, :, SH + n * 2 * C : SH + (n + 1) * 2 * C])
+        for lo, hi in ((4, 5), (5, 6), (6, E)):
+            round_x(last_bf[1][:, (lo - 4) * PACK * C : (hi - 4) * PACK * C], planes[:, :, lo * C : hi * C])
+
+        def quantise_last(lo, hi):
+            values = last_bf[1][:, (lo - 4) * PACK * C : (hi - 4) * PACK * C]
+            quantise_x(LAST, lo * C, hi * C, values, AT_WCODES + lo * 5 * C)
 
         def quantise_late(h, at):
             quantise_w(("late", h), [(g, 4 * h + 2 * i + q, 0) for i in range(2) for g in (2, LAST) for q in range(2)], at)
@@ -267,6 +271,7 @@ def tile_moe_pre_lin_bias_kernel(tc, xT, w, b, gate, offs, pos1, pos2, pos3, pos
             multiply(LAST, e, 0)
         for i in range(2):
             add_bias(0, i)
+        quantise_last(4, 5)
         behind = unit(UNITS - 1)
         quantise_held(0, behind)
         multiply_held(0)
@@ -275,7 +280,7 @@ def tile_moe_pre_lin_bias_kernel(tc, xT, w, b, gate, offs, pos1, pos2, pos3, pos
             lo = SH + n * 2 * C
             cols = slice(n * 2 * PACK * C, (n + 1) * 2 * PACK * C)
             quantise_x(2, lo, lo + 2 * C, x_bf[2, 1][:, cols], behind + 15 * KB // 2 + n * 5 * KB // 2)
-            quantise_x(LAST, lo, lo + 2 * C, last_bf[1][:, cols], AT_WCODES + 5 * KB + n * 5 * KB // 2)
+            quantise_last(5 + n, 6 + 2 * n)
             for g in (2, LAST):
                 for e in range(lo // C, lo // C + 2):
                     multiply(g, e, 0)

@@ -33,14 +33,14 @@ UNITS = 6
 KB = 1024
 
 SLOT = 4 * WINDOW
-AT_WINDOWS = 0
-AT_STAGE = -(-SLOTS * SLOT // 256) * 256
-AT_UNITS = AT_STAGE + 64 * KB
-AT_W = AT_UNITS + UNITS * 8 * KB
-AT_HELD = AT_W + 16 * KB
+AT_STAGE = 0
+AT_HELD = AT_STAGE + 64 * KB
 AT_WCODES = AT_HELD + 16 * KB
 AT_XCODES = AT_WCODES + 20 * KB
 AT_BIAS = AT_XCODES + 10 * KB
+AT_WINDOWS = AT_BIAS + 64
+AT_UNITS = AT_WINDOWS + SLOTS * SLOT
+AT_W = AT_UNITS + UNITS * 8 * KB
 
 
 def tile_moe_pre_lin_bias_kernel(tc, xT, w, b, gate, offs, pos1, pos2, pos3, pos4, out):
@@ -97,7 +97,7 @@ def tile_moe_pre_lin_bias_kernel(tc, xT, w, b, gate, offs, pos1, pos2, pos3, pos
 
         def rounded_w(g, i, t):
             if g < 2:
-                key, at, width, first = (g, t), AT_W + (g * NT + t) * 8 * KB, 8, 2 * i
+                key, at, width, first = (g, t), (AT_W, AT_HELD)[g] + t * 8 * KB, 8, 2 * i
             elif t == 0:
                 key, at, width, first = ("late", i // 2), AT_W + (i // 2) * 8 * KB, 8, 4 * (i % 2) + 2 * (g - 2)
             else:

@@ -18,29 +18,27 @@ FP8X4 = mybir.dt.float8_e4m3fn_x4
 MULT = mybir.AluOpType.mult
 ADD = mybir.AluOpType.add
 IDENT = mybir.ActivationFunctionType.Identity
+COPY = mybir.ActivationFunctionType.Copy
 
 P = 128
 PACK = 4
 PASSES = K // (P * PACK)
-LAST = PASSES - 1
 NT = N // P
-PAIRS = E // 2
-SH = S // 2
+HALVES = 2
+EH = E // HALVES
+SH = S // HALVES
 LIST = 16
-WINDOW = S + LIST
-SLOTS = 7
-UNITS = 6
+WINDOW = SH + LIST
+RUN = 4
+STEPS = [(h, g) for h in range(HALVES) for g in range(PASSES)]
+LAST = len(STEPS) - 1
 KB = 1024
 
-SLOT = 4 * WINDOW
-AT_STAGE = 0
-AT_HELD = AT_STAGE + 64 * KB
-AT_WCODES = AT_HELD + 16 * KB
-AT_XCODES = AT_WCODES + 20 * KB
-AT_BIAS = AT_XCODES + 10 * KB
-AT_WINDOWS = AT_BIAS + 64
-AT_UNITS = AT_WINDOWS + SLOTS * SLOT
-AT_W = AT_UNITS + UNITS * 8 * KB
+AT_WINDOWS = 0
+AT_STAGE = AT_WINDOWS + PASSES * PACK * 4 * WINDOW
+AT_FIRST = AT_STAGE + 2 * 16 * KB
+AT_SECOND = AT_FIRST + 2 * 8 * KB
+AT_WBF = AT_SECOND + 3 * 8 * KB
 
 
 def tile_moe_pre_lin_bias_kernel(tc, xT, w, b, gate, offs, pos1, pos2, pos3, pos4, out):
@@ -50,268 +48,189 @@ def tile_moe_pre_lin_bias_kernel(tc, xT, w, b, gate, offs, pos1, pos2, pos3, pos
 
     with ExitStack() as ctx:
         keep = ctx.enter_context(tc.tile_pool(name="keep", bufs=1))
+        ring = ctx.enter_context(tc.tile_pool(name="ring", bufs=2))
         arena = ctx.enter_context(tc.tile_pool(name="arena", bufs=1))
         psum = ctx.enter_context(tc.psum_pool(name="psum", bufs=1))
 
         def placed(name, shape, dtype, at):
             return arena.tile([P] + shape, dtype, name=name, offset=at, align_bytes=64)
 
+        def window_at(g, j):
+            return AT_WINDOWS + (g * PACK + j) * 4 * WINDOW
+
         slot_tokens = keep.tile([P, S // LIST], U16, name="slot_tokens")
         token_slots = [keep.tile([P, T // LIST], U16, name="token_slots%d" % r) for r in range(TOP)]
-        gates = keep.tile([P, S], F32, name="gates")
-        bias = placed("bias", [NT, E], F32, AT_BIAS)
-        banks = {(t, i): psum.tile([P, 2 * C], F32, name="bank%d_%d" % (t, i)) for t in range(NT) for i in range(PAIRS)}
-        added = {key: 0 for key in banks}
+        gates = [keep.tile([P, SH], F32, name="gates%d" % h) for h in range(HALVES)]
+        bias = keep.tile([P, NT, E], F32, name="bias")
+        windows = {(g, j): placed("window%d_%d" % (g, j), [WINDOW], F32, window_at(g, j)) for g in range(PASSES) for j in range(PACK)}
+        banks = {(t, i): psum.tile([P, 2 * C], F32, name="bank%d_%d" % (t, i)) for t in range(NT) for i in range(E // 2)}
 
-        windows, w_raw, w_bf, w_mx, x_mx = {}, {}, {}, {}, {}
-
-        def window_at(g, j):
-            return AT_WINDOWS + (g * PACK + j) % SLOTS * SLOT
-
-        def unit(n):
-            return AT_UNITS + n * 8 * KB
+        w_raw, w_mx, stage, x_bf, x_mx = {}, {}, {}, {}, {}
 
         def load_x(g, j, queue=nc.sync):
-            if (g, j) == (LAST, PACK - 1):
-                windows[g, j] = placed("window_end", [SH + LIST], F32, raw_at[LAST][0])
-            else:
-                windows[g, j] = placed("window%d_%d" % (g, j), [WINDOW], F32, window_at(g, j))
             queue.dma_start(out=windows[g, j][:, 0:T], in_=x_rows[g, j])
 
-        raw_at = {
-            0: (unit(0), unit(1), unit(2), unit(3)),
-            1: (AT_XCODES, AT_WCODES + 10 * KB, unit(4), window_at(1, 2)),
-            2: (unit(0), unit(1), unit(2), unit(2)),
-            3: (unit(4), unit(5), unit(0), unit(0)),
-        }
-        double = {}
+        def raw_at(s, i):
+            return (AT_FIRST + s % 2 * 8 * KB, AT_SECOND + s % 3 * 8 * KB)[i]
 
-        def load_w(g, i):
-            if g > 0 and raw_at[g][i] == raw_at[g][2]:
-                if g not in double:
-                    double[g] = placed("w_raw%d_end" % g, [2, 2, PACK * N], F32, raw_at[g][i])
-                w_raw[g, i] = double[g][:, i % 2]
-            else:
-                w_raw[g, i] = placed("w_raw%d_%d" % (g, i), [2, PACK * N], F32, raw_at[g][i])[:]
-            nc.sync.dma_start(out=w_raw[g, i], in_=w_rows[g, :, 2 * i : 2 * i + 2, :])
+        def load_w(s, i):
+            h, g = STEPS[s]
+            w_raw[s, i] = placed("w_raw%d_%d" % (s, i), [2, PACK * N], F32, raw_at(s, i))
+            nc.sync.dma_start(out=w_raw[s, i][:], in_=w_rows[g, :, h * EH + 2 * i : h * EH + 2 * i + 2, :])
 
-        def rounded_w(g, i, t):
-            if g < 2:
-                key, at, width, first = (g, t), (AT_W, AT_HELD)[g] + t * 8 * KB, 8, 2 * i
-            elif t == 0:
-                key, at, width, first = ("late", i // 2), AT_W + (i // 2) * 8 * KB, 8, 4 * (i % 2) + 2 * (g - 2)
-            else:
-                key, at, width, first = ("held", i), AT_HELD + i * 4 * KB, 4, 2 * (g - 2)
-            if key not in w_bf:
-                w_bf[key] = placed("w_bf_%s_%d" % key, [width * P * PACK], BF16, at)
-            return w_bf[key][:, first * P * PACK : (first + 2) * P * PACK]
+        def round_w(dst, s, i, lo, hi):
+            nc.vector.tensor_copy(
+                out=dst.rearrange("p (q c i j) -> p q c j i", q=2, i=RUN, j=PACK),
+                in_=w_raw[s, i][:].rearrange("p q (j c i) -> p q c j i", j=PACK, i=RUN)[:, :, lo // RUN : hi // RUN],
+            )
 
-        def round_w(g, i, tiles=range(NT)):
-            rows = w_raw[g, i].rearrange("p q (j t c i) -> p t q c j i", j=PACK, t=NT, i=4)
-            for t in tiles:
-                nc.scalar.copy(out=rounded_w(g, i, t).rearrange("p (q c i j) -> p q c j i", q=2, i=4, j=PACK), in_=rows[:, t])
-
-        def quantise(name, values, words, at):
-            scales = placed("scales_" + name, [words], U8, at)
-            codes = placed("codes_" + name, [words], U32, at + words)
+        def quantise(name, values, words):
+            codes = ring.tile([P, words], U32, name=name + "_codes", align_bytes=64)
+            scales = ring.tile([P, words], U8, name=name + "_scales", align_bytes=64)
             nc.vector.quantize_mx(out=codes[:].bitcast(FP8X4), scales=scales[:], in_=values)
             return codes, scales
 
-        def quantise_w(key, members, at):
-            codes, scales = quantise("w_%s_%d" % key, w_bf[key][:], len(members) * P, at)
+        def quantise_w(name, values, members):
+            codes, scales = quantise(name, values, len(members) * P)
             for n, member in enumerate(members):
                 w_mx[member] = (codes[:, n * P : (n + 1) * P], scales[:, n * P : (n + 1) * P])
 
-        def quantise_x(g, lo, hi, values, at):
-            codes, scales = quantise("x%d_%d" % (g, lo), values, hi - lo, at)
-            for e in range(lo // C, hi // C):
-                cols = slice(e * C - lo, (e + 1) * C - lo)
-                x_mx[g, e] = (codes[:, cols], scales[:, cols])
+        def quantise_x(name, s, lo, hi):
+            codes, scales = quantise(name, x_bf[s][:, lo * PACK : hi * PACK], hi - lo)
+            for q in range(lo // C, hi // C):
+                cols = slice(q * C - lo, (q + 1) * C - lo)
+                x_mx[s, q] = (codes[:, cols], scales[:, cols])
 
-        def gather(g, j, lo, hi, into):
-            nc.vector.tensor_tensor(into, windows[g, j][:].indirect(slot_tokens[:, lo // LIST : hi // LIST]), gates[:, lo:hi], MULT)
+        def gather(s, j, lo, hi, engine):
+            h, g = STEPS[s]
+            if s not in stage:
+                stage[s] = placed("stage%d" % s, [PACK, SH], F32, AT_STAGE + s % 2 * 16 * KB)
+            picked = windows[g, j][:].indirect(slot_tokens[:, (h * SH + lo) // LIST : (h * SH + hi) // LIST])
+            if engine is nc.scalar:
+                nc.scalar.activation(stage[s][:, j, lo:hi], picked, COPY)
+            else:
+                nc.vector.tensor_copy(stage[s][:, j, lo:hi], picked)
 
-        def round_x(dst, src):
-            nc.scalar.copy(
-                out=dst.rearrange("p (c i t) -> p c t i", i=4, t=PACK),
-                in_=src.rearrange("p t (c i) -> p c t i", i=4),
+        def weigh(s, lo, hi):
+            h, g = STEPS[s]
+            if s not in x_bf:
+                x_bf[s] = placed("x_bf%d" % s, [SH * PACK], BF16, raw_at(min(s, LAST - 1), 1 if s < LAST else 0))
+            nc.vector.tensor_tensor(
+                x_bf[s][:, lo * PACK : hi * PACK].rearrange("p (c i j) -> p c j i", i=RUN, j=PACK),
+                stage[s][:, :, lo:hi].rearrange("p j (c i) -> p c j i", i=RUN),
+                gates[h][:, lo:hi].rearrange("p (c o i) -> p c o i", o=1, i=RUN).to_broadcast([P, (hi - lo) // RUN, PACK, RUN]),
+                MULT,
             )
 
-        def multiply(g, e, t):
-            key = (t, e // 2)
+        def multiply(s, q, t):
+            h, g = STEPS[s]
+            e = h * EH + q
             nc.tensor.matmul_mx(
-                out=banks[key][:, (e % 2) * C : (e % 2 + 1) * C],
-                lhsT=w_mx[g, e, t][0].bitcast(FP8X4),
-                lhsT_scale=w_mx[g, e, t][1],
-                rhs=x_mx[g, e][0].bitcast(FP8X4),
-                rhs_scale=x_mx[g, e][1],
-                start=(added[key] == 0),
-                stop=(added[key] == 2 * PASSES - 1),
+                out=banks[t, e // 2][:, (e % 2) * C : (e % 2 + 1) * C],
+                lhsT=w_mx[s, q, t][0].bitcast(FP8X4),
+                lhsT_scale=w_mx[s, q, t][1],
+                rhs=x_mx[s, q][0].bitcast(FP8X4),
+                rhs_scale=x_mx[s, q][1],
+                start=(g == 0 and e % 2 == 0),
+                stop=(g == PASSES - 1 and e % 2 == 1),
             )
-            added[key] = added[key] + 1
 
-        def add_bias(t, i):
-            for e in (2 * i, 2 * i + 1):
+        def add_bias(t, experts):
+            for e in experts:
                 nc.scalar.activation(
                     out=y[t][:, e * C : (e + 1) * C],
-                    in_=banks[t, i][:, (e % 2) * C : (e % 2 + 1) * C],
+                    in_=banks[t, e // 2][:, (e % 2) * C : (e % 2 + 1) * C],
                     func=IDENT,
                     bias=bias[:, t, e : e + 1],
                 )
 
-        stage = [placed("stage%d" % g, [PACK, S], F32, AT_STAGE + (g % 2) * 32 * KB) for g in range(LAST)]
-        x_bf = {}
+        def prepare_w(s, between):
+            w_bf = placed("w_bf%d" % s, [EH * N * PACK], BF16, AT_WBF)
+            for i in range(2):
+                round_w(w_bf[:, i * 2 * N * PACK : (i + 1) * 2 * N * PACK], s, i, 0, N)
+            between()
+            quantise_w("w", w_bf[:], [(s, q, t) for q in range(EH) for t in range(NT)])
 
-        def round_half(g, h):
-            x_bf[g, h] = placed("x_bf%d_%d" % (g, h), [SH * PACK], BF16, raw_at[g + 1][2] + h * 8 * KB)
-            round_x(x_bf[g, h][:], stage[g][:, :, h * SH : (h + 1) * SH])
-
-        def finish_half(g, h, at):
-            quantise_x(g, h * SH, (h + 1) * SH, x_bf[g, h][:], at)
-            for e in range(h * PAIRS, (h + 1) * PAIRS):
-                for t in range(NT):
-                    multiply(g, e, t)
-
-        gate_cuts = (0, 256, 832, S)
         nc.sync.dma_start(slot_tokens[:], offs)
         load_x(0, 0, nc.scalar)
-        for lo, hi in zip(gate_cuts, gate_cuts[1:]):
-            nc.sync.dma_start(out=gates[:, lo:hi], in_=gate[0:P, lo:hi])
         for j in range(1, PACK):
             load_x(0, j)
-            load_w(0, j - 1)
-        load_w(0, PAIRS - 1)
-        for j in (0, 1, 3):
-            load_x(1, j)
-        for i in range(PAIRS):
-            round_w(0, i)
-            load_w(1, i)
+        load_w(0, 0)
+        load_w(0, 1)
+        nc.sync.dma_start(out=gates[0][:], in_=gate[0:P, 0:SH])
+        for g in range(1, PASSES):
+            for i in range(2):
+                load_x(g, 2 * i)
+                load_x(g, 2 * i + 1)
+                if g < PASSES - 1:
+                    load_w(g, i)
+        nc.sync.dma_start(out=gates[1][:], in_=gate[0:P, SH:S])
         nc.sync.dma_start(out=bias[:], in_=b.rearrange("(t p) e -> p t e", p=P))
         for r, pos in enumerate((pos1, pos2, pos3, pos4)):
             nc.sync.dma_start(token_slots[r][:], pos)
 
-        for lo, hi in zip(gate_cuts, gate_cuts[1:]):
-            gather(0, 0, lo, hi, stage[0][:, 0, lo:hi])
-        for j in range(1, PACK):
-            gather(0, j, 0, S, stage[0][:, j, :])
-            if j == 2:
-                for t in range(NT):
-                    quantise_w((0, t), [(0, e, t) for e in range(E)], AT_WCODES + t * 5 * KB)
-        for i in range(PAIRS):
-            round_w(1, i)
-            load_w(2, i)
-        load_x(1, 2, nc.scalar)
-        for j in range(PACK):
-            load_x(2, j)
-        for h in range(2):
-            round_half(0, h)
-
-        for j in (0, 1, 3):
-            gather(1, j, 0, S, stage[1][:, j, :])
-        for t in range(NT):
-            quantise_w((1, t), [(1, e, t) for e in range(E)], AT_WCODES + (NT + t) * 5 * KB)
-        gather(1, 2, 0, S, stage[1][:, 2, :])
-        for h in range(2):
-            finish_half(0, h, AT_XCODES + h * 5 * KB)
-        for i in range(PAIRS):
-            round_w(2, i, (0,))
-        for i in range(PAIRS):
-            round_w(2, i, (1,))
-            load_w(LAST, i)
-        for j in range(PACK - 1):
-            load_x(LAST, j)
-        for h in range(2):
-            round_half(1, h)
+        def finish(s):
+            quantise_x("x", s, 0, SH)
+            for t in range(NT):
+                for q in range(EH):
+                    multiply(s, q, t)
 
         for j in range(PACK):
-            gather(2, j, 0, S, stage[2][:, j, :])
-        finish_half(1, 0, AT_XCODES)
-        for i in range(PAIRS):
-            round_w(LAST, i)
-        load_x(LAST, PACK - 1)
-        for h in range(2):
-            round_half(2, h)
+            gather(0, j, 0, SH, nc.vector if j == 1 else nc.scalar)
+        prepare_w(0, lambda: None)
+        cut = SH - C
+        for s in range(LAST):
+            for lo, hi in ((0, SH),) if s + 1 < LAST else ((0, cut), (cut, SH)):
+                for j in range(PACK):
+                    gather(s + 1, j, lo, hi, nc.scalar)
+            weigh(s, 0, SH)
+            if s + 3 <= LAST:
+                for i in range(2):
+                    load_w(s + 3, i)
+            if s + 1 < LAST:
+                prepare_w(s + 1, lambda: finish(s))
 
-        y = [placed("y%d" % t, [S], F32, window_at(2, t + 1)) for t in range(NT)]
-        flat = placed("last_stage", [8 * SH], F32, AT_STAGE + 32 * KB)
-        for j in range(2):
-            gather(LAST, j, 0, S, flat[:, j * S : (j + 1) * S])
-        for h in range(2):
-            for j in range(2, PACK):
-                gather(LAST, j, h * SH, (h + 1) * SH, flat[:, (2 * j + h) * SH : (2 * j + h + 1) * SH])
-        planes = flat[:].rearrange("p (j s) -> p j s", j=PACK)
-        last_bf = [placed("last_bf%d" % h, [SH * PACK], BF16, unit(UNITS - 1 - h)) for h in range(2)]
-        round_x(last_bf[0][:], planes[:, :, 0:SH])
-        for lo, hi in ((4, 5), (5, 6), (6, E)):
-            round_x(last_bf[1][:, (lo - 4) * PACK * C : (hi - 4) * PACK * C], planes[:, :, lo * C : hi * C])
-
-        def quantise_last(lo, hi):
-            values = last_bf[1][:, (lo - 4) * PACK * C : (hi - 4) * PACK * C]
-            quantise_x(LAST, lo * C, hi * C, values, AT_WCODES + lo * 5 * C)
-
-        def quantise_late(h, at):
-            quantise_w(("late", h), [(g, 4 * h + 2 * i + q, 0) for i in range(2) for g in (2, LAST) for q in range(2)], at)
-
-        def quantise_held(i, at):
-            quantise_w(("held", i), [(g, 2 * i + q, 1) for g in (2, LAST) for q in range(2)], at)
-
-        def multiply_held(i):
-            for g in (2, LAST):
-                for e in (2 * i, 2 * i + 1):
-                    multiply(g, e, 1)
-            add_bias(1, i)
-
-        finish_half(1, 1, window_at(LAST, 0))
-        quantise_late(0, window_at(LAST, 1))
-        quantise_x(2, 0, SH, x_bf[2, 0][:], AT_XCODES)
-        for e in range(PAIRS):
-            multiply(2, e, 0)
-        quantise_x(LAST, 0, SH, last_bf[0][:], AT_WCODES)
-        for e in range(PAIRS):
-            multiply(LAST, e, 0)
+        y = [placed("y%d" % t, [S], F32, window_at(PASSES - 1, 2 * t)) for t in range(NT)]
+        piece = 2 * P * PACK
+        w_first = placed("w_first", [2 * piece], BF16, AT_WBF)
         for i in range(2):
-            add_bias(0, i)
-        quantise_last(4, 5)
-        behind = unit(UNITS - 1)
-        quantise_held(0, behind)
-        multiply_held(0)
-        quantise_late(1, behind + 5 * KB // 2)
-        for n in range(2):
-            lo = SH + n * 2 * C
-            cols = slice(n * 2 * PACK * C, (n + 1) * 2 * PACK * C)
-            quantise_x(2, lo, lo + 2 * C, x_bf[2, 1][:, cols], behind + 15 * KB // 2 + n * 5 * KB // 2)
-            quantise_last(5 + n, 6 + 2 * n)
-            for g in (2, LAST):
-                for e in range(lo // C, lo // C + 2):
-                    multiply(g, e, 0)
-            add_bias(0, 2 + n)
-        for i in range(1, PAIRS):
-            quantise_held(i, AT_STAGE + 32 * KB + i * 3 * KB)
-            multiply_held(i)
+            round_w(w_first[:, i * piece : (i + 1) * piece], LAST, i, 0, P)
+        finish(LAST - 1)
+        quantise_w("w", w_first[:], [(LAST, q, 0) for q in range(EH)])
+        weigh(LAST, 0, 2 * C)
+        weigh(LAST, 2 * C, cut)
+        quantise_x("x", LAST, 0, 2 * C)
+        weigh(LAST, cut, SH)
+        quantise_x("x2", LAST, 2 * C, cut)
+        w_held = [placed("w_held%d" % i, [piece], BF16, AT_STAGE + 16 * KB + i * 2 * piece) for i in range(2)]
+        round_w(w_held[0][:], LAST, 0, P, N)
+        quantise_x("x2", LAST, cut, SH)
+        round_w(w_held[1][:], LAST, 1, P, N)
+        for q in range(EH):
+            multiply(LAST, q, 0)
+        for i in range(2):
+            quantise_w("held", w_held[i][:], [(LAST, 2 * i + q, 1) for q in range(2)])
+        for q in range(EH):
+            multiply(LAST, q, 1)
+        add_bias(0, range(0, EH))
+        add_bias(1, range(0, EH))
+        add_bias(0, range(EH, E))
 
-        running = [placed("running%d" % t, [TOP, T], F32, AT_STAGE + t * 4 * TOP * T) for t in range(NT)]
-        first, second, whole = slice(0, T // 2), slice(T // 2, T), slice(0, T)
-        partial = {(t, r): running[t][:, r, :] for t in range(NT) for r in range(TOP)}
-        third = placed("third", [T], F32, AT_BIAS + 64 - 4 * T)
-        partial[0, 2] = third[:]
+        sums = [placed("sums%d" % t, [TOP + 1, T], F32, AT_SECOND + t * 10 * KB) for t in range(NT)]
 
-        def combine(t, r, tokens, queue=nc.sync):
-            picked = y[t][:].indirect(token_slots[r][:, tokens.start // LIST : tokens.stop // LIST])
-            if r == 0:
-                nc.vector.tensor_copy(partial[t, 0][:, tokens], picked)
-            else:
-                nc.vector.tensor_tensor(partial[t, r][:, tokens], picked, partial[t, r - 1][:, tokens], ADD)
-            if r == TOP - 1:
-                queue.dma_start(out=out[t * P : (t + 1) * P, tokens], in_=partial[t, r][:, tokens])
+        def picked(t, r):
+            return y[t][:].indirect(token_slots[r][:])
 
+        nc.scalar.activation(sums[0][:, 0, :], picked(0, 0), COPY)
+        add_bias(1, range(EH, E))
+        nc.vector.tensor_copy(sums[0][:, 1, :], picked(0, 1))
         for r in range(2):
-            combine(0, r, first)
-            combine(0, r, second)
-        for r in range(2):
-            combine(1, r, whole)
-            combine(0, r + 2, whole)
-        combine(1, 2, first)
-        combine(1, 2, second)
-        combine(1, 3, first)
-        combine(1, 3, slice(T // 2, 3 * T // 4), nc.scalar)
-        combine(1, 3, slice(3 * T // 4, T))
+            nc.vector.tensor_tensor(sums[0][:, r + 2, :], picked(0, r + 2), sums[0][:, 1 - r, :], ADD)
+        for r in range(3):
+            nc.scalar.activation(sums[1][:, r, :], picked(1, r), COPY)
+        nc.vector.tensor_tensor(sums[1][:, 3, :], picked(1, 3), sums[1][:, 0, :], ADD)
+        nc.vector.tensor_tensor(sums[0][:, 4, :], sums[0][:, 2, :], sums[0][:, 3, :], ADD)
+        nc.sync.dma_start(out=out[0:P, :], in_=sums[0][:, 4, :])
+        nc.vector.tensor_tensor(sums[1][:, 4, :], sums[1][:, 3, :], sums[1][:, 1, :], ADD)
+        nc.vector.tensor_tensor(sums[1][:, 0, :], sums[1][:, 4, :], sums[1][:, 2, :], ADD)
+        nc.sync.dma_start(out=out[P : 2 * P, :], in_=sums[1][:, 0, :])

@@ -1,6 +1,7 @@
 from contextlib import ExitStack
 
 import concourse.mybir as mybir
+from concourse.masks import make_identity
 
 K, T, E, C, N = 2048, 512, 8, 256, 256
 TOP = 4
@@ -32,13 +33,20 @@ WINDOW = SH + LIST
 RUN = 4
 STEPS = [(h, g) for h in range(HALVES) for g in range(PASSES)]
 LAST = len(STEPS) - 1
+BANK = 512
 KB = 1024
+PAD = 32
 
 AT_WINDOWS = 0
 AT_STAGE = AT_WINDOWS + PASSES * PACK * 4 * WINDOW
-AT_FIRST = AT_STAGE + 2 * 16 * KB
-AT_SECOND = AT_FIRST + 2 * 8 * KB
-AT_WBF = AT_SECOND + 3 * 8 * KB
+AT_RAW = AT_STAGE + 2 * 16 * KB
+RAWS = 6
+AT_BF = AT_RAW + RAWS * 8 * KB
+
+PIECES = {s: ((0, SH),) for s in range(LAST - 1)}
+PIECES[LAST - 1] = ((0, BANK), (BANK, SH))
+PIECES[LAST] = ((0, BANK), (BANK, SH - C), (SH - C, SH))
+SHARED_STEPS = range(1, LAST - 1)
 
 
 def tile_moe_pre_lin_bias_kernel(tc, xT, w, b, gate, offs, pos1, pos2, pos3, pos4, out):
@@ -55,34 +63,46 @@ def tile_moe_pre_lin_bias_kernel(tc, xT, w, b, gate, offs, pos1, pos2, pos3, pos
         def placed(name, shape, dtype, at):
             return arena.tile([P] + shape, dtype, name=name, offset=at, align_bytes=64)
 
+        def bank(name, n):
+            return psum.tile([P, BANK], F32, name=name, offset=n * 4 * BANK)
+
         def window_at(g, j):
             return AT_WINDOWS + (g * PACK + j) * 4 * WINDOW
 
         slot_tokens = keep.tile([P, S // LIST], U16, name="slot_tokens")
         token_slots = [keep.tile([P, T // LIST], U16, name="token_slots%d" % r) for r in range(TOP)]
-        gates = [keep.tile([P, SH], F32, name="gates%d" % h) for h in range(HALVES)]
+        gate_rows = keep.tile([P, P], F32, name="gate_rows")
+        gate_cols = keep.tile([P, S // P], F32, name="gate_cols")
+        identity = keep.tile([P, P], F32, name="identity")
         bias = keep.tile([P, NT, E], F32, name="bias")
         windows = {(g, j): placed("window%d_%d" % (g, j), [WINDOW], F32, window_at(g, j)) for g in range(PASSES) for j in range(PACK)}
-        banks = {(t, i): psum.tile([P, 2 * C], F32, name="bank%d_%d" % (t, i)) for t in range(NT) for i in range(E // 2)}
+        y = [keep.tile([P, S], F32, name="y0"), placed("y1", [S], F32, window_at(PASSES - 1, 0))]
+        acc_bank = {(0, 0): 0, (0, 1): 1, (1, 0): 2, (1, 1): 3, (0, 2): 4, (0, 3): 5, (1, 2): 0, (1, 3): 1}
+        acc = {key: bank("acc%d_%d" % key, n) for key, n in acc_bank.items()}
+        gates = [bank("gates%d" % n, 4 + n) for n in range(S // BANK)]
 
-        w_raw, w_mx, stage, x_bf, x_mx = {}, {}, {}, {}, {}
+        w_raw, w_bf, w_mx, stage, x_bf, x_mx = {}, {}, {}, {}, {}, {}
 
         def load_x(g, j, queue=nc.sync):
             queue.dma_start(out=windows[g, j][:, 0:T], in_=x_rows[g, j])
 
-        def raw_at(s, i):
-            return (AT_FIRST + s % 2 * 8 * KB, AT_SECOND + s % 3 * 8 * KB)[i]
-
         def load_w(s, i):
             h, g = STEPS[s]
-            w_raw[s, i] = placed("w_raw%d_%d" % (s, i), [2, PACK * N], F32, raw_at(s, i))
+            w_raw[s, i] = placed("w_raw%d_%d" % (s, i), [2, PACK * N], F32, AT_RAW + (2 * s + i) % RAWS * 8 * KB)
             nc.sync.dma_start(out=w_raw[s, i][:], in_=w_rows[g, :, h * EH + 2 * i : h * EH + 2 * i + 2, :])
 
-        def round_w(dst, s, i, lo, hi):
-            nc.vector.tensor_copy(
-                out=dst.rearrange("p (q c i j) -> p q c j i", q=2, i=RUN, j=PACK),
-                in_=w_raw[s, i][:].rearrange("p q (j c i) -> p q c j i", j=PACK, i=RUN)[:, :, lo // RUN : hi // RUN],
-            )
+        def round_w(s):
+            first = s % 2 * PAD
+            w_bf[s] = placed("w_bf%d" % s, [SH * PACK + PAD], BF16, AT_BF + s % 2 * 8 * KB)[:, first : first + SH * PACK]
+            for q in range(EH):
+                nc.gpsimd.tensor_scalar(
+                    w_bf[s][:, q * N * PACK : (q + 1) * N * PACK].rearrange("p (n j) -> p n j", j=PACK),
+                    w_raw[s, q // 2][:, q % 2, :].rearrange("p (j n) -> p n j", j=PACK),
+                    1.0,
+                    0.0,
+                    MULT,
+                    ADD,
+                )
 
         def quantise(name, values, words):
             codes = ring.tile([P, words], U32, name=name + "_codes", align_bytes=64)
@@ -90,10 +110,10 @@ def tile_moe_pre_lin_bias_kernel(tc, xT, w, b, gate, offs, pos1, pos2, pos3, pos
             nc.vector.quantize_mx(out=codes[:].bitcast(FP8X4), scales=scales[:], in_=values)
             return codes, scales
 
-        def quantise_w(name, values, members):
-            codes, scales = quantise(name, values, len(members) * P)
-            for n, member in enumerate(members):
-                w_mx[member] = (codes[:, n * P : (n + 1) * P], scales[:, n * P : (n + 1) * P])
+        def quantise_w(s):
+            codes, scales = quantise("w", w_bf[s], SH)
+            for n in range(EH * NT):
+                w_mx[s, n // NT, n % NT] = (codes[:, n * P : (n + 1) * P], scales[:, n * P : (n + 1) * P])
 
         def quantise_x(name, s, lo, hi):
             codes, scales = quantise(name, x_bf[s][:, lo * PACK : hi * PACK], hi - lo)
@@ -101,136 +121,139 @@ def tile_moe_pre_lin_bias_kernel(tc, xT, w, b, gate, offs, pos1, pos2, pos3, pos
                 cols = slice(q * C - lo, (q + 1) * C - lo)
                 x_mx[s, q] = (codes[:, cols], scales[:, cols])
 
+        def staged(s, lo, hi):
+            first, last = [piece for piece in PIECES[s] if piece[0] <= lo < piece[1]][0]
+            if (s, first) not in stage:
+                at = AT_STAGE + s % 2 * 16 * KB + first * PACK * 4
+                stage[s, first] = placed("stage%d_%d" % (s, first), [PACK, last - first], F32, at)
+            return stage[s, first][:, :, lo - first : hi - first]
+
         def gather(s, j, lo, hi, engine):
             h, g = STEPS[s]
-            if s not in stage:
-                stage[s] = placed("stage%d" % s, [PACK, SH], F32, AT_STAGE + s % 2 * 16 * KB)
             picked = windows[g, j][:].indirect(slot_tokens[:, (h * SH + lo) // LIST : (h * SH + hi) // LIST])
             if engine is nc.scalar:
-                nc.scalar.activation(stage[s][:, j, lo:hi], picked, COPY)
+                nc.scalar.activation(staged(s, lo, hi)[:, j, :], picked, COPY)
             else:
-                nc.vector.tensor_copy(stage[s][:, j, lo:hi], picked)
+                nc.vector.tensor_copy(staged(s, lo, hi)[:, j, :], picked)
 
         def weigh(s, lo, hi):
             h, g = STEPS[s]
             if s not in x_bf:
-                x_bf[s] = placed("x_bf%d" % s, [SH * PACK], BF16, raw_at(min(s, LAST - 1), 1 if s < LAST else 0))
+                x_bf[s] = placed("x_bf%d" % s, [SH * PACK], BF16, AT_BF + (s + 1) % 2 * (8 * KB + 2 * PAD))
+            weights = gates[(h * SH + lo) // BANK][:, lo % BANK : lo % BANK + hi - lo]
             nc.vector.tensor_tensor(
                 x_bf[s][:, lo * PACK : hi * PACK].rearrange("p (c i j) -> p c j i", i=RUN, j=PACK),
-                stage[s][:, :, lo:hi].rearrange("p j (c i) -> p c j i", i=RUN),
-                gates[h][:, lo:hi].rearrange("p (c o i) -> p c o i", o=1, i=RUN).to_broadcast([P, (hi - lo) // RUN, PACK, RUN]),
+                staged(s, lo, hi).rearrange("p j (c i) -> p c j i", i=RUN),
+                weights.rearrange("p (c o i) -> p c o i", o=1, i=RUN).to_broadcast([P, (hi - lo) // RUN, PACK, RUN]),
                 MULT,
             )
 
-        def multiply(s, q, t):
+        def multiply(s, experts):
             h, g = STEPS[s]
-            e = h * EH + q
-            nc.tensor.matmul_mx(
-                out=banks[t, e // 2][:, (e % 2) * C : (e % 2 + 1) * C],
-                lhsT=w_mx[s, q, t][0].bitcast(FP8X4),
-                lhsT_scale=w_mx[s, q, t][1],
-                rhs=x_mx[s, q][0].bitcast(FP8X4),
-                rhs_scale=x_mx[s, q][1],
-                start=(g == 0 and e % 2 == 0),
-                stop=(g == PASSES - 1 and e % 2 == 1),
-            )
+            for t in range(NT):
+                for q in experts:
+                    e = h * EH + q
+                    nc.tensor.matmul_mx(
+                        out=acc[t, e // 2][:, (e % 2) * C : (e % 2 + 1) * C],
+                        lhsT=w_mx[s, q, t][0].bitcast(FP8X4),
+                        lhsT_scale=w_mx[s, q, t][1],
+                        rhs=x_mx[s, q][0].bitcast(FP8X4),
+                        rhs_scale=x_mx[s, q][1],
+                        start=(g == 0 and e % 2 == 0),
+                        stop=(g == PASSES - 1 and e % 2 == 1),
+                    )
 
-        def add_bias(t, experts):
-            for e in experts:
+        def bias_on_scalar(t, i):
+            for e in (2 * i, 2 * i + 1):
                 nc.scalar.activation(
                     out=y[t][:, e * C : (e + 1) * C],
-                    in_=banks[t, e // 2][:, (e % 2) * C : (e % 2 + 1) * C],
+                    in_=acc[t, i][:, (e % 2) * C : (e % 2 + 1) * C],
                     func=IDENT,
                     bias=bias[:, t, e : e + 1],
                 )
 
-        def prepare_w(s, between):
-            w_bf = placed("w_bf%d" % s, [EH * N * PACK], BF16, AT_WBF)
-            for i in range(2):
-                round_w(w_bf[:, i * 2 * N * PACK : (i + 1) * 2 * N * PACK], s, i, 0, N)
-            between()
-            quantise_w("w", w_bf[:], [(s, q, t) for q in range(EH) for t in range(NT)])
+        def bias_on_vector(t, i):
+            nc.vector.tensor_tensor(
+                y[t][:, i * BANK : (i + 1) * BANK].rearrange("p (e c) -> p e c", e=2),
+                acc[t, i][:].rearrange("p (e c) -> p e c", e=2),
+                bias[:, t, 2 * i : 2 * i + 2].rearrange("p (e o) -> p e o", o=1).to_broadcast([P, 2, C]),
+                ADD,
+            )
 
         nc.sync.dma_start(slot_tokens[:], offs)
         load_x(0, 0, nc.scalar)
-        for j in range(1, PACK):
+        load_x(0, 1)
+        nc.sync.dma_start(out=gate_rows[:], in_=gate[0 : P * P // S, :].rearrange("r (q p) -> (r q) p", p=P))
+        for j in range(2, PACK):
             load_x(0, j)
-        load_w(0, 0)
-        load_w(0, 1)
-        nc.sync.dma_start(out=gates[0][:], in_=gate[0:P, 0:SH])
-        for g in range(1, PASSES):
+        for g in range(PASSES - 1):
             for i in range(2):
-                load_x(g, 2 * i)
-                load_x(g, 2 * i + 1)
-                if g < PASSES - 1:
-                    load_w(g, i)
-        nc.sync.dma_start(out=gates[1][:], in_=gate[0:P, SH:S])
+                load_w(g, i)
+                load_x(g + 1, 2 * i)
+                load_x(g + 1, 2 * i + 1)
         nc.sync.dma_start(out=bias[:], in_=b.rearrange("(t p) e -> p t e", p=P))
         for r, pos in enumerate((pos1, pos2, pos3, pos4)):
             nc.sync.dma_start(token_slots[r][:], pos)
 
-        def finish(s):
-            quantise_x("x", s, 0, SH)
-            for t in range(NT):
-                for q in range(EH):
-                    multiply(s, q, t)
-
+        make_identity(nc, identity[:])
+        turned = bank("turned", 7)
+        nc.tensor.transpose(turned[:, 0:P], gate_rows[:], identity[:])
         for j in range(PACK):
-            gather(0, j, 0, SH, nc.vector if j == 1 else nc.scalar)
-        prepare_w(0, lambda: None)
-        cut = SH - C
+            gather(0, j, 0, SH, nc.vector if j % 2 else nc.scalar)
+            if j == 1:
+                nc.vector.tensor_copy(gate_cols[:], turned[:, 0 : S // P])
+        for q in range(S // P):
+            nc.tensor.transpose(
+                gates[q * P // BANK][:, q * P % BANK : q * P % BANK + P], gate_cols[:, q : q + 1].to_broadcast([P, P]), identity[:]
+            )
+
         for s in range(LAST):
-            for lo, hi in ((0, SH),) if s + 1 < LAST else ((0, cut), (cut, SH)):
+            shared = s + 1 in SHARED_STEPS
+            for lo, hi in PIECES[s + 1]:
                 for j in range(PACK):
-                    gather(s + 1, j, lo, hi, nc.scalar)
-            weigh(s, 0, SH)
+                    gather(s + 1, j, BANK if shared and j == PACK - 1 else lo, hi, nc.scalar)
+            round_w(s)
             if s + 3 <= LAST:
                 for i in range(2):
                     load_w(s + 3, i)
-            if s + 1 < LAST:
-                prepare_w(s + 1, lambda: finish(s))
+            for lo in range(0, SH, BANK):
+                weigh(s, lo, lo + BANK)
+            if shared:
+                gather(s + 1, PACK - 1, 0, BANK, nc.vector)
+            if s == PASSES:
+                for i in range(2):
+                    bias_on_vector(0, i)
+            quantise_w(s)
+            quantise_x("x", s, 0, SH)
+            multiply(s, range(EH))
 
-        y = [placed("y%d" % t, [S], F32, window_at(PASSES - 1, 2 * t)) for t in range(NT)]
-        piece = 2 * P * PACK
-        w_first = placed("w_first", [2 * piece], BF16, AT_WBF)
-        for i in range(2):
-            round_w(w_first[:, i * piece : (i + 1) * piece], LAST, i, 0, P)
-        finish(LAST - 1)
-        quantise_w("w", w_first[:], [(LAST, q, 0) for q in range(EH)])
-        weigh(LAST, 0, 2 * C)
-        weigh(LAST, 2 * C, cut)
-        quantise_x("x", LAST, 0, 2 * C)
-        weigh(LAST, cut, SH)
-        quantise_x("x2", LAST, 2 * C, cut)
-        w_held = [placed("w_held%d" % i, [piece], BF16, AT_STAGE + 16 * KB + i * 2 * piece) for i in range(2)]
-        round_w(w_held[0][:], LAST, 0, P, N)
-        quantise_x("x2", LAST, cut, SH)
-        round_w(w_held[1][:], LAST, 1, P, N)
-        for q in range(EH):
-            multiply(LAST, q, 0)
-        for i in range(2):
-            quantise_w("held", w_held[i][:], [(LAST, 2 * i + q, 1) for q in range(2)])
-        for q in range(EH):
-            multiply(LAST, q, 1)
-        add_bias(0, range(0, EH))
-        add_bias(1, range(0, EH))
-        add_bias(0, range(EH, E))
+        round_w(LAST)
+        weigh(LAST, *PIECES[LAST][0])
+        weigh(LAST, *PIECES[LAST][1])
+        quantise_w(LAST)
+        quantise_x("x", LAST, *PIECES[LAST][0])
+        multiply(LAST, range(2))
+        weigh(LAST, *PIECES[LAST][2])
+        quantise_x("x2", LAST, *PIECES[LAST][1])
+        bias_on_vector(0, 2)
+        quantise_x("x2", LAST, *PIECES[LAST][2])
+        multiply(LAST, range(2, EH))
+        for i in range(3):
+            bias_on_scalar(1, i)
+        bias_on_scalar(0, 3)
+        bias_on_vector(1, 3)
 
-        sums = [placed("sums%d" % t, [TOP + 1, T], F32, AT_SECOND + t * 10 * KB) for t in range(NT)]
+        sums = [placed("sums%d" % t, [TOP + 1, T], F32, AT_RAW + t * 10 * KB) for t in range(NT)]
 
         def picked(t, r):
             return y[t][:].indirect(token_slots[r][:])
 
-        nc.scalar.activation(sums[0][:, 0, :], picked(0, 0), COPY)
-        add_bias(1, range(EH, E))
-        nc.vector.tensor_copy(sums[0][:, 1, :], picked(0, 1))
         for r in range(2):
-            nc.vector.tensor_tensor(sums[0][:, r + 2, :], picked(0, r + 2), sums[0][:, 1 - r, :], ADD)
-        for r in range(3):
-            nc.scalar.activation(sums[1][:, r, :], picked(1, r), COPY)
-        nc.vector.tensor_tensor(sums[1][:, 3, :], picked(1, 3), sums[1][:, 0, :], ADD)
-        nc.vector.tensor_tensor(sums[0][:, 4, :], sums[0][:, 2, :], sums[0][:, 3, :], ADD)
-        nc.sync.dma_start(out=out[0:P, :], in_=sums[0][:, 4, :])
-        nc.vector.tensor_tensor(sums[1][:, 4, :], sums[1][:, 3, :], sums[1][:, 1, :], ADD)
-        nc.vector.tensor_tensor(sums[1][:, 0, :], sums[1][:, 4, :], sums[1][:, 2, :], ADD)
-        nc.sync.dma_start(out=out[P : 2 * P, :], in_=sums[1][:, 0, :])
+            for t in range(NT):
+                nc.scalar.activation(sums[t][:, r, :], picked(t, r), COPY)
+        for r in range(2, TOP):
+            for t in range(NT):
+                nc.vector.tensor_tensor(sums[t][:, r, :], picked(t, r), sums[t][:, (0, 2)[r - 2], :], ADD)
+        for t in range(NT):
+            nc.vector.tensor_tensor(sums[t][:, 4, :], sums[t][:, 3, :], sums[t][:, 1, :], ADD)
+            nc.sync.dma_start(out=out[t * P : (t + 1) * P, :], in_=sums[t][:, 4, :])

@@ -35,7 +35,7 @@ STEPS = [(h, g) for h in range(HALVES) for g in range(PASSES)]
 LAST = len(STEPS) - 1
 BANK = 512
 KB = 1024
-PAD = 32
+SHARE = 416
 
 AT_WINDOWS = 0
 AT_STAGE = AT_WINDOWS + PASSES * PACK * 4 * WINDOW
@@ -46,7 +46,7 @@ AT_BF = AT_RAW + RAWS * 8 * KB
 PIECES = {s: ((0, SH),) for s in range(LAST - 1)}
 PIECES[LAST - 1] = ((0, BANK), (BANK, SH))
 PIECES[LAST] = ((0, BANK), (BANK, SH - C), (SH - C, SH))
-SHARED_STEPS = range(1, LAST - 1)
+SHARED_STEPS = range(1, PASSES + 1)
 
 
 def tile_moe_pre_lin_bias_kernel(tc, xT, w, b, gate, offs, pos1, pos2, pos3, pos4, out):
@@ -92,17 +92,22 @@ def tile_moe_pre_lin_bias_kernel(tc, xT, w, b, gate, offs, pos1, pos2, pos3, pos
             nc.sync.dma_start(out=w_raw[s, i][:], in_=w_rows[g, :, h * EH + 2 * i : h * EH + 2 * i + 2, :])
 
         def round_w(s):
-            first = s % 2 * PAD
-            w_bf[s] = placed("w_bf%d" % s, [SH * PACK + PAD], BF16, AT_BF + s % 2 * 8 * KB)[:, first : first + SH * PACK]
-            for q in range(EH):
+            w_bf[s] = placed("w_bf%d" % s, [EH, N * PACK], BF16, AT_BF)
+            for i, count in ((0, 2), (1, 1)):
                 nc.gpsimd.tensor_scalar(
-                    w_bf[s][:, q * N * PACK : (q + 1) * N * PACK].rearrange("p (n j) -> p n j", j=PACK),
-                    w_raw[s, q // 2][:, q % 2, :].rearrange("p (j n) -> p n j", j=PACK),
+                    w_bf[s][:, 2 * i : 2 * i + count, :].rearrange("p q (n j) -> p q n j", j=PACK),
+                    w_raw[s, i][:, 0:count, :].rearrange("p q (j n) -> p q n j", j=PACK),
                     1.0,
                     0.0,
                     MULT,
                     ADD,
                 )
+
+        def round_last_expert(s):
+            nc.vector.tensor_copy(
+                out=w_bf[s][:, EH - 1, :].rearrange("p (c i j) -> p c j i", i=RUN, j=PACK),
+                in_=w_raw[s, 1][:, 1, :].rearrange("p (j c i) -> p c j i", j=PACK, i=RUN),
+            )
 
         def quantise(name, values, words):
             codes = ring.tile([P, words], U32, name=name + "_codes", align_bytes=64)
@@ -111,7 +116,7 @@ def tile_moe_pre_lin_bias_kernel(tc, xT, w, b, gate, offs, pos1, pos2, pos3, pos
             return codes, scales
 
         def quantise_w(s):
-            codes, scales = quantise("w", w_bf[s], SH)
+            codes, scales = quantise("w", w_bf[s][:].rearrange("p q n -> p (q n)"), SH)
             for n in range(EH * NT):
                 w_mx[s, n // NT, n % NT] = (codes[:, n * P : (n + 1) * P], scales[:, n * P : (n + 1) * P])
 
@@ -139,7 +144,7 @@ def tile_moe_pre_lin_bias_kernel(tc, xT, w, b, gate, offs, pos1, pos2, pos3, pos
         def weigh(s, lo, hi):
             h, g = STEPS[s]
             if s not in x_bf:
-                x_bf[s] = placed("x_bf%d" % s, [SH * PACK], BF16, AT_BF + (s + 1) % 2 * (8 * KB + 2 * PAD))
+                x_bf[s] = placed("x_bf%d" % s, [SH * PACK], BF16, AT_BF + 8 * KB)
             weights = gates[(h * SH + lo) // BANK][:, lo % BANK : lo % BANK + hi - lo]
             nc.vector.tensor_tensor(
                 x_bf[s][:, lo * PACK : hi * PACK].rearrange("p (c i j) -> p c j i", i=RUN, j=PACK),
@@ -211,35 +216,36 @@ def tile_moe_pre_lin_bias_kernel(tc, xT, w, b, gate, offs, pos1, pos2, pos3, pos
             shared = s + 1 in SHARED_STEPS
             for lo, hi in PIECES[s + 1]:
                 for j in range(PACK):
-                    gather(s + 1, j, BANK if shared and j == PACK - 1 else lo, hi, nc.scalar)
+                    gather(s + 1, j, SHARE if shared and j == PACK - 1 else lo, hi, nc.scalar)
             round_w(s)
             if s + 3 <= LAST:
                 for i in range(2):
                     load_w(s + 3, i)
             for lo in range(0, SH, BANK):
                 weigh(s, lo, lo + BANK)
-            if shared:
-                gather(s + 1, PACK - 1, 0, BANK, nc.vector)
             if s == PASSES:
                 for i in range(2):
                     bias_on_vector(0, i)
-            quantise_w(s)
+            if shared:
+                gather(s + 1, PACK - 1, 0, SHARE, nc.vector)
+            round_last_expert(s)
             quantise_x("x", s, 0, SH)
+            quantise_w(s)
             multiply(s, range(EH))
 
         round_w(LAST)
-        weigh(LAST, *PIECES[LAST][0])
-        weigh(LAST, *PIECES[LAST][1])
+        for lo, hi in PIECES[LAST]:
+            weigh(LAST, lo, hi)
+        round_last_expert(LAST)
+        quantise_x("x", LAST, 0, BANK)
         quantise_w(LAST)
-        quantise_x("x", LAST, *PIECES[LAST][0])
         multiply(LAST, range(2))
-        weigh(LAST, *PIECES[LAST][2])
-        quantise_x("x2", LAST, *PIECES[LAST][1])
-        bias_on_vector(0, 2)
-        quantise_x("x2", LAST, *PIECES[LAST][2])
+        quantise_x("x", LAST, BANK, SH)
         multiply(LAST, range(2, EH))
-        for i in range(3):
+        for i in range(2):
             bias_on_scalar(1, i)
+        bias_on_scalar(0, 2)
+        bias_on_vector(1, 2)
         bias_on_scalar(0, 3)
         bias_on_vector(1, 3)
 

@@ -36,12 +36,13 @@ LAST = len(STEPS) - 1
 BANK = 512
 KB = 1024
 SHARE = 416
+POOL_COLUMNS = 176
 
 AT_WINDOWS = 0
 AT_STAGE = AT_WINDOWS + PASSES * PACK * 4 * WINDOW
 AT_RAW = AT_STAGE + 2 * 16 * KB
-RAWS = 6
-AT_BF = AT_RAW + RAWS * 8 * KB
+RAWS = 3
+AT_BF = AT_RAW + RAWS * 16 * KB
 
 PIECES = {s: ((0, SH),) for s in range(LAST - 1)}
 PIECES[LAST - 1] = ((0, BANK), (BANK, SH))
@@ -81,32 +82,31 @@ def tile_moe_pre_lin_bias_kernel(tc, xT, w, b, gate, offs, pos1, pos2, pos3, pos
         acc = {key: bank("acc%d_%d" % key, n) for key, n in acc_bank.items()}
         gates = [bank("gates%d" % n, 4 + n) for n in range(S // BANK)]
 
-        w_raw, w_bf, w_mx, stage, x_bf, x_mx = {}, {}, {}, {}, {}, {}
+        w_raw, w_mx, stage, x_bf, x_mx = {}, {}, {}, {}, {}
 
         def load_x(g, j, queue=nc.sync):
             queue.dma_start(out=windows[g, j][:, 0:T], in_=x_rows[g, j])
 
         def load_w(s, i):
             h, g = STEPS[s]
-            w_raw[s, i] = placed("w_raw%d_%d" % (s, i), [2, PACK * N], F32, AT_RAW + (2 * s + i) % RAWS * 8 * KB)
-            nc.sync.dma_start(out=w_raw[s, i][:], in_=w_rows[g, :, h * EH + 2 * i : h * EH + 2 * i + 2, :])
+            if i == 0:
+                w_raw[s] = placed("w_raw%d" % s, [EH, PACK * N], F32, AT_RAW + s % RAWS * 16 * KB)
+            nc.sync.dma_start(out=w_raw[s][:, 2 * i : 2 * i + 2, :], in_=w_rows[g, :, h * EH + 2 * i : h * EH + 2 * i + 2, :])
 
-        def round_w(s):
-            w_bf[s] = placed("w_bf%d" % s, [EH, N * PACK], BF16, AT_BF)
-            for i, count in ((0, 2), (1, 1)):
-                nc.gpsimd.tensor_scalar(
-                    w_bf[s][:, 2 * i : 2 * i + count, :].rearrange("p q (n j) -> p q n j", j=PACK),
-                    w_raw[s, i][:, 0:count, :].rearrange("p q (j n) -> p q n j", j=PACK),
-                    1.0,
-                    0.0,
-                    MULT,
-                    ADD,
-                )
+        def round_on_gpsimd(dst, s, lo, hi):
+            nc.gpsimd.tensor_scalar(
+                dst.rearrange("p q (n j) -> p q n j", j=PACK),
+                w_raw[s][:].rearrange("p q (j n) -> p q n j", j=PACK)[:, :, lo:hi],
+                1.0,
+                0.0,
+                MULT,
+                ADD,
+            )
 
-        def round_last_expert(s):
+        def round_on_vector(dst, s, experts, lo, hi):
             nc.vector.tensor_copy(
-                out=w_bf[s][:, EH - 1, :].rearrange("p (c i j) -> p c j i", i=RUN, j=PACK),
-                in_=w_raw[s, 1][:, 1, :].rearrange("p (j c i) -> p c j i", j=PACK, i=RUN),
+                out=dst.rearrange("p q (c i j) -> p q c j i", i=RUN, j=PACK),
+                in_=w_raw[s][:, experts, :].rearrange("p q (j c i) -> p q c j i", j=PACK, i=RUN)[:, :, lo // RUN : hi // RUN],
             )
 
         def quantise(name, values, words):
@@ -115,10 +115,10 @@ def tile_moe_pre_lin_bias_kernel(tc, xT, w, b, gate, offs, pos1, pos2, pos3, pos
             nc.vector.quantize_mx(out=codes[:].bitcast(FP8X4), scales=scales[:], in_=values)
             return codes, scales
 
-        def quantise_w(s):
-            codes, scales = quantise("w", w_bf[s][:].rearrange("p q n -> p (q n)"), SH)
-            for n in range(EH * NT):
-                w_mx[s, n // NT, n % NT] = (codes[:, n * P : (n + 1) * P], scales[:, n * P : (n + 1) * P])
+        def quantise_w(name, values, members):
+            codes, scales = quantise(name, values.rearrange("p q n -> p (q n)"), len(members) * P)
+            for n, member in enumerate(members):
+                w_mx[member] = (codes[:, n * P : (n + 1) * P], scales[:, n * P : (n + 1) * P])
 
         def quantise_x(name, s, lo, hi):
             codes, scales = quantise(name, x_bf[s][:, lo * PACK : hi * PACK], hi - lo)
@@ -153,9 +153,9 @@ def tile_moe_pre_lin_bias_kernel(tc, xT, w, b, gate, offs, pos1, pos2, pos3, pos
                 MULT,
             )
 
-        def multiply(s, experts):
+        def multiply(s, experts, tiles):
             h, g = STEPS[s]
-            for t in range(NT):
+            for t in tiles:
                 for q in experts:
                     e = h * EH + q
                     nc.tensor.matmul_mx(
@@ -217,7 +217,8 @@ def tile_moe_pre_lin_bias_kernel(tc, xT, w, b, gate, offs, pos1, pos2, pos3, pos
             for lo, hi in PIECES[s + 1]:
                 for j in range(PACK):
                     gather(s + 1, j, SHARE if shared and j == PACK - 1 else lo, hi, nc.scalar)
-            round_w(s)
+            w_bf = placed("w_bf%d" % s, [EH, N * PACK], BF16, AT_BF)
+            round_on_gpsimd(w_bf[:, :, 0 : POOL_COLUMNS * PACK], s, 0, POOL_COLUMNS)
             if s + 3 <= LAST:
                 for i in range(2):
                     load_w(s + 3, i)
@@ -228,38 +229,51 @@ def tile_moe_pre_lin_bias_kernel(tc, xT, w, b, gate, offs, pos1, pos2, pos3, pos
                     bias_on_vector(0, i)
             if shared:
                 gather(s + 1, PACK - 1, 0, SHARE, nc.vector)
-            round_last_expert(s)
+            round_on_vector(w_bf[:, :, POOL_COLUMNS * PACK :], s, slice(0, EH), POOL_COLUMNS, N)
             quantise_x("x", s, 0, SH)
-            quantise_w(s)
-            multiply(s, range(EH))
+            quantise_w("w", w_bf[:], [(s, q, t) for q in range(EH) for t in range(NT)])
+            multiply(s, range(EH), range(NT))
 
-        round_w(LAST)
-        for lo, hi in PIECES[LAST]:
-            weigh(LAST, lo, hi)
-        round_last_expert(LAST)
-        quantise_x("x", LAST, 0, BANK)
-        quantise_w(LAST)
-        multiply(LAST, range(2))
-        quantise_x("x", LAST, BANK, SH)
-        multiply(LAST, range(2, EH))
+        w_last = [placed("w_last%d" % t, [EH, P * PACK], BF16, AT_BF + t * 4 * KB) for t in range(NT)]
+        round_on_gpsimd(w_last[0][:], LAST, 0, P)
+        weigh(LAST, *PIECES[LAST][0])
+        weigh(LAST, *PIECES[LAST][1])
+        quantise_x("x", LAST, *PIECES[LAST][0])
+        quantise_w("w", w_last[0][:], [(LAST, q, 0) for q in range(EH)])
+        quantise_x("x2", LAST, *PIECES[LAST][1])
+        multiply(LAST, range(EH - 1), (0,))
+        weigh(LAST, *PIECES[LAST][2])
+        pairs = (slice(0, 2), slice(2, EH))
+        round_on_vector(w_last[1][:, pairs[0], :], LAST, pairs[0], P, N)
+        quantise_x("x2", LAST, *PIECES[LAST][2])
+        multiply(LAST, (EH - 1,), (0,))
+        round_on_vector(w_last[1][:, pairs[1], :], LAST, pairs[1], P, N)
         for i in range(2):
-            bias_on_scalar(1, i)
-        bias_on_scalar(0, 2)
-        bias_on_vector(1, 2)
-        bias_on_scalar(0, 3)
-        bias_on_vector(1, 3)
+            quantise_w("held", w_last[1][:, pairs[i], :], [(LAST, 2 * i + q, 1) for q in range(2)])
+            multiply(LAST, (2 * i, 2 * i + 1), (1,))
+        for t, i in ((1, 0), (1, 1), (0, 2), (0, 3)):
+            bias_on_scalar(t, i)
+        for i in range(2, EH):
+            bias_on_vector(1, i)
 
-        sums = [placed("sums%d" % t, [TOP + 1, T], F32, AT_RAW + t * 10 * KB) for t in range(NT)]
+        sums = [placed("sums%d" % t, [TOP + 1, T], F32, AT_STAGE + t * 10 * KB) for t in range(NT)]
+        halves = (slice(0, T // 2), slice(T // 2, T))
 
-        def picked(t, r):
-            return y[t][:].indirect(token_slots[r][:])
+        def picked(t, r, tokens=slice(0, T)):
+            return y[t][:].indirect(token_slots[r][:, tokens.start // LIST : tokens.stop // LIST])
 
-        for r in range(2):
-            for t in range(NT):
-                nc.scalar.activation(sums[t][:, r, :], picked(t, r), COPY)
-        for r in range(2, TOP):
-            for t in range(NT):
-                nc.vector.tensor_tensor(sums[t][:, r, :], picked(t, r), sums[t][:, (0, 2)[r - 2], :], ADD)
         for t in range(NT):
-            nc.vector.tensor_tensor(sums[t][:, 4, :], sums[t][:, 3, :], sums[t][:, 1, :], ADD)
-            nc.sync.dma_start(out=out[t * P : (t + 1) * P, :], in_=sums[t][:, 4, :])
+            for r in range(2):
+                nc.scalar.activation(sums[t][:, r, :], picked(t, r), COPY)
+        for tokens in halves:
+            nc.scalar.activation(sums[1][:, 2, tokens], picked(1, 2, tokens), COPY)
+        for r in range(2):
+            nc.vector.tensor_tensor(sums[0][:, 2 + r, :], picked(0, 2 + r), sums[0][:, r, :], ADD)
+        nc.vector.tensor_tensor(sums[1][:, 3, :], picked(1, 3), sums[1][:, 0, :], ADD)
+        nc.vector.tensor_tensor(sums[0][:, 4, :], sums[0][:, 2, :], sums[0][:, 3, :], ADD)
+        nc.sync.dma_start(out=out[0:P, :], in_=sums[0][:, 4, :])
+        for tokens in halves:
+            nc.vector.tensor_tensor(sums[1][:, 4, tokens], sums[1][:, 3, tokens], sums[1][:, 1, tokens], ADD)
+        for tokens, queue in zip(halves, (nc.sync, nc.scalar)):
+            nc.vector.tensor_tensor(sums[1][:, 0, tokens], sums[1][:, 4, tokens], sums[1][:, 2, tokens], ADD)
+            queue.dma_start(out=out[P : 2 * P, tokens], in_=sums[1][:, 0, tokens])

@@ -34,9 +34,11 @@ RUN = 4
 STEPS = [(h, g) for h in range(HALVES) for g in range(PASSES)]
 LAST = len(STEPS) - 1
 BANK = 512
+QUAD = 32
 KB = 1024
 SHARE = 416
 POOL_COLUMNS = 176
+POOL_COLUMNS_WIDE = 232
 
 AT_WINDOWS = 0
 AT_STAGE = AT_WINDOWS + PASSES * PACK * 4 * WINDOW
@@ -72,8 +74,8 @@ def tile_moe_pre_lin_bias_kernel(tc, xT, w, b, gate, offs, pos1, pos2, pos3, pos
 
         slot_tokens = keep.tile([P, S // LIST], U16, name="slot_tokens")
         token_slots = [keep.tile([P, T // LIST], U16, name="token_slots%d" % r) for r in range(TOP)]
-        gate_rows = keep.tile([P, P], F32, name="gate_rows")
-        gate_cols = keep.tile([P, S // P], F32, name="gate_cols")
+        gate_rows = keep.tile([P, QUAD], F32, name="gate_rows", align_bytes=64)
+        gate_cols = keep.tile([P, QUAD], F32, name="gate_cols", align_bytes=64)
         identity = keep.tile([P, P], F32, name="identity")
         bias = keep.tile([P, NT, E], F32, name="bias")
         windows = {(g, j): placed("window%d_%d" % (g, j), [WINDOW], F32, window_at(g, j)) for g in range(PASSES) for j in range(PACK)}
@@ -93,10 +95,10 @@ def tile_moe_pre_lin_bias_kernel(tc, xT, w, b, gate, offs, pos1, pos2, pos3, pos
                 w_raw[s] = placed("w_raw%d" % s, [EH, PACK * N], F32, AT_RAW + s % RAWS * 16 * KB)
             nc.sync.dma_start(out=w_raw[s][:, 2 * i : 2 * i + 2, :], in_=w_rows[g, :, h * EH + 2 * i : h * EH + 2 * i + 2, :])
 
-        def round_on_gpsimd(dst, s, lo, hi):
+        def round_on_gpsimd(dst, s, experts, lo, hi):
             nc.gpsimd.tensor_scalar(
                 dst.rearrange("p q (n j) -> p q n j", j=PACK),
-                w_raw[s][:].rearrange("p q (j n) -> p q n j", j=PACK)[:, :, lo:hi],
+                w_raw[s][:, experts, :].rearrange("p q (j n) -> p q n j", j=PACK)[:, :, lo:hi],
                 1.0,
                 0.0,
                 MULT,
@@ -185,40 +187,47 @@ def tile_moe_pre_lin_bias_kernel(tc, xT, w, b, gate, offs, pos1, pos2, pos3, pos
                 ADD,
             )
 
+        warm = keep.tile([P, 1], F32, name="warm")
+        cold = keep.tile([P, 1], F32, name="cold")
+        nc.gpsimd.memset(cold[:], 0.0)
+        nc.scalar.activation(warm[:], cold[:], COPY)
         nc.sync.dma_start(slot_tokens[:], offs)
-        load_x(0, 0, nc.scalar)
-        load_x(0, 1)
-        nc.sync.dma_start(out=gate_rows[:], in_=gate[0 : P * P // S, :].rearrange("r (q p) -> (r q) p", p=P))
+        for j in range(2):
+            load_x(0, j, nc.scalar)
+        gate_blocks = gate[0 : QUAD * P // S, :].rearrange("u (q a r) -> a (u q) r", a=P // QUAD, r=QUAD)
+        for a in range(P // QUAD):
+            nc.sync.dma_start(out=gate_rows[a * QUAD : (a + 1) * QUAD, :], in_=gate_blocks[a])
         for j in range(2, PACK):
             load_x(0, j)
         for g in range(PASSES - 1):
             for i in range(2):
+                load_x(g + 1, i)
                 load_w(g, i)
-                load_x(g + 1, 2 * i)
-                load_x(g + 1, 2 * i + 1)
+            for j in range(2, PACK):
+                load_x(g + 1, j)
         nc.sync.dma_start(out=bias[:], in_=b.rearrange("(t p) e -> p t e", p=P))
         for r, pos in enumerate((pos1, pos2, pos3, pos4)):
             nc.sync.dma_start(token_slots[r][:], pos)
 
         make_identity(nc, identity[:])
-        turned = bank("turned", 7)
-        nc.tensor.transpose(turned[:, 0:P], gate_rows[:], identity[:])
+        nc.vector.transpose(gate_cols[:], gate_rows[:])
         for j in range(PACK):
             gather(0, j, 0, SH, nc.vector if j % 2 else nc.scalar)
-            if j == 1:
-                nc.vector.tensor_copy(gate_cols[:], turned[:, 0 : S // P])
         for q in range(S // P):
             nc.tensor.transpose(
                 gates[q * P // BANK][:, q * P % BANK : q * P % BANK + P], gate_cols[:, q : q + 1].to_broadcast([P, P]), identity[:]
             )
 
+        pairs = (slice(0, 2), slice(2, EH))
         for s in range(LAST):
             shared = s + 1 in SHARED_STEPS
             for lo, hi in PIECES[s + 1]:
                 for j in range(PACK):
                     gather(s + 1, j, SHARE if shared and j == PACK - 1 else lo, hi, nc.scalar)
             w_bf = placed("w_bf%d" % s, [EH, N * PACK], BF16, AT_BF)
-            round_on_gpsimd(w_bf[:, :, 0 : POOL_COLUMNS * PACK], s, 0, POOL_COLUMNS)
+            split = POOL_COLUMNS_WIDE if s == PASSES else POOL_COLUMNS
+            for experts in pairs if s == 0 else (slice(0, EH),):
+                round_on_gpsimd(w_bf[:, experts, 0 : split * PACK], s, experts, 0, split)
             if s + 3 <= LAST:
                 for i in range(2):
                     load_w(s + 3, i)
@@ -229,13 +238,13 @@ def tile_moe_pre_lin_bias_kernel(tc, xT, w, b, gate, offs, pos1, pos2, pos3, pos
                     bias_on_vector(0, i)
             if shared:
                 gather(s + 1, PACK - 1, 0, SHARE, nc.vector)
-            round_on_vector(w_bf[:, :, POOL_COLUMNS * PACK :], s, slice(0, EH), POOL_COLUMNS, N)
+            round_on_vector(w_bf[:, :, split * PACK :], s, slice(0, EH), split, N)
             quantise_x("x", s, 0, SH)
             quantise_w("w", w_bf[:], [(s, q, t) for q in range(EH) for t in range(NT)])
             multiply(s, range(EH), range(NT))
 
         w_last = [placed("w_last%d" % t, [EH, P * PACK], BF16, AT_BF + t * 4 * KB) for t in range(NT)]
-        round_on_gpsimd(w_last[0][:], LAST, 0, P)
+        round_on_gpsimd(w_last[0][:], LAST, slice(0, EH), 0, P)
         weigh(LAST, *PIECES[LAST][0])
         weigh(LAST, *PIECES[LAST][1])
         quantise_x("x", LAST, *PIECES[LAST][0])
@@ -243,7 +252,6 @@ def tile_moe_pre_lin_bias_kernel(tc, xT, w, b, gate, offs, pos1, pos2, pos3, pos
         quantise_x("x2", LAST, *PIECES[LAST][1])
         multiply(LAST, range(EH - 1), (0,))
         weigh(LAST, *PIECES[LAST][2])
-        pairs = (slice(0, 2), slice(2, EH))
         round_on_vector(w_last[1][:, pairs[0], :], LAST, pairs[0], P, N)
         quantise_x("x2", LAST, *PIECES[LAST][2])
         multiply(LAST, (EH - 1,), (0,))

@@ -43,13 +43,13 @@ POOL_COLUMNS_WIDE = 232
 AT_WINDOWS = 0
 AT_STAGE = AT_WINDOWS + PASSES * PACK * 4 * WINDOW
 AT_RAW = AT_STAGE + 2 * 16 * KB
-RAWS = 3
+RAWS = 4
 AT_BF = AT_RAW + RAWS * 16 * KB
 
 PIECES = {s: ((0, SH),) for s in range(LAST - 1)}
 PIECES[LAST - 1] = ((0, BANK), (BANK, SH))
 PIECES[LAST] = ((0, BANK), (BANK, SH - C), (SH - C, SH))
-SHARED_STEPS = range(1, PASSES + 1)
+ON_VECTOR = {1: {0: SH, 1: 704}, 2: {PACK - 1: SHARE}, 3: {PACK - 1: SHARE}}
 
 
 def tile_moe_pre_lin_bias_kernel(tc, xT, w, b, gate, offs, pos1, pos2, pos3, pos4, out):
@@ -146,7 +146,7 @@ def tile_moe_pre_lin_bias_kernel(tc, xT, w, b, gate, offs, pos1, pos2, pos3, pos
         def weigh(s, lo, hi):
             h, g = STEPS[s]
             if s not in x_bf:
-                x_bf[s] = placed("x_bf%d" % s, [SH * PACK], BF16, AT_BF + 8 * KB)
+                x_bf[s] = placed("x_bf%d" % s, [SH * PACK], BF16, AT_RAW + (s - 1) % RAWS * 16 * KB)
             weights = gates[(h * SH + lo) // BANK][:, lo % BANK : lo % BANK + hi - lo]
             nc.vector.tensor_tensor(
                 x_bf[s][:, lo * PACK : hi * PACK].rearrange("p (c i j) -> p c j i", i=RUN, j=PACK),
@@ -197,13 +197,16 @@ def tile_moe_pre_lin_bias_kernel(tc, xT, w, b, gate, offs, pos1, pos2, pos3, pos
         gate_blocks = gate[0 : QUAD * P // S, :].rearrange("u (q a r) -> a (u q) r", a=P // QUAD, r=QUAD)
         for a in range(P // QUAD):
             nc.sync.dma_start(out=gate_rows[a * QUAD : (a + 1) * QUAD, :], in_=gate_blocks[a])
-        for j in range(2, PACK):
-            load_x(0, j)
-        for g in range(PASSES - 1):
-            for i in range(2):
-                load_x(g + 1, i)
-                load_w(g, i)
-            for j in range(2, PACK):
+        for g, j in ((0, 2), (1, 0), (0, 3), (1, 1), (1, 2)):
+            load_x(g, j)
+        for i in range(2):
+            load_w(0, i)
+        load_x(1, PACK - 1)
+        for g in range(1, PASSES - 1):
+            load_w(g, 0)
+            load_x(g + 1, 0)
+            load_w(g, 1)
+            for j in range(1, PACK):
                 load_x(g + 1, j)
         nc.sync.dma_start(out=bias[:], in_=b.rearrange("(t p) e -> p t e", p=P))
         for r, pos in enumerate((pos1, pos2, pos3, pos4)):
@@ -212,7 +215,9 @@ def tile_moe_pre_lin_bias_kernel(tc, xT, w, b, gate, offs, pos1, pos2, pos3, pos
         make_identity(nc, identity[:])
         nc.vector.transpose(gate_cols[:], gate_rows[:])
         for j in range(PACK):
-            gather(0, j, 0, SH, nc.vector if j % 2 else nc.scalar)
+            gather(0, j, 0, SH, nc.vector if j == 1 else nc.scalar)
+        for j, hi in ON_VECTOR[1].items():
+            gather(1, j, 0, hi, nc.vector)
         for q in range(S // P):
             nc.tensor.transpose(
                 gates[q * P // BANK][:, q * P % BANK : q * P % BANK + P], gate_cols[:, q : q + 1].to_broadcast([P, P]), identity[:]
@@ -220,24 +225,26 @@ def tile_moe_pre_lin_bias_kernel(tc, xT, w, b, gate, offs, pos1, pos2, pos3, pos
 
         pairs = (slice(0, 2), slice(2, EH))
         for s in range(LAST):
-            shared = s + 1 in SHARED_STEPS
             for lo, hi in PIECES[s + 1]:
                 for j in range(PACK):
-                    gather(s + 1, j, SHARE if shared and j == PACK - 1 else lo, hi, nc.scalar)
+                    first = ON_VECTOR.get(s + 1, {}).get(j, lo)
+                    if first < hi:
+                        gather(s + 1, j, first, hi, nc.scalar)
+            for lo in range(0, SH, BANK):
+                weigh(s, lo, lo + BANK)
             w_bf = placed("w_bf%d" % s, [EH, N * PACK], BF16, AT_BF)
             split = POOL_COLUMNS_WIDE if s == PASSES else POOL_COLUMNS
-            for experts in pairs if s == 0 else (slice(0, EH),):
+            for experts in pairs if s < 2 else (slice(0, EH),):
                 round_on_gpsimd(w_bf[:, experts, 0 : split * PACK], s, experts, 0, split)
             if s + 3 <= LAST:
                 for i in range(2):
                     load_w(s + 3, i)
-            for lo in range(0, SH, BANK):
-                weigh(s, lo, lo + BANK)
             if s == PASSES:
                 for i in range(2):
                     bias_on_vector(0, i)
-            if shared:
-                gather(s + 1, PACK - 1, 0, SHARE, nc.vector)
+            if s > 0:
+                for j, hi in ON_VECTOR.get(s + 1, {}).items():
+                    gather(s + 1, j, 0, hi, nc.vector)
             round_on_vector(w_bf[:, :, split * PACK :], s, slice(0, EH), split, N)
             quantise_x("x", s, 0, SH)
             quantise_w("w", w_bf[:], [(s, q, t) for q in range(EH) for t in range(NT)])

@@ -37,7 +37,8 @@ BANK = 512
 QUAD = 32
 KB = 1024
 SHARE = 416
-POOL_COLUMNS = 176
+POOL_COLUMNS = 184
+POOL_COLUMNS_EARLY = 176
 POOL_COLUMNS_WIDE = 232
 
 AT_WINDOWS = 0
@@ -233,7 +234,7 @@ def tile_moe_pre_lin_bias_kernel(tc, xT, w, b, gate, offs, pos1, pos2, pos3, pos
             for lo in range(0, SH, BANK):
                 weigh(s, lo, lo + BANK)
             w_bf = placed("w_bf%d" % s, [EH, N * PACK], BF16, AT_BF)
-            split = POOL_COLUMNS_WIDE if s == PASSES else POOL_COLUMNS
+            split = POOL_COLUMNS_WIDE if s == PASSES else POOL_COLUMNS if s >= 2 else POOL_COLUMNS_EARLY
             for experts in pairs if s < 2 else (slice(0, EH),):
                 round_on_gpsimd(w_bf[:, experts, 0 : split * PACK], s, experts, 0, split)
             if s + 3 <= LAST:

@@ -25,38 +25,37 @@ P = 128
 PACK = 4
 PASSES = K // (P * PACK)
 NT = N // P
-HALVES = 2
-EH = E // HALVES
-SH = S // HALVES
+EH = E // 2
+SH = S // 2
 LIST = 16
 WINDOW = SH + LIST
 RUN = 4
-STEPS = [(h, g) for h in range(HALVES) for g in range(PASSES)]
+PAIR = 2
+STEPS = ((0, 0), (1, 0), (0, 1), (1, 1), (0, 2), (0, 3), (1, 2), (1, 3))
 LAST = len(STEPS) - 1
+DEFERRED = (1, 3)
+FIRST_HALF_DONE = 5
 BANK = 512
 QUAD = 32
 KB = 1024
-SHARE = 416
-POOL_COLUMNS = 184
-POOL_COLUMNS_EARLY = 176
-POOL_COLUMNS_WIDE = 232
+SHARES = {0: 192, 2: 512, 3: 512, 4: 416, 5: 416, 6: 128}
+
 
 AT_WINDOWS = 0
-AT_STAGE = AT_WINDOWS + PASSES * PACK * 4 * WINDOW
-AT_RAW = AT_STAGE + 2 * 16 * KB
-RAWS = 4
-AT_BF = AT_RAW + RAWS * 16 * KB
+PITCH = 17 * 256
+AT_EARLY = (AT_WINDOWS + (2 * PACK + 1) * PITCH, AT_WINDOWS + (3 * PACK + 1) * PITCH)
+AT_SLOTS = AT_EARLY[1] + 16 * KB
+SLOT_KB = (24, 24, 24, 16, 16, 24)
 
 PIECES = {s: ((0, SH),) for s in range(LAST - 1)}
 PIECES[LAST - 1] = ((0, BANK), (BANK, SH))
 PIECES[LAST] = ((0, BANK), (BANK, SH - C), (SH - C, SH))
-ON_VECTOR = {1: {0: SH, 1: 704}, 2: {PACK - 1: SHARE}, 3: {PACK - 1: SHARE}}
 
 
 def tile_moe_pre_lin_bias_kernel(tc, xT, w, b, gate, offs, pos1, pos2, pos3, pos4, out):
     nc = tc.nc
     x_rows = xT.rearrange("(g p j) t -> g j p t", p=P, j=PACK)
-    w_rows = w.rearrange("e (g p j) n -> g p e (j n)", p=P, j=PACK)
+    w_rows = w.rearrange("e (g p j) n -> g e p j n", p=P, j=PACK)
 
     with ExitStack() as ctx:
         keep = ctx.enter_context(tc.tile_pool(name="keep", bufs=1))
@@ -65,74 +64,81 @@ def tile_moe_pre_lin_bias_kernel(tc, xT, w, b, gate, offs, pos1, pos2, pos3, pos
         psum = ctx.enter_context(tc.psum_pool(name="psum", bufs=1))
 
         def placed(name, shape, dtype, at):
-            return arena.tile([P] + shape, dtype, name=name, offset=at, align_bytes=64)
+            return arena.tile([P] + shape, dtype, name=name, offset=at, align_bytes=256)
 
         def bank(name, n):
             return psum.tile([P, BANK], F32, name=name, offset=n * 4 * BANK)
 
         def window_at(g, j):
-            return AT_WINDOWS + (g * PACK + j) * 4 * WINDOW
+            return AT_WINDOWS + (g * PACK + j) * PITCH
+
+        def raw_at(s):
+            return AT_SLOTS + sum(SLOT_KB[: s % len(SLOT_KB)]) * KB
 
         slot_tokens = keep.tile([P, S // LIST], U16, name="slot_tokens")
         token_slots = [keep.tile([P, T // LIST], U16, name="token_slots%d" % r) for r in range(TOP)]
         gate_rows = keep.tile([P, QUAD], F32, name="gate_rows", align_bytes=64)
-        gate_cols = keep.tile([P, QUAD], F32, name="gate_cols", align_bytes=64)
+        gate_cols = placed("gate_cols", [QUAD], F32, raw_at(2 - 3) + 8 * KB)
         identity = keep.tile([P, P], F32, name="identity")
         bias = keep.tile([P, NT, E], F32, name="bias")
         windows = {(g, j): placed("window%d_%d" % (g, j), [WINDOW], F32, window_at(g, j)) for g in range(PASSES) for j in range(PACK)}
-        y = [keep.tile([P, S], F32, name="y0"), placed("y1", [S], F32, window_at(PASSES - 1, 0))]
+        y = [placed("y0", [S], F32, raw_at(FIRST_HALF_DONE) + 8 * KB), placed("y1", [S], F32, window_at(PASSES - 1, 0))]
         acc_bank = {(0, 0): 0, (0, 1): 1, (1, 0): 2, (1, 1): 3, (0, 2): 4, (0, 3): 5, (1, 2): 0, (1, 3): 1}
         acc = {key: bank("acc%d_%d" % key, n) for key, n in acc_bank.items()}
         gates = [bank("gates%d" % n, 4 + n) for n in range(S // BANK)]
 
-        w_raw, w_mx, stage, x_bf, x_mx = {}, {}, {}, {}, {}
+        w_raw, w_mx, stage, x_bf, x_mx, x_codes = {}, {}, {}, {}, {}, {}
 
         def load_x(g, j, queue=nc.sync):
             queue.dma_start(out=windows[g, j][:, 0:T], in_=x_rows[g, j])
 
-        def load_w(s, i):
+        def load_w(s, experts=range(EH)):
             h, g = STEPS[s]
-            if i == 0:
-                w_raw[s] = placed("w_raw%d" % s, [EH, PACK * N], F32, AT_RAW + s % RAWS * 16 * KB)
-            nc.sync.dma_start(out=w_raw[s][:, 2 * i : 2 * i + 2, :], in_=w_rows[g, :, h * EH + 2 * i : h * EH + 2 * i + 2, :])
+            if s not in w_raw:
+                w_raw[s] = placed("w_raw%d" % s, [EH, PACK, N], F32, raw_at(s))
+            for q in experts:
+                nc.sync.dma_start(out=w_raw[s][:, q], in_=w_rows[g, h * EH + q])
 
-        def round_on_gpsimd(dst, s, experts, lo, hi):
-            nc.gpsimd.tensor_scalar(
-                dst.rearrange("p q (n j) -> p q n j", j=PACK),
-                w_raw[s][:, experts, :].rearrange("p q (j n) -> p q n j", j=PACK)[:, :, lo:hi],
-                1.0,
-                0.0,
-                MULT,
-                ADD,
+        def round_w(engine, dst, s, experts, columns):
+            run = RUN if engine is nc.vector else PAIR
+            engine.tensor_copy(
+                out=dst.rearrange("p q (c i j) -> p q c j i", i=run, j=PACK),
+                in_=w_raw[s][:, experts, :, columns].rearrange("p q j (c i) -> p q c j i", i=run),
             )
 
-        def round_on_vector(dst, s, experts, lo, hi):
-            nc.vector.tensor_copy(
-                out=dst.rearrange("p q (c i j) -> p q c j i", i=RUN, j=PACK),
-                in_=w_raw[s][:, experts, :].rearrange("p q (j c i) -> p q c j i", j=PACK, i=RUN)[:, :, lo // RUN : hi // RUN],
-            )
-
-        def quantise(name, values, words):
-            codes = ring.tile([P, words], U32, name=name + "_codes", align_bytes=64)
-            scales = ring.tile([P, words], U8, name=name + "_scales", align_bytes=64)
-            nc.vector.quantize_mx(out=codes[:].bitcast(FP8X4), scales=scales[:], in_=values)
+        def mx_tiles(name, s, words):
+            if s in DEFERRED:
+                at = window_at(STEPS[s][1], 0) + (0 if name == "x" else 5 * KB)
+                codes = placed("%s_codes%d" % (name, s), [words], U32, at)
+                scales = placed("%s_scales%d" % (name, s), [words], U8, at + 4 * KB)
+            else:
+                codes = ring.tile([P, words], U32, name=name + "_codes", align_bytes=64)
+                scales = ring.tile([P, words], U8, name=name + "_scales", align_bytes=64)
             return codes, scales
 
-        def quantise_w(name, values, members):
-            codes, scales = quantise(name, values.rearrange("p q n -> p (q n)"), len(members) * P)
+        def quantise_w(name, s, values, members):
+            codes, scales = mx_tiles(name, s, len(members) * P)
+            nc.vector.quantize_mx(out=codes[:].bitcast(FP8X4), scales=scales[:], in_=values)
             for n, member in enumerate(members):
                 w_mx[member] = (codes[:, n * P : (n + 1) * P], scales[:, n * P : (n + 1) * P])
 
-        def quantise_x(name, s, lo, hi):
-            codes, scales = quantise(name, x_bf[s][:, lo * PACK : hi * PACK], hi - lo)
+        def quantise_x(s, lo, hi):
+            if s not in x_codes:
+                x_codes[s] = mx_tiles("x", s, SH)
+            codes, scales = x_codes[s]
+            nc.vector.quantize_mx(out=codes[:, lo:hi].bitcast(FP8X4), scales=scales[:, lo:hi], in_=x_bf[s][:, lo * PACK : hi * PACK])
             for q in range(lo // C, hi // C):
-                cols = slice(q * C - lo, (q + 1) * C - lo)
-                x_mx[s, q] = (codes[:, cols], scales[:, cols])
+                x_mx[s, q] = (codes[:, q * C : (q + 1) * C], scales[:, q * C : (q + 1) * C])
 
         def staged(s, lo, hi):
             first, last = [piece for piece in PIECES[s] if piece[0] <= lo < piece[1]][0]
             if (s, first) not in stage:
-                at = AT_STAGE + s % 2 * 16 * KB + first * PACK * 4
+                if s < 2:
+                    at = AT_EARLY[s]
+                elif (s, first) == (LAST - 1, 0):
+                    at = raw_at(s - 2) + 8 * KB
+                else:
+                    at = raw_at(s - (3 if s < LAST - 1 else 5)) + 8 * KB + first * PACK * 4
                 stage[s, first] = placed("stage%d_%d" % (s, first), [PACK, last - first], F32, at)
             return stage[s, first][:, :, lo - first : hi - first]
 
@@ -147,12 +153,12 @@ def tile_moe_pre_lin_bias_kernel(tc, xT, w, b, gate, offs, pos1, pos2, pos3, pos
         def weigh(s, lo, hi):
             h, g = STEPS[s]
             if s not in x_bf:
-                x_bf[s] = placed("x_bf%d" % s, [SH * PACK], BF16, AT_RAW + (s - 1) % RAWS * 16 * KB)
+                x_bf[s] = placed("x_bf%d" % s, [SH * PACK], BF16, raw_at(s - 1))
             weights = gates[(h * SH + lo) // BANK][:, lo % BANK : lo % BANK + hi - lo]
             nc.vector.tensor_tensor(
-                x_bf[s][:, lo * PACK : hi * PACK].rearrange("p (c i j) -> p c j i", i=RUN, j=PACK),
-                staged(s, lo, hi).rearrange("p j (c i) -> p c j i", i=RUN),
-                weights.rearrange("p (c o i) -> p c o i", o=1, i=RUN).to_broadcast([P, (hi - lo) // RUN, PACK, RUN]),
+                x_bf[s][:, lo * PACK : hi * PACK].rearrange("p (c i j) -> p c j i", i=PAIR, j=PACK),
+                staged(s, lo, hi).rearrange("p j (c i) -> p c j i", i=PAIR),
+                weights.rearrange("p (c o i) -> p c o i", o=1, i=PAIR).to_broadcast([P, (hi - lo) // PAIR, PACK, PAIR]),
                 MULT,
             )
 
@@ -198,81 +204,106 @@ def tile_moe_pre_lin_bias_kernel(tc, xT, w, b, gate, offs, pos1, pos2, pos3, pos
         gate_blocks = gate[0 : QUAD * P // S, :].rearrange("u (q a r) -> a (u q) r", a=P // QUAD, r=QUAD)
         for a in range(P // QUAD):
             nc.sync.dma_start(out=gate_rows[a * QUAD : (a + 1) * QUAD, :], in_=gate_blocks[a])
-        for g, j in ((0, 2), (1, 0), (0, 3), (1, 1), (1, 2)):
-            load_x(g, j)
-        for i in range(2):
-            load_w(0, i)
-        load_x(1, PACK - 1)
-        for g in range(1, PASSES - 1):
-            load_w(g, 0)
-            load_x(g + 1, 0)
-            load_w(g, 1)
-            for j in range(1, PACK):
-                load_x(g + 1, j)
+        for j in range(2, PACK):
+            load_x(0, j)
+        load_w(0)
+        load_x(1, 0)
+        load_w(1, range(2))
+        load_x(1, 1)
+        load_w(1, range(2, EH))
+        for j in range(2, PACK):
+            load_x(1, j)
+        load_w(2)
+        load_x(2, 0)
+        load_w(3)
         nc.sync.dma_start(out=bias[:], in_=b.rearrange("(t p) e -> p t e", p=P))
         for r, pos in enumerate((pos1, pos2, pos3, pos4)):
             nc.sync.dma_start(token_slots[r][:], pos)
 
         make_identity(nc, identity[:])
         nc.vector.transpose(gate_cols[:], gate_rows[:])
-        for j in range(PACK):
-            gather(0, j, 0, SH, nc.vector if j == 1 else nc.scalar)
-        for j, hi in ON_VECTOR[1].items():
-            gather(1, j, 0, hi, nc.vector)
+        gather(0, 0, 0, SHARES[0], nc.vector)
+        for s, j in ((1, 0), (0, 1), (1, 1)):
+            gather(s, j, 0, SH, nc.vector)
+        for j in (0, 2, 3):
+            gather(0, j, SHARES[0] if j == 0 else 0, SH, nc.scalar)
         for q in range(S // P):
             nc.tensor.transpose(
                 gates[q * P // BANK][:, q * P % BANK : q * P % BANK + P], gate_cols[:, q : q + 1].to_broadcast([P, P]), identity[:]
             )
 
-        pairs = (slice(0, 2), slice(2, EH))
         for s in range(LAST):
             for lo, hi in PIECES[s + 1]:
-                for j in range(PACK):
-                    first = ON_VECTOR.get(s + 1, {}).get(j, lo)
-                    if first < hi:
-                        gather(s + 1, j, first, hi, nc.scalar)
-            for lo in range(0, SH, BANK):
-                weigh(s, lo, lo + BANK)
-            w_bf = placed("w_bf%d" % s, [EH, N * PACK], BF16, AT_BF)
-            split = POOL_COLUMNS_WIDE if s == PASSES else POOL_COLUMNS if s >= 2 else POOL_COLUMNS_EARLY
-            for experts in pairs if s < 2 else (slice(0, EH),):
-                round_on_gpsimd(w_bf[:, experts, 0 : split * PACK], s, experts, 0, split)
-            if s + 3 <= LAST:
-                for i in range(2):
-                    load_w(s + 3, i)
-            if s == PASSES:
+                first = 2 if s == 0 else 0
+                for j in range(first, PACK):
+                    gather(s + 1, j, SHARES.get(s + 1, 0) if j == first and lo == 0 else lo, hi, nc.scalar)
+            tiles = NT if s < LAST - 1 else 1
+            w_bf = placed("w_bf%d" % s, [EH, tiles * P * PACK], BF16, raw_at(s - 2))
+            round_w(nc.gpsimd, w_bf[:], s, slice(0, EH), slice(0, tiles * P))
+            if tiles < NT:
+                w_late = placed("w_late", [EH, P * PACK], BF16, raw_at(s - 2) + 4 * KB)
+                round_w(nc.gpsimd, w_late[:], s, slice(0, EH), slice(P, N))
+            weigh(s, 0, BANK)
+            if s == FIRST_HALF_DONE + 1:
                 for i in range(2):
                     bias_on_vector(0, i)
-            if s > 0:
-                for j, hi in ON_VECTOR.get(s + 1, {}).items():
-                    gather(s + 1, j, 0, hi, nc.vector)
-            round_on_vector(w_bf[:, :, split * PACK :], s, slice(0, EH), split, N)
-            quantise_x("x", s, 0, SH)
-            quantise_w("w", w_bf[:], [(s, q, t) for q in range(EH) for t in range(NT)])
-            multiply(s, range(EH), range(NT))
+            weigh(s, BANK, SH)
+            if s in (FIRST_HALF_DONE, FIRST_HALF_DONE + 1):
+                for early in DEFERRED:
+                    multiply(early, range(EH), (s - FIRST_HALF_DONE,))
+            ahead = s + 2 if s < FIRST_HALF_DONE - 1 else s + 1
+            if ahead in SHARES and s != FIRST_HALF_DONE - 1:
+                gather(ahead, 0, 0, SHARES[ahead], nc.vector)
+                quantise_x(s, 0, SH)
+            else:
+                for lo in range(0, SH, BANK):
+                    quantise_x(s, lo, lo + BANK)
+            quantise_w("w", s, w_bf[:].rearrange("p q n -> p (q n)"), [(s, q, t) for q in range(EH) for t in range(tiles)])
+            if s not in DEFERRED:
+                multiply(s, range(EH), range(tiles))
+            if s == 0:
+                for g, j in ((2, 1), (2, 2), (2, 3), (3, 0)):
+                    load_x(g, j)
+            if 0 < s <= LAST - 3:
+                load_w(s + 3)
+            if s == 1:
+                for j in range(1, PACK):
+                    load_x(3, j)
 
-        w_last = [placed("w_last%d" % t, [EH, P * PACK], BF16, AT_BF + t * 4 * KB) for t in range(NT)]
-        round_on_gpsimd(w_last[0][:], LAST, slice(0, EH), 0, P)
+        w_first = placed("w_first", [EH, P * PACK], BF16, raw_at(LAST - 2))
+        w_pairs = [placed("w_pair%d" % i, [2, P * PACK], BF16, raw_at(LAST - 3 + i)) for i in range(2)]
+
+        def round_second(engine, q):
+            round_w(engine, w_pairs[q // 2][:, q % 2 : q % 2 + 1, :], LAST, slice(q, q + 1), slice(P, N))
+
+        def second_tile(s, rounded, i):
+            quantise_w("held%d" % s, s, rounded.rearrange("p q n -> p (q n)"), [(s, 2 * i + q, 1) for q in range(2)])
+            multiply(s, (2 * i, 2 * i + 1), (1,))
+
+        round_w(nc.gpsimd, w_first[:], LAST, slice(0, EH), slice(0, P))
+        round_second(nc.gpsimd, 0)
         weigh(LAST, *PIECES[LAST][0])
         weigh(LAST, *PIECES[LAST][1])
-        quantise_x("x", LAST, *PIECES[LAST][0])
-        quantise_w("w", w_last[0][:], [(LAST, q, 0) for q in range(EH)])
-        quantise_x("x2", LAST, *PIECES[LAST][1])
+        quantise_x(LAST, *PIECES[LAST][0])
+        second_tile(LAST - 1, w_late[:, 0:2, :], 0)
+        quantise_w("w", LAST, w_first[:].rearrange("p q n -> p (q n)"), [(LAST, q, 0) for q in range(EH)])
+        quantise_x(LAST, *PIECES[LAST][1])
         multiply(LAST, range(EH - 1), (0,))
+        round_second(nc.gpsimd, 2)
         weigh(LAST, *PIECES[LAST][2])
-        round_on_vector(w_last[1][:, pairs[0], :], LAST, pairs[0], P, N)
-        quantise_x("x2", LAST, *PIECES[LAST][2])
+        round_second(nc.vector, 1)
+        quantise_x(LAST, *PIECES[LAST][2])
         multiply(LAST, (EH - 1,), (0,))
-        round_on_vector(w_last[1][:, pairs[1], :], LAST, pairs[1], P, N)
-        for i in range(2):
-            quantise_w("held", w_last[1][:, pairs[i], :], [(LAST, 2 * i + q, 1) for q in range(2)])
-            multiply(LAST, (2 * i, 2 * i + 1), (1,))
+        round_second(nc.vector, 3)
+        second_tile(LAST, w_pairs[0][:], 0)
+        second_tile(LAST - 1, w_late[:, 2:EH, :], 1)
+        second_tile(LAST, w_pairs[1][:], 1)
         for t, i in ((1, 0), (1, 1), (0, 2), (0, 3)):
             bias_on_scalar(t, i)
         for i in range(2, EH):
             bias_on_vector(1, i)
 
-        sums = [placed("sums%d" % t, [TOP + 1, T], F32, AT_STAGE + t * 10 * KB) for t in range(NT)]
+        sums = [placed("sums%d" % t, [TOP + 1, T], F32, raw_at(LAST - 1) + t * 10 * KB) for t in range(NT)]
         halves = (slice(0, T // 2), slice(T // 2, T))
 
         def picked(t, r, tokens=slice(0, T)):

from contextlib import ExitStack

import concourse.mybir as mybir
from concourse.masks import make_identity

K, T, E, C, N = 2048, 512, 8, 256, 256
TOP = 4
S = E * C

FLOPS = 2 * K * N * S
BYTES = 4 * (K * T + E * K * N + N * E + S + N * T) + 2 * 128 * (S + TOP * T) // 16

F32 = mybir.dt.float32
BF16 = mybir.dt.bfloat16
U32 = mybir.dt.uint32
U16 = mybir.dt.uint16
U8 = mybir.dt.uint8
FP8X4 = mybir.dt.float8_e4m3fn_x4
MULT = mybir.AluOpType.mult
ADD = mybir.AluOpType.add
IDENT = mybir.ActivationFunctionType.Identity
COPY = mybir.ActivationFunctionType.Copy

P = 128
PACK = 4
PASSES = K // (P * PACK)
NT = N // P
EH = E // 2
SH = S // 2
LIST = 16
WINDOW = SH + LIST
RUN = 4
PAIR = 2
STEPS = ((0, 0), (1, 0), (0, 1), (1, 1), (0, 2), (0, 3), (1, 2), (1, 3))
LAST = len(STEPS) - 1
DEFERRED = (1, 3)
FIRST_HALF_DONE = 5
BANK = 512
QUAD = 32
KB = 1024
SHARES = {0: 192, 2: 512, 3: 512, 4: 416, 5: 416, 6: 128}


AT_WINDOWS = 0
PITCH = 17 * 256
AT_EARLY = (AT_WINDOWS + (2 * PACK + 1) * PITCH, AT_WINDOWS + (3 * PACK + 1) * PITCH)
AT_SLOTS = AT_EARLY[1] + 16 * KB
SLOT_KB = (24, 24, 24, 16, 16, 24)

PIECES = {s: ((0, SH),) for s in range(LAST - 1)}
PIECES[LAST - 1] = ((0, BANK), (BANK, SH))
PIECES[LAST] = ((0, BANK), (BANK, SH - C), (SH - C, SH))


def tile_moe_pre_lin_bias_kernel(tc, xT, w, b, gate, offs, pos1, pos2, pos3, pos4, out):
    nc = tc.nc
    x_rows = xT.rearrange("(g p j) t -> g j p t", p=P, j=PACK)
    w_rows = w.rearrange("e (g p j) n -> g e p j n", p=P, j=PACK)

    with ExitStack() as ctx:
        keep = ctx.enter_context(tc.tile_pool(name="keep", bufs=1))
        ring = ctx.enter_context(tc.tile_pool(name="ring", bufs=2))
        arena = ctx.enter_context(tc.tile_pool(name="arena", bufs=1))
        psum = ctx.enter_context(tc.psum_pool(name="psum", bufs=1))

        def placed(name, shape, dtype, at):
            return arena.tile([P] + shape, dtype, name=name, offset=at, align_bytes=256)

        def bank(name, n):
            return psum.tile([P, BANK], F32, name=name, offset=n * 4 * BANK)

        def window_at(g, j):
            return AT_WINDOWS + (g * PACK + j) * PITCH

        def raw_at(s):
            return AT_SLOTS + sum(SLOT_KB[: s % len(SLOT_KB)]) * KB

        slot_tokens = keep.tile([P, S // LIST], U16, name="slot_tokens")
        token_slots = [keep.tile([P, T // LIST], U16, name="token_slots%d" % r) for r in range(TOP)]
        gate_rows = keep.tile([P, QUAD], F32, name="gate_rows", align_bytes=64)
        gate_cols = placed("gate_cols", [QUAD], F32, raw_at(2 - 3) + 8 * KB)
        identity = keep.tile([P, P], F32, name="identity")
        bias = keep.tile([P, NT, E], F32, name="bias")
        windows = {(g, j): placed("window%d_%d" % (g, j), [WINDOW], F32, window_at(g, j)) for g in range(PASSES) for j in range(PACK)}
        y = [placed("y0", [S], F32, raw_at(FIRST_HALF_DONE) + 8 * KB), placed("y1", [S], F32, window_at(PASSES - 1, 0))]
        acc_bank = {(0, 0): 0, (0, 1): 1, (1, 0): 2, (1, 1): 3, (0, 2): 4, (0, 3): 5, (1, 2): 0, (1, 3): 1}
        acc = {key: bank("acc%d_%d" % key, n) for key, n in acc_bank.items()}
        gates = [bank("gates%d" % n, 4 + n) for n in range(S // BANK)]

        w_raw, w_mx, stage, x_bf, x_mx, x_codes = {}, {}, {}, {}, {}, {}

        def load_x(g, j, queue=nc.sync):
            queue.dma_start(out=windows[g, j][:, 0:T], in_=x_rows[g, j])

        def load_w(s, experts=range(EH)):
            h, g = STEPS[s]
            if s not in w_raw:
                w_raw[s] = placed("w_raw%d" % s, [EH, PACK, N], F32, raw_at(s))
            for q in experts:
                nc.sync.dma_start(out=w_raw[s][:, q], in_=w_rows[g, h * EH + q])

        def round_w(engine, dst, s, experts, columns):
            run = RUN if engine is nc.vector else PAIR
            engine.tensor_copy(
                out=dst.rearrange("p q (c i j) -> p q c j i", i=run, j=PACK),
                in_=w_raw[s][:, experts, :, columns].rearrange("p q j (c i) -> p q c j i", i=run),
            )

        def mx_tiles(name, s, words):
            if s in DEFERRED:
                at = window_at(STEPS[s][1], 0) + (0 if name == "x" else 5 * KB)
                codes = placed("%s_codes%d" % (name, s), [words], U32, at)
                scales = placed("%s_scales%d" % (name, s), [words], U8, at + 4 * KB)
            else:
                codes = ring.tile([P, words], U32, name=name + "_codes", align_bytes=64)
                scales = ring.tile([P, words], U8, name=name + "_scales", align_bytes=64)
            return codes, scales

        def quantise_w(name, s, values, members):
            codes, scales = mx_tiles(name, s, len(members) * P)
            nc.vector.quantize_mx(out=codes[:].bitcast(FP8X4), scales=scales[:], in_=values)
            for n, member in enumerate(members):
                w_mx[member] = (codes[:, n * P : (n + 1) * P], scales[:, n * P : (n + 1) * P])

        def quantise_x(s, lo, hi):
            if s not in x_codes:
                x_codes[s] = mx_tiles("x", s, SH)
            codes, scales = x_codes[s]
            nc.vector.quantize_mx(out=codes[:, lo:hi].bitcast(FP8X4), scales=scales[:, lo:hi], in_=x_bf[s][:, lo * PACK : hi * PACK])
            for q in range(lo // C, hi // C):
                x_mx[s, q] = (codes[:, q * C : (q + 1) * C], scales[:, q * C : (q + 1) * C])

        def staged(s, lo, hi):
            first, last = [piece for piece in PIECES[s] if piece[0] <= lo < piece[1]][0]
            if (s, first) not in stage:
                if s < 2:
                    at = AT_EARLY[s]
                elif (s, first) == (LAST - 1, 0):
                    at = raw_at(s - 2) + 8 * KB
                else:
                    at = raw_at(s - (3 if s < LAST - 1 else 5)) + 8 * KB + first * PACK * 4
                stage[s, first] = placed("stage%d_%d" % (s, first), [PACK, last - first], F32, at)
            return stage[s, first][:, :, lo - first : hi - first]

        def gather(s, j, lo, hi, engine):
            h, g = STEPS[s]
            picked = windows[g, j][:].indirect(slot_tokens[:, (h * SH + lo) // LIST : (h * SH + hi) // LIST])
            if engine is nc.scalar:
                nc.scalar.activation(staged(s, lo, hi)[:, j, :], picked, COPY)
            else:
                nc.vector.tensor_copy(staged(s, lo, hi)[:, j, :], picked)

        def weigh(s, lo, hi):
            h, g = STEPS[s]
            if s not in x_bf:
                x_bf[s] = placed("x_bf%d" % s, [SH * PACK], BF16, raw_at(s - 1))
            weights = gates[(h * SH + lo) // BANK][:, lo % BANK : lo % BANK + hi - lo]
            nc.vector.tensor_tensor(
                x_bf[s][:, lo * PACK : hi * PACK].rearrange("p (c i j) -> p c j i", i=PAIR, j=PACK),
                staged(s, lo, hi).rearrange("p j (c i) -> p c j i", i=PAIR),
                weights.rearrange("p (c o i) -> p c o i", o=1, i=PAIR).to_broadcast([P, (hi - lo) // PAIR, PACK, PAIR]),
                MULT,
            )

        def multiply(s, experts, tiles):
            h, g = STEPS[s]
            for t in tiles:
                for q in experts:
                    e = h * EH + q
                    nc.tensor.matmul_mx(
                        out=acc[t, e // 2][:, (e % 2) * C : (e % 2 + 1) * C],
                        lhsT=w_mx[s, q, t][0].bitcast(FP8X4),
                        lhsT_scale=w_mx[s, q, t][1],
                        rhs=x_mx[s, q][0].bitcast(FP8X4),
                        rhs_scale=x_mx[s, q][1],
                        start=(g == 0 and e % 2 == 0),
                        stop=(g == PASSES - 1 and e % 2 == 1),
                    )

        def bias_on_scalar(t, i):
            for e in (2 * i, 2 * i + 1):
                nc.scalar.activation(
                    out=y[t][:, e * C : (e + 1) * C],
                    in_=acc[t, i][:, (e % 2) * C : (e % 2 + 1) * C],
                    func=IDENT,
                    bias=bias[:, t, e : e + 1],
                )

        def bias_on_vector(t, i):
            nc.vector.tensor_tensor(
                y[t][:, i * BANK : (i + 1) * BANK].rearrange("p (e c) -> p e c", e=2),
                acc[t, i][:].rearrange("p (e c) -> p e c", e=2),
                bias[:, t, 2 * i : 2 * i + 2].rearrange("p (e o) -> p e o", o=1).to_broadcast([P, 2, C]),
                ADD,
            )

        warm = keep.tile([P, 1], F32, name="warm")
        cold = keep.tile([P, 1], F32, name="cold")
        nc.gpsimd.memset(cold[:], 0.0)
        nc.scalar.activation(warm[:], cold[:], COPY)
        nc.sync.dma_start(slot_tokens[:], offs)
        for j in range(2):
            load_x(0, j, nc.scalar)
        gate_blocks = gate[0 : QUAD * P // S, :].rearrange("u (q a r) -> a (u q) r", a=P // QUAD, r=QUAD)
        for a in range(P // QUAD):
            nc.sync.dma_start(out=gate_rows[a * QUAD : (a + 1) * QUAD, :], in_=gate_blocks[a])
        for j in range(2, PACK):
            load_x(0, j)
        load_w(0)
        load_x(1, 0)
        load_w(1, range(2))
        load_x(1, 1)
        load_w(1, range(2, EH))
        for j in range(2, PACK):
            load_x(1, j)
        load_w(2)
        load_x(2, 0)
        load_w(3)
        nc.sync.dma_start(out=bias[:], in_=b.rearrange("(t p) e -> p t e", p=P))
        for r, pos in enumerate((pos1, pos2, pos3, pos4)):
            nc.sync.dma_start(token_slots[r][:], pos)

        make_identity(nc, identity[:])
        nc.vector.transpose(gate_cols[:], gate_rows[:])
        gather(0, 0, 0, SHARES[0], nc.vector)
        for s, j in ((1, 0), (0, 1), (1, 1)):
            gather(s, j, 0, SH, nc.vector)
        for j in (0, 2, 3):
            gather(0, j, SHARES[0] if j == 0 else 0, SH, nc.scalar)
        for q in range(S // P):
            nc.tensor.transpose(
                gates[q * P // BANK][:, q * P % BANK : q * P % BANK + P], gate_cols[:, q : q + 1].to_broadcast([P, P]), identity[:]
            )

        for s in range(LAST):
            for lo, hi in PIECES[s + 1]:
                first = 2 if s == 0 else 0
                for j in range(first, PACK):
                    gather(s + 1, j, SHARES.get(s + 1, 0) if j == first and lo == 0 else lo, hi, nc.scalar)
            tiles = NT if s < LAST - 1 else 1
            w_bf = placed("w_bf%d" % s, [EH, tiles * P * PACK], BF16, raw_at(s - 2))
            round_w(nc.gpsimd, w_bf[:], s, slice(0, EH), slice(0, tiles * P))
            if tiles < NT:
                w_late = placed("w_late", [EH, P * PACK], BF16, raw_at(s - 2) + 4 * KB)
                round_w(nc.gpsimd, w_late[:], s, slice(0, EH), slice(P, N))
            weigh(s, 0, BANK)
            if s == FIRST_HALF_DONE + 1:
                for i in range(2):
                    bias_on_vector(0, i)
            weigh(s, BANK, SH)
            if s in (FIRST_HALF_DONE, FIRST_HALF_DONE + 1):
                for early in DEFERRED:
                    multiply(early, range(EH), (s - FIRST_HALF_DONE,))
            ahead = s + 2 if s < FIRST_HALF_DONE - 1 else s + 1
            if ahead in SHARES and s != FIRST_HALF_DONE - 1:
                gather(ahead, 0, 0, SHARES[ahead], nc.vector)
                quantise_x(s, 0, SH)
            else:
                for lo in range(0, SH, BANK):
                    quantise_x(s, lo, lo + BANK)
            quantise_w("w", s, w_bf[:].rearrange("p q n -> p (q n)"), [(s, q, t) for q in range(EH) for t in range(tiles)])
            if s not in DEFERRED:
                multiply(s, range(EH), range(tiles))
            if s == 0:
                for g, j in ((2, 1), (2, 2), (2, 3), (3, 0)):
                    load_x(g, j)
            if 0 < s <= LAST - 3:
                load_w(s + 3)
            if s == 1:
                for j in range(1, PACK):
                    load_x(3, j)

        w_first = placed("w_first", [EH, P * PACK], BF16, raw_at(LAST - 2))
        w_pairs = [placed("w_pair%d" % i, [2, P * PACK], BF16, raw_at(LAST - 3 + i)) for i in range(2)]

        def round_second(engine, q):
            round_w(engine, w_pairs[q // 2][:, q % 2 : q % 2 + 1, :], LAST, slice(q, q + 1), slice(P, N))

        def second_tile(s, rounded, i):
            quantise_w("held%d" % s, s, rounded.rearrange("p q n -> p (q n)"), [(s, 2 * i + q, 1) for q in range(2)])
            multiply(s, (2 * i, 2 * i + 1), (1,))

        round_w(nc.gpsimd, w_first[:], LAST, slice(0, EH), slice(0, P))
        round_second(nc.gpsimd, 0)
        weigh(LAST, *PIECES[LAST][0])
        weigh(LAST, *PIECES[LAST][1])
        quantise_x(LAST, *PIECES[LAST][0])
        second_tile(LAST - 1, w_late[:, 0:2, :], 0)
        quantise_w("w", LAST, w_first[:].rearrange("p q n -> p (q n)"), [(LAST, q, 0) for q in range(EH)])
        quantise_x(LAST, *PIECES[LAST][1])
        multiply(LAST, range(EH - 1), (0,))
        round_second(nc.gpsimd, 2)
        weigh(LAST, *PIECES[LAST][2])
        round_second(nc.vector, 1)
        quantise_x(LAST, *PIECES[LAST][2])
        multiply(LAST, (EH - 1,), (0,))
        round_second(nc.vector, 3)
        second_tile(LAST, w_pairs[0][:], 0)
        second_tile(LAST - 1, w_late[:, 2:EH, :], 1)
        second_tile(LAST, w_pairs[1][:], 1)
        for t, i in ((1, 0), (1, 1), (0, 2), (0, 3)):
            bias_on_scalar(t, i)
        for i in range(2, EH):
            bias_on_vector(1, i)

        sums = [placed("sums%d" % t, [TOP + 1, T], F32, raw_at(LAST - 1) + t * 10 * KB) for t in range(NT)]
        halves = (slice(0, T // 2), slice(T // 2, T))

        def picked(t, r, tokens=slice(0, T)):
            return y[t][:].indirect(token_slots[r][:, tokens.start // LIST : tokens.stop // LIST])

        for t in range(NT):
            for r in range(2):
                nc.scalar.activation(sums[t][:, r, :], picked(t, r), COPY)
        for tokens in halves:
            nc.scalar.activation(sums[1][:, 2, tokens], picked(1, 2, tokens), COPY)
        for r in range(2):
            nc.vector.tensor_tensor(sums[0][:, 2 + r, :], picked(0, 2 + r), sums[0][:, r, :], ADD)
        nc.vector.tensor_tensor(sums[1][:, 3, :], picked(1, 3), sums[1][:, 0, :], ADD)
        nc.vector.tensor_tensor(sums[0][:, 4, :], sums[0][:, 2, :], sums[0][:, 3, :], ADD)
        nc.sync.dma_start(out=out[0:P, :], in_=sums[0][:, 4, :])
        for tokens in halves:
            nc.vector.tensor_tensor(sums[1][:, 4, tokens], sums[1][:, 3, tokens], sums[1][:, 1, tokens], ADD)
        for tokens, queue in zip(halves, (nc.sync, nc.scalar)):
            nc.vector.tensor_tensor(sums[1][:, 0, tokens], sums[1][:, 4, tokens], sums[1][:, 2, tokens], ADD)
            queue.dma_start(out=out[P : 2 * P, tokens], in_=sums[1][:, 0, tokens])
